import numpy as np, ml_dtypes
CORES = [48,51,52,55]
N = 4
BF = ml_dtypes.bfloat16
def gentries(a):
    return np.ascontiguousarray(a.reshape(8, 16, -1).transpose(0, 2, 1)).reshape(8, -1)
def gtable(e):
    e = np.asarray(e); return np.ascontiguousarray(e.reshape(8, -1, 16).transpose(0, 2, 1)).reshape(128, -1).astype(np.int32)
V, SH, L, RO, WT = 2048, 1, 256, 5, 3
R = V << SH
NC = 8
def near(rng, X, x):
    return np.clip(np.take_along_axis(X, x[:, :, None, :], 3) + rng.integers(-1, 2, (N, 8, 16, L)), 0, 15)
def scene(rng, strong):
    M = V // NC
    lab = rng.permuted(np.tile(np.arange(V) % NC, (8, 1)), axis=1); order = np.argsort(lab, axis=1, kind="stable")
    if strong: cen = np.tile(2 + 11 * (np.arange(NC) % 2), (8, 16, 1)); w = 1
    else: cen = rng.integers(2, 14, (8, 16, NC)); w = 3
    X = np.clip(np.take_along_axis(cen, np.repeat(lab, 2 ** SH, axis=1)[:, None, :], 2)[None] + rng.integers(-w, w + 1, (N, 8, 16, R)), 0, 15)
    to = np.where(rng.random((N, 8, 16, V)) < 0.4, rng.integers(0, NC, (N, 8, 16, V)), lab[None, :, None, :])
    gene = order[np.arange(8)[None, :, None, None], to * M + rng.integers(0, M, (N, 8, 16, V))]
    P = gene * 2 ** SH + rng.integers(0, 2 ** SH, (N, 8, 16, V))
    x = rng.integers(0, R, (N, 8, L)); th = rng.integers(0, 21, (N, 8, 16, RO))
    return lab, X, P, x, near(rng, X, x), th
def pack(X, P, x, z, th):
    return {"prof": X.reshape(N, 128, R).astype(np.float32).astype(BF), "par": np.ascontiguousarray(P.reshape(N, 128, V)).astype(np.int32),
            "rec": np.stack([gtable(a) for a in x]), "zf": z.reshape(N, 128, L).astype(np.float32).astype(BF), "th": np.ascontiguousarray(th.reshape(N, 128, RO)).astype(np.int32)}
def setup_inputs(rng):
    lab, X, P, x, z, th = scene(rng, False)
    return pack(X, P, x, z, th)
def setup_inputs_spread(rng):
    X = (rng.random((N, 8, 16, R)) * 2.0 ** rng.integers(0, 5, (N, 8, 1, R))).astype(np.int64)
    P = (R * rng.random((N, 8, 16, V)) ** rng.choice(np.array([1, 1, 3]), (N, 8, 1, V))).astype(np.int64)
    x = (R * rng.random((N, 8, L)) ** rng.choice(np.array([1, 2, 4]), (N, 8, 1))).astype(np.int64)
    z = (rng.random((N, 8, 16, L)) * 2.0 ** rng.integers(0, 5, (N, 8, 1, L))).astype(np.int64)
    th = (64 * rng.random((N, 8, 16, RO)) ** 5).astype(np.int64)
    return pack(np.minimum(X, 15), np.minimum(P, R - 1), np.minimum(x, R - 1), np.minimum(z, 15), np.minimum(th, 63))
def setup_inputs_ends(rng):
    f = rng.integers(0, 2, 8); cls = rng.integers(0, 2, (8, V)); cls[:, 0] = f; cls[:, V - 1] = 1 - f
    cr = np.repeat(cls, 2 ** SH, axis=1); pure = rng.random((8, R)) < 0.75; pure[:, 0] = True; pure[:, R - 1] = True
    X = np.where(pure[None, :, None, :], 15 * cr[None, :, None, :], 15 * rng.integers(0, 2, (N, 8, 16, R)))
    own = np.where(cls == f[:, None], 0, R - 1)[None, :, None, :]; e = rng.random((N, 8, 16, V))
    P = np.where(e < 0.45, own, np.where(e < 0.65, R - 1 - own, rng.integers(0, R, (N, 8, 16, V))))
    e = rng.random((N, 8, L)); x = np.where(e < 0.35, 0, np.where(e < 0.7, R - 1, rng.integers(0, R, (N, 8, L))))
    x[:, :, 0] = 0; x[:, :, 1] = R - 1; x[:, :, L - 2] = R - 1; x[:, :, L - 1] = 0
    c = cr[np.arange(8)[None, :, None], x]; like = rng.random((N, 8, L)) < 0.8; like[:, :, :2] = True; like[:, :, L - 2:] = True
    z = np.where(like[:, :, None, :], 15 * c[:, :, None, :], 15 * rng.integers(0, 2, (N, 8, 16, L)))
    th = 63 * rng.integers(0, 2, (N, 8, 16, RO)); turn = rng.integers(0, 2, (N, 8)); turn[N - 1, 7] = 0
    for g in range(8):
        lo = np.flatnonzero(pure[g] & (cr[g] == f[g])); hi = np.flatnonzero(pure[g] & (cr[g] != f[g]))
        for q in range(N):
            a = np.where(rng.random(16) < 0.5, 0, rng.choice(lo, 16)); b = np.where(rng.random(16) < 0.5, R - 1, rng.choice(hi, 16))
            a[:2] = R - 1
            if turn[q, g]: b[15] = 0; b[1] = 0
            P[q, g, :, 0] = a; P[q, g, :, V - 1] = b
    return pack(X, P, x, z, th)
def level(rng, m):
    sh = rng.integers(0, 16, m.shape)
    return (m >> 4)[None] + (((np.arange(16)[:, None] + sh[None]) & 15) < (m & 15)[None])
def setup_inputs_corners(rng):
    lab, X, P, x, z, th = scene(rng, False)
    th[..., 0] = rng.choice(np.array([0, 0, 1, 5, 20, 63]), (N, 8, 16)); k = np.arange(16)[:, None]; l = np.arange(L)
    half = (l & 7) == 3; farx = (l & 7) == 5; fary = (l & 7) == 6; few = farx | fary; hl = np.flatnonzero(half)
    for q in range(N):
        for g in range(8):
            o = 1 + rng.permutation(V - 2); u, v, w = np.array(o[:L]), o[L:2 * L], o[2 * L:3 * L]; u[0] = 0; u[L - 1] = V - 1
            pool = rng.permutation(((o[3 * L:] << SH)[:, None] + np.arange(2 ** SH)[None]).reshape(-1))[:482]
            xr, yr, br = [(a << SH) + rng.integers(0, 2 ** SH, L) for a in (u, v, w)]; xr[0] = 0; xr[L - 1] = R - 1
            flip = rng.integers(0, 2, L); beta = rng.integers(80, 240, L); beta[hl] = 240; bm = np.where(flip == 1, 240 - beta, beta)
            X[q, g][:, pool] = level(rng, np.arange(482) % 241); X[q, g][:, yr] = (15 * (1 - flip))[None]; X[q, g][:, br] = level(rng, bm)
            rho = xr & 15; key = rng.random((16, L)); key[rho, l] = 2.0; place = np.argsort(np.argsort(key, axis=0), axis=0)
            nw = np.where(half | few, 15, rng.choice(np.array([0, WT - 1, WT, WT, WT + 1, 15]), L))
            twin = (nw == WT - 1) & (rng.random(L) < 0.25)
            X[q, g][:, yr[twin] ^ 1] = (15 * (1 - flip[twin]))[None]; th[q, g, rho[twin], 0] = 0
            e = np.where(place < nw[None], rng.choice(np.array([0, 0, 1, 5]), (16, L)), -1)
            m = beta[None] - th[q, g, :, :1] - e
            A = pool[np.where(flip[None] == 1, 240 - m, m)]
            odd = (rng.integers(0, 2, L) == 1) & ~(half | few)
            B = np.where(odd[None] & ((k & 1) == 1), pool[241 + bm][None], br[None])
            B[rho[twin], l[twin]] = yr[twin] ^ 1
            A = np.where((place == 14) & (nw[None] < 15), B, A); A[rho, l] = yr
            lo = np.where(rho == 0, 1, 0)[hl]; hi = np.where(rho == 15, 14, 15)[hl]
            A[lo, hl] = pool[np.where(flip[hl] == 1, 239, 1)]; A[hi, hl] = pool[240 * flip[hl]]; B[lo, hl] = pool[241 + bm[hl]]
            mode = rng.integers(0, 5, L)[None]; some = rng.choice(pool, (16, L))
            C = np.where(mode == 0, yr[None], np.where(mode == 1, xr[None], np.where(mode == 2, np.where(k == 15, some, yr[None]), np.where(mode == 3, np.where(rng.random((16, L)) < 0.5, yr[None], xr[None]), some))))
            far = pool[240 * np.where(farx, flip, 1 - flip)[None] + 241 * rng.integers(0, 2, (16, L))]; far[0] = np.where(farx, xr, yr)
            C = np.where(few[None], far, C)
            P[q, g][:, u] = A; P[q, g][:, v] = B; P[q, g][:, w] = C
            x[q, g] = xr; z[q, g] = (15 * flip)[None]
    return pack(X, P, x, z, th)
def setup_inputs_crowd(rng):
    lab, X, P, x, z, th = scene(rng, True); th = rng.integers(0, 64, th.shape)
    for q in range(N):
        for g in range(8):
            c = int(rng.integers(0, 2)); a = rng.permutation(np.flatnonzero((lab[g] & 1) == c)); b = rng.permutation(np.flatnonzero((lab[g] & 1) != c))
            x0 = (a[:4] << SH) + rng.integers(0, 2 ** SH, 4); y0 = (b[:4] << SH) + rng.integers(0, 2 ** SH, 4)
            for i in range(4):
                P[q, g, :, a[i]] = (rng.choice(a, 16) << SH) + rng.integers(0, 2 ** SH, 16)
                P[q, g, ((a[i] << SH) + np.arange(2 ** SH)) & 15, a[i]] = y0[i]
                P[q, g, :, b[i]] = (rng.choice(b, 16) << SH) + rng.integers(0, 2 ** SH, 16)
            mode = (g + q) % 3
            if mode == 0: x[q, g] = x0[0]
            elif mode == 1: x[q, g] = x0[rng.integers(0, 4, L)]
            else: x[q, g] = (a[0] << SH) + rng.integers(0, 2 ** SH, L)
            if q % 4 == 1 and g % 2 == 1:
                r = (a[4] << SH) + int(rng.integers(0, 2 ** SH)); P[q, g, :, a[4]] = r; x[q, g, int(rng.integers(0, L))] = r
    z = near(rng, X, x)
    for q in range(3, N, 4):
        away = rng.random((8, L)) < 0.5; away[:, 0] = True; away[:, L - 1] = False
        z[q] = np.where(away[:, None, :], 15 - z[q], z[q])
    return pack(X, P, x, z, th)
def setup_inputs_counts(rng):
    cls = rng.permuted(np.tile(np.arange(V) & 1, (8, 1)), axis=1); order = np.argsort(cls, axis=1, kind="stable")
    X = 6 + 2 * np.repeat(cls, 2 ** SH, axis=1)[None, :, None, :] + rng.integers(0, 2, (N, 8, 16, R))
    off = ((np.arange(16)[:, None] - (np.arange(V) << SH)[None]) & 15) < 2 ** SH + 2
    to = np.where(off[None, None], 1 - cls[None, :, None, :], cls[None, :, None, :])
    gene = order[np.arange(8)[None, :, None, None], to * (V // 2) + rng.integers(0, V // 2, (N, 8, 16, V))]
    P = gene * 2 ** SH + rng.integers(0, 2 ** SH, (N, 8, 16, V))
    x = rng.integers(0, R - 2 ** SH, (N, 8, L))
    for q in range(1, N, 2):
        g = int(rng.integers(0, 8)); r = ((V - 1) << SH) + int(rng.integers(0, 2 ** SH))
        P[q, g, :, V - 1] = r; x[q, g, int(rng.integers(0, L))] = r
    z = 6 + 2 * cls[np.arange(8)[None, :, None], x >> SH][:, :, None, :] + rng.integers(0, 2, (N, 8, 16, L))
    lev = 4 + 4 * rng.permuted(np.tile(np.arange(8), (N, RO, 1)), axis=2)
    th = lev.transpose(0, 2, 1)[:, :, None, :] + rng.integers(0, 4, (N, 8, 16, RO))
    th[..., 0] = 0; th[1::4, :, :, 1] = 63; th[2::4, :, :, 2] = 63; th[3::4, :, :, 2] = 63
    for q in range(1, N, 4):
        g = int(rng.integers(0, 8)); X[q, g] = 6 + rng.integers(0, 4, (16, 1))
        th[q, g, :, 2] = 63; th[q, g, rng.permutation(16)[:WT], 2] = 0
    return pack(X, P, x, z, th)
def check_inputs(d):
    bad = []
    for k, lo, hi in (("prof", 0, 15), ("par", 0, R - 1), ("rec", 0, R - 1), ("zf", 0, 15), ("th", 0, 63)):
        a = np.asarray(d[k]).astype(np.float64)
        if not (np.min(a) >= lo and np.max(a) <= hi): bad.append("range of " + k)
        elif np.any(a != np.floor(a)): bad.append("whole numbers in " + k)
    return bad
def look(tab, n):
    return np.take_along_axis(tab, n[:, None, :], 2)
def row_of(tile, k):
    return np.take_along_axis(tile, k[:, None, :], 1)[:, 0]
def dist(w, p):
    return np.add.reduce(np.abs(w - p[:, :, None, :]), axis=1)
def reference(prof, par, rec, zf, th):
    X = prof.astype(np.float32).astype(np.int32).reshape(N, 8, 16, R); P = par.astype(np.int64).reshape(N, 8, 16, V)
    x = np.stack([gentries(a) for a in rec]).astype(np.int64); z = zf.astype(np.float32).astype(np.int32).reshape(N, 8, 16, L)
    tt = th.astype(np.int64).reshape(N, 8, 16, RO); breaks = [0] * N; rows = np.arange(16)[None, :, None]
    for t in range(RO):
        for q in range(N):
            h = (q - t) % N; xs, zs = x[h], z[h]
            A = look(P[q], xs >> SH); rho = (xs + t) & 15; y = row_of(A, rho); B = look(P[q], y >> SH); Xy = look(X[q], y)
            wa = look(X[q], A.reshape(8, -1)).reshape(8, 16, 16, L); wb = look(X[q], B.reshape(8, -1)).reshape(8, 16, 16, L)
            e1 = dist(wb, zs) - dist(wa, zs); e2 = dist(wa, Xy) - dist(wb, Xy)
            s = tt[q, :, :, t][:, :, None] + (breaks[q] & 15)
            wit = (rows != rho[:, None, :]) & (A != B) & (e1 >= s) & (e2 >= s)
            broken = np.count_nonzero(wit, axis=1) >= WT
            kb = np.argmax(np.where(wit, e1 + e2, -1), axis=1)
            C = look(P[q], row_of(B, kb) >> SH); wc = look(X[q], C.reshape(8, -1)).reshape(8, 16, 16, L)
            y1 = row_of(C, np.argmin(np.where(C == y[:, None, :], 1000, dist(wc, zs)), axis=1))
            x1 = row_of(C, np.argmin(np.where(C == xs[:, None, :], 1000, dist(wc, Xy)), axis=1))
            for g in range(8):
                b = np.flatnonzero(broken[g])
                for a, new in ((xs, y1), (y, x1)):
                    u, i = np.unique(a[g, b] >> SH, return_index=True); P[q, g, rho[g, b[i]], u] = new[g, b[i]]
            breaks[q] = int(np.count_nonzero(broken))
            z[h] = np.where(broken[:, None, :], (zs + look(X[q], y1)) >> 1, zs); x[h] = np.where(broken, y1, y)
    return {"ypar": P.reshape(N, 128, V).astype(np.float32), "yrec": np.stack([gtable(a) for a in x]).astype(np.float32), "yz": z.reshape(N, 128, L).astype(np.float32).astype(BF)}

@@ -1,0 +1,594 @@
+import numpy as np
+from concourse.mybir import AluOpType as Alu, ActivationFunctionType as Act
+
+V, R, L, RO = 2048, 4096, 256, 5
+DUP = 4
+GCH = 2
+WARQ = False
+BM = 4
+ABS = (("mzB", 0), ("mzC", 1), ("mzC", 0))
+VG = (("wa", 1, 1), ("wc", 0, 1))
+P16 = False
+MINC = 1.0
+PAIRS = [(d, i) for d in range(1, BM) for i in range(d, BM)]
+NB = 32 // BM
+NE = 32 + NB * len(PAIRS)
+KW = 65536.0
+
+SCRATCH = {
+    "win": ("sbuf", [128, R + RO * L], "bfloat16"), "pari": ("sbuf", [128, V], "int32"),
+    "P": ("sbuf", [128, V + L], "float32"), "cnt4k": ("sbuf", [128, R], "float32"),
+    "rmt": ("sbuf", [128, R + 16], "bfloat16"), "tri": ("sbuf", [128, 2048], "bfloat16"),
+    "reci": ("sbuf", [128, 16], "int32"), "thi": ("sbuf", [128, 8], "int32"), "thf": ("sbuf", [128, 8], "float32"),
+    "XU": ("sbuf", [128, RO * 48], "uint16"), "XS": ("sbuf", [128, RO * 48], "uint16"),
+    "ZS": ("sbuf", [128, RO * L], "bfloat16"), "XV": ("sbuf", [128, 48], "float32"),
+    "ones": ("sbuf", [128, 128], "bfloat16"), "idb": ("sbuf", [128, 128], "bfloat16"),
+    "bo": ("sbuf", [128, 128], "bfloat16"), "tt0": ("sbuf", [128, 128], "bfloat16"),
+    "idf": ("sbuf", [128, 256], "float32"), "bof": ("sbuf", [128, 128], "float32"), "fs": ("sbuf", [128, 144], "float32"),
+    "negi": ("sbuf", [128, 256], "bfloat16"), "i512": ("sbuf", [128, 128], "bfloat16"), "ih": ("sbuf", [128, 128], "bfloat16"),
+    "i241": ("sbuf", [128, 128], "bfloat16"), "boz": ("sbuf", [128, 128], "bfloat16"),
+    "eb": ("sbuf", [128, 128], "bfloat16"), "ff": ("sbuf", [128, 144], "bfloat16"),
+    "W": ("sbuf", [128, 232], "bfloat16"), "SD": ("sbuf", [128, 512], "bfloat16"),
+    "rsa": ("sbuf", [128, 256], "float32"), "rsm": ("sbuf", [128, 128], "bfloat16"),
+    "pmi": ("sbuf", [128, 8], "int32"), "pmf": ("sbuf", [128, 8], "float32"), "jrow": ("sbuf", [128, 64], "float32"),
+    "cdi": ("sbuf", [128, 160], "int32"), "cdu": ("sbuf", [128, 160], "uint16"), "f4k": ("sbuf", [128, 144], "bfloat16"),
+    "bon": ("sbuf", [128, 128], "bfloat16"), "boh": ("sbuf", [128, 128], "bfloat16"), "dum": ("sbuf", [128, 32], "float32"),
+    "Au": ("sbuf", [128, L], "uint16"), "Bu": ("sbuf", [128, L], "uint16"), "Cu": ("sbuf", [128, L], "uint16"),
+    "Af": ("sbuf", [128, L], "float32"), "Bf": ("sbuf", [128, L], "float32"), "Cf": ("sbuf", [128, L], "float32"),
+    "yv": ("sbuf", [128, L], "float32"), "rm": ("sbuf", [128, L], "bfloat16"), "nrm": ("sbuf", [128, L], "bfloat16"),
+    "eqab": ("sbuf", [128, L], "bfloat16"), "nex": ("sbuf", [128, L], "bfloat16"), "ney": ("sbuf", [128, L], "bfloat16"),
+    "pp": ("sbuf", [128, L], "bfloat16"), "YU": ("sbuf", [128, 32], "uint16"), "GC": ("sbuf", [128, 16], "uint16"),
+    "QU": ("sbuf", [128, 16], "uint16"), "GL": ("sbuf", [128, 32], "float32"), "YS": ("sbuf", [128, 32], "float32"),
+    "NS": ("sbuf", [128, 32], "float32"), "BS": ("sbuf", [128, 32], "float32"), "KE": ("sbuf", [128, 32], "float32"),
+    "YB": ("sbuf", [128, 32], "float32"), "XN": ("sbuf", [128, 32], "float32"), "OF": ("sbuf", [128, 32], "float32"),
+    "OU": ("sbuf", [128, 64], "uint16"), "gbc": ("sbuf", [128, 16 * NE], "float32"), "eqd": ("sbuf", [128, 16 * NE], "bfloat16"),
+    "wa": ("sbuf", [128, 4096], "bfloat16"), "wb": ("sbuf", [128, 4096], "bfloat16"), "wc": ("sbuf", [128, 4096], "bfloat16"),
+    "mzA": ("sbuf", [128, 4096], "bfloat16"), "mpA": ("sbuf", [128, 4096], "bfloat16"),
+    "mzB": ("sbuf", [128, 4096], "bfloat16"), "mpB": ("sbuf", [128, 4096], "bfloat16"),
+    "mzC": ("sbuf", [128, 4096], "bfloat16"), "mpC": ("sbuf", [128, 4096], "bfloat16"),
+    "Xb": ("sbuf", [128, L], "bfloat16"), "wt": ("sbuf", [128, L], "bfloat16"), "wk": ("sbuf", [128, L], "float32"),
+    "sc": ("sbuf", [128, 512], "float32"), "cs": ("sbuf", [128, L], "bfloat16"),
+    "ki": ("sbuf", [128, 32], "int32"), "vi": ("sbuf", [128, 64], "int32"), "VV": ("sbuf", [128, 96], "bfloat16"),
+    "vts": ("sbuf", [128, 768], "bfloat16"), "ym": ("sbuf", [128, L], "float32"), "xm": ("sbuf", [128, L], "float32"),
+    "bb": ("sbuf", [128, L], "float32"), "qh": ("sbuf", [128, L], "bfloat16"), "zt": ("sbuf", [128, L], "bfloat16"),
+    "cj": ("sbuf", [128, 16], "float32"), "cf": ("sbuf", [128, 8], "float32"), "ci": ("sbuf", [128, 8], "int32"),
+    "pz0": ("psum", [128, 512], "float32"), "pz1": ("psum", [128, 512], "float32"),
+    "pq0": ("psum", [128, 1024], "bfloat16") if P16 else ("psum", [128, 512], "float32"),
+    "pq1": ("psum", [128, 1024], "bfloat16") if P16 else ("psum", [128, 512], "float32"),
+    "ipen": ("sbuf", [128, 128], "bfloat16"), "yx": ("sbuf", [128, 2 * L], "float32"), "Ab": ("sbuf", [128, L], "float32"),
+    "sg": ("sbuf", [128, 16], "bfloat16"), "dxs": ("sbuf", [128, 64], "bfloat16"),
+    "k0": ("psum", [128, 512], "float32"), "k1": ("psum", [128, 512], "float32"),
+    "m0": ("psum", [128, 512], "float32"), "m1": ("psum", [128, 512], "float32"),
+}
+SEMAPHORES = (["sV", "sA", "sP", "sG", "sent", "ld0", "ld1", "ld2", "ld3", "ld4", "ld5", "st0", "st1", "st2", "st3"]
+              + ["ax%d" % t for t in range(1, RO)] + ["az%d_%d" % (t, h) for t in range(1, RO) for h in (0, 1)])
+
+CY, PCY, GA, SCA, CALL, WAKE = 1.0, 0.5, 1.56, 3.8, 60.0, 120.0
+SEED, ROUNDS, NOISE, STEADY, MOVES, TEMP = 1, 12, 600.0, 20000, 3000, 500.0
+ORDER = []
+
+
+def build(g, T, topo, core):
+    ops = []
+    last_w, readers, times, visit = {}, {}, {}, [-1]
+    vec, act, pe = g.vector, g.scalar, g.tensor
+
+    def op(eng, busy, fn, rd=(), wr=(), lat=0.0, sem=None, after=()):
+        i = len(ops); deps = {}
+        for r in rd:
+            if r in last_w: deps[last_w[r]] = deps.get(last_w[r], False) or not r.startswith("@")
+        for r in wr:
+            for j in readers.get(r, []):
+                deps[j] = deps.get(j, False) or (WARQ and not r.startswith("@"))
+            if r in last_w: deps[last_w[r]] = deps.get(last_w[r], False) or not r.startswith("@")
+        for r in rd: readers.setdefault(r, []).append(i)
+        for r in wr: last_w[r] = i; readers[r] = []
+        nm = (list(wr) + list(rd) + ["-"])[0]
+        if nm[0] in "zxX" and nm[1] not in "btpnmv": nm = nm[0:2] + nm[-2:] if "_" in nm else nm[0:2]
+        times[nm] = times.get(nm, 0) + 1
+        ops.append({"kin": (nm, times[nm], visit[0] < 0), "vis": visit[0], "eng": eng, "busy": busy, "lat": lat, "fn": fn, "deps": deps, "sem": sem, "name": (list(wr) + list(rd) + ["-"])[0], "after": list(after)})
+        return i
+
+    def vcost(n, per=1.0): return CALL + max(64.0, n * per) * CY
+    def V_(n, per, fn, rd, wr): return op("V", vcost(n, per), fn, rd, wr)
+    def A_(n, per, fn, rd, wr): return op("A", vcost(n, per), fn, rd, wr)
+    def G_(n, fn, rd, wr): return op("G", 170.0 + 2 * n * CY, fn, rd, wr)
+
+    def mm(items, rd, wr):
+        def fn():
+            for o, l, r, s, e, c in items: ins = pe.matmul(o, l, r, s, e)
+            return ins
+        return op("P", sum(max(64, it[5]) for it in items) * PCY, fn, rd, wr, lat=60.0)
+
+    def ts(out, in0, s1, s2, o0, o1, n, rd, wr, per=1.0):
+        if s2 is None: return V_(n, per, lambda: vec.tensor_scalar(out, in0, s1, None, o0), rd, wr)
+        return V_(n, per, lambda: vec.tensor_scalar(out, in0, s1, s2, o0, o1), rd, wr)
+    def tt(out, a, b, o, n, rd, wr, per=1.0): return V_(n, per, lambda: vec.tensor_tensor(out, a, b, o), rd, wr)
+    def cp(out, a, n, rd, wr, per=1.0): return V_(n, per, lambda: vec.tensor_copy(out, a), rd, wr)
+    def ms(out, c, n, wr): return V_(n, 0.5, lambda: vec.memset(out, c), [], wr)
+    def ac(out, a, n, rd, wr, f=Act.Identity, bias=0.0, scale=1.0, per=1.0):
+        return A_(n, per, lambda: act.activation(out, a, f, bias=bias, scale=scale), rd, wr)
+    def sel(out, a, pat, cmp, fill, base, cm, n, rd, wr):
+        return G_(n, lambda: g.affine_select(out, a, pat, cmp, fill, base, cm), rd, wr)
+    def io(out, pat, base, cm, n, wr, flt=True):
+        if flt: return G_(n, lambda: g.iota(out, pat, base, cm, allow_small_or_imprecise_dtypes=True), [], wr)
+        return G_(n, lambda: g.iota(out, pat, base, cm), [], wr)
+    def dma(eng, out, a, sem, lat, rd, wr):
+        q = g.sync if eng == "S" else act
+        return op(eng, 60.0, lambda: q.dma_start(out, a).then_inc(T.sem[sem], 16), rd, wr, lat=lat, sem=(sem, 16))
+
+    rank = T.rank_of(core)
+    nxt = T.cores[(rank + 1) % len(T.cores)]
+    rid, pid, _se = topo.addr(nxt)
+    emask = topo.mask(core, nxt)
+    neng = len(topo.engines(core, nxt))
+    prv = T.cores[(rank - 1) % len(T.cores)]
+    nin = len(topo.engines(prv, core))
+    nsent = [0]
+
+    def send(dst, src, sem, rd, landed):
+        def fn():
+            g.remote_dma(dst, src, T.sem[sem], T.sem.sent, pid, rid, emask)
+        nsent[0] += neng
+        s = op("G", 500.0, fn, rd, [])
+        return op(None, 0.0, None, [], [landed], lat=2000.0, sem=(sem, nin), after=[s])
+
+    dma("S", T.pari[:, 0:1024], T.par[:, 0:1024], "ld0", 4000.0, [], ["pari0"])
+    dma("S", T.pari[:, 1024:V], T.par[:, 1024:V], "ld1", 5500.0, [], ["pari1"])
+    dma("S", T.win[:, 0:R], T.prof[:, :], "ld2", 8000.0, [], ["prof"])
+    dma("A", T.reci[:, :], T.rec[:, :], "ld3", 2500.0, [], ["reci"])
+    dma("A", T.win[:, R:R + L], T.zf[:, :], "ld4", 3000.0, [], ["z0_0", "z0_1"])
+    dma("A", T.thi[:, 0:RO], T.th[:, :], "ld5", 2500.0, [], ["thi"])
+    ms(T.ones[:, :], 1.0, 128, ["ones"])
+    sel(T.idb[:, :], T.ones[:, :], [[-1, 128]], Alu.is_equal, 0.0, 0, 1, 128, ["ones"], ["idb"])
+    sel(T.bo[:, :], T.ones[:, :], [[-16, 8], [0, 16]], Alu.is_ge, 0.0, 0, 1, 128, ["ones"], ["bo"])
+    sel(T.bo[:, :], T.bo[:, :], [[16, 8], [0, 16]], Alu.is_ge, 0.0, 15, -1, 128, ["bo"], ["bo"])
+    io(T.pmi[:, 0:1], [[0, 1]], 0, 1, 1, ["pmi"], False)
+    io(T.jrow[:, 0:16], [[1, 16]], 0, 0, 16, ["jrow"])
+    io(T.jrow[:, 16:48], [[0, 2], [16, 16]], V, 0, 32, ["jrow2"])
+    io(T.cdi[:, 0:32], [[1, 32]], 0, 0, 32, ["cdi"], False)
+    for s, (d, i) in enumerate(PAIRS):
+        io(T.cdi[:, 32 + NB * s:32 + NB * s + NB], [[BM, NB]], i - d, 0, NB, ["cdi%d" % s], False)
+        io(T.cdi[:, 96 + NB * s:96 + NB * s + NB], [[16 * BM, NB]], 16 * i, 0, NB, ["cdj%d" % s], False)
+    ts(T.pmi[:, 4:5], T.pmi[:, 0:1], 15, None, Alu.bitwise_and, None, 1, ["pmi"], ["pmi2"])
+    cp(T.pmf[:, 0:1], T.pmi[:, 4:5], 1, ["pmi2"], ["pmf"])
+    ts(T.rmt[:, 0:16], T.jrow[:, 0:16], T.pmf[:, 0:1], None, Alu.is_equal, None, 16, ["jrow", "pmf"], ["rmt"])
+    n = 16
+    while n < R:
+        ac(T.rmt[:, n:2 * n], T.rmt[:, 0:n], n, ["rmt"], ["rmt"], f=Act.Copy); n *= 2
+    ac(T.rmt[:, R:R + 16], T.rmt[:, 0:16], 16, ["rmt"], ["rmt"], f=Act.Copy)
+    ts(T.dum[:, :], T.jrow[:, 16:48], T.pmf[:, 0:1], None, Alu.add, None, 32, ["jrow2", "pmf"], ["dum"])
+    cp(T.cdu[:, 0:NE], T.cdi[:, 0:NE], NE, ["cdi"] + ["cdi%d" % s for s in range(len(PAIRS))], ["cdu"])
+    ts(T.cdu[:, 96:64 + NE], T.cdi[:, 96:64 + NE], T.pmf[:, 0:1], None, Alu.add, None, NE, ["pmf"] + ["cdj%d" % s for s in range(len(PAIRS))], ["cdv"])
+    ts(T.pmf[:, 4:5], T.pmf[:, 0:1], -4096.0, 61440.0, Alu.mult, Alu.add, 1, ["pmf"], ["pmf2"])
+    for c in (256, 384):
+        ac(T.SD[:, c:c + 128], T.idb[:, :], 128, ["idb", "pmf2"], ["cd%d" % c], scale=T.pmf[:, 4:5])
+    for c in (0, 128):
+        ac(T.idf[:, c:c + 128], T.idb[:, :], 128, ["idb"], ["idf%d" % c], f=Act.Copy)
+        ac(T.negi[:, c:c + 128], T.idb[:, :], 128, ["idb"], ["negi%d" % c], scale=-1.0)
+    ac(T.i512[:, :], T.idb[:, :], 128, ["idb"], ["i512"], scale=-512.0)
+    ac(T.ih[:, :], T.idb[:, :], 128, ["idb"], ["ih"], scale=0.5)
+    ac(T.i241[:, :], T.idb[:, :], 128, ["idb"], ["i241"], scale=241.0 * KW)
+    ac(T.boz[:, :], T.bo[:, :], 128, ["bo"], ["boz"], scale=-KW)
+    ac(T.ipen[:, :], T.idb[:, :], 128, ["idb"], ["ipen"], scale=-8192.0)
+    ms(T.fs[:, :], 0.0, 288, ["fs"])
+    cp(T.fs[:, 15:143:16], T.bo[:, 0:128:16], 8, ["bo", "fs"], ["fs"])
+    ac(T.f4k[:, :], T.fs[:, :], 144, ["fs"], ["f4k"], scale=4096.0)
+    ac(T.bon[:, :], T.bo[:, :], 128, ["bo"], ["bon"], scale=-1.0)
+    ac(T.boh[:, :], T.bo[:, :], 128, ["bo"], ["boh"], scale=-KW / 2)
+    ms(T.W[:, :], 0.0, 232, ["W"])
+    WOF = {"mzA": 0, "mpA": 24, "mzB": 48, "mpB": 72, "wa": 96, "wb": 120, "wc": 144, "mC": 160, "dB": 168, "wb2": 192}
+    for name, cs in (("mzA", (2, 0, KW)), ("mpA", (0, -2, -KW)), ("mzB", (-2, 0, -KW)), ("mpB", (0, 2, KW)),
+                     ("wa", (-1, 1)), ("wb", (1, -1)), ("wc", (-KW, -KW)), ("mC", (2 * KW,)),
+                     ("dB", (1, 0, KW / 2)), ("wb2", (0, -1, -KW / 2))):
+        for b, c in enumerate(cs):
+            if c:
+                o = WOF[name] + 8 * b
+                ts(T.W[:, o:o + 8], T.bo[:, 0:128:16], float(c), None, Alu.mult, None, 8, ["bo", "W"], ["W%d" % o])
+    WR = {k: ["W%d" % (o + 8 * b) for b in range(3)] + ["W"] for k, o in WOF.items()}
+    sel(T.eb[0:24, :], T.ones[0:24, :], [[-2, 8], [0, 16]], Alu.is_ge, 0.0, 0, 1, 128, ["ones"], ["eb"])
+    sel(T.eb[0:24, :], T.eb[0:24, :], [[2, 8], [0, 16]], Alu.is_ge, 0.0, 1, -1, 128, ["eb"], ["eb"])
+    sel(T.eb[0:24, :], T.eb[0:24, :], [[-1, 8], [0, 16]], Alu.not_equal, 1.0, -16, 1, 128, ["eb"], ["eb"])
+    ms(T.ff[:, :], 0.0, 144, ["ff"])
+    cp(T.ff[0:24, 15:143:16], T.eb[0:24, 0:128:16], 8, ["eb", "ff"], ["ff"])
+    ms(T.rsa[:, :], 0.0, 512, ["rsa"])
+    V_(16, 1.0, lambda: vec.memset(T.rsa[:, 0:256:16], -67108864.0), ["rsa"], ["rsa"])
+    ms(T.rsm[:, :], 1.0, 128, ["rsm"])
+    V_(8, 1.0, lambda: vec.memset(T.rsm[:, 0:128:16], 0.0), ["rsm"], ["rsm"])
+    io(T.cnt4k[:, 0:V], [[1, V]], 0, 0, V, ["cnt_lo"])
+    io(T.cnt4k[:, V:R], [[1, V]], V, 0, V, ["cnt_hi"])
+    ac(T.tt0[:, :], T.bo[:, :], 128, ["bo"], ["tt0"], scale=4096.0)
+    sel(T.tt0[:, :], T.tt0[:, :], [[1, 128]], Alu.is_ge, 0.0, 0, -1, 128, ["tt0"], ["tt0"])
+    sel(T.tt0[:, :], T.tt0[:, :], [[1, 128]], Alu.not_equal, -4096.0, 0, -1, 128, ["tt0"], ["tt0"])
+    for j in range(16):
+        sel(T.tri[:, 128 * j:128 * j + 128], T.tt0[:, :], [[0, 8], [1, 16]], Alu.is_equal, 0.0, -j, 0, 128, ["tt0"], ["tri%d" % j])
+    cp(T.P[:, 0:1024], T.pari[:, 0:1024], 1024, ["pari0"], ["P"])
+    cp(T.P[:, 1024:V], T.pari[:, 1024:V], 1024, ["pari1"], ["P"])
+    cp(T.thf[:, 0:RO], T.thi[:, 0:RO], RO, ["thi"], ["thf"])
+    ts(T.XU[:, 0:16], T.reci[:, :], 0.5, -0.25, Alu.mult, Alu.add, 16, ["reci"], ["XU0"])
+    cp(T.XU[:, 16:32], T.reci[:, :], 16, ["reci"], ["XU0b"])
+    cp(T.XU[:, 32:48], T.reci[:, :], 16, ["reci"], ["XU0c"])
+
+    Pw, Pall, prof = T.P[:, 0:V], T.P[:, 0:V + L], T.win[:, 0:R]
+    PZ, PQ, KB, MB = [T.pz0, T.pz1], [T.pq0, T.pq1], [T.k0, T.k1], [T.m0, T.m1]
+    HS = (1, 0)
+    NQ = 16 // DUP
+    DB = {}; seq = [("mzB", 1), ("mzB", 0), ("mzC", 1), ("mzC", 0)]
+    for n, e in enumerate(seq):
+        DB[e] = [b for b in (1, 0) if P16 or all(u in ABS for u in seq[n:] if u[1] == b) and not (b == 0 and n == 0)]
+
+    def gather(w, U, name, uname, h):
+        m = 128 // GCH
+        for c in range(GCH):
+            a = 128 * h + m * c
+            if (name, h, c) in VG:
+                cp(w[:, 16 * a:16 * (a + m)], prof.indirect(U[:, a:a + m]), 16 * m, ["prof", uname], ["%s%d_%d" % (name, h, c)], GA)
+            else:
+                ac(w[:, 16 * a:16 * (a + m)], prof.indirect(U[:, a:a + m]), 16 * m, ["prof", uname], ["%s%d_%d" % (name, h, c)], f=Act.Copy, per=GA)
+
+    def wres(name, h): return ["%s%d_%d" % (name, h, c) for c in range(GCH)]
+
+    def mins(w, wname, mname, bank, bname, h, outs, wmat, wr):
+        m = T[mname]; n = 128 * DUP; c0 = 0; br = [bname]
+        if P16:
+            bank, bname, c0 = (T.pq0, "pq0", n * h) if mname[1] == "z" else (T.pq1, "pq1", n * h)
+            br = ["%s_%d" % (bname, i) for i in range(DUP)]
+        for q in range(NQ):
+            a = 2048 * h + n * q; r = "%s%d_%d" % (mname, h, q)
+            tt(m[:, a:a + n], w[:, 2048 * h + q:2048 * (h + 1):NQ], bank[:, c0:c0 + n], Alu.min, n, wres(wname, h) + br + ["@" + bname], [r], MINC)
+            mm([(outs(NQ * i + q), m[:, a + i:a + n:DUP], wmat, False, False, 64) for i in range(DUP)], [r, "@k%d" % h] + wr, [])
+
+    def dists(w, wname, mname, src, sname, banks, h, outs, wmat, wr):
+        m = T[mname]
+        for q in range(4):
+            b = banks[q % len(banks)]; bank = PZ[b]; bn = "pz%d" % b
+            a = 2048 * h + 512 * q; r = "%s%d_%d" % (mname, h, q); its = []
+            for i in range(4):
+                its += [(bank[:, 128 * i:128 * i + 128], T.idb[:, :], w[:, 2048 * h + 4 * q + i:2048 * (h + 1):16], True, False, 128),
+                        (bank[:, 128 * i:128 * i + 128], T.negi[:, 0:128], src, False, True, 128)]
+            mm(its, wres(wname, h) + ["idb", "negi0", sname], [bn, "@" + bn])
+            ac(m[:, a:a + 512], bank[:, :], 512, [bn], [r, "@" + bn], f=Act.Abs)
+            mm([(outs(4 * q + i), m[:, a + 128 * i:a + 128 * i + 128], wmat, False, False, 64) for i in range(4)], [r, "@k%d" % h] + wr, [])
+
+    def sums(w, wname, h, outs, wmat, wr):
+        mm([(outs(k), w[:, 2048 * h + k:2048 * (h + 1):16], wmat, False, False, 64) for k in range(16)], wres(wname, h) + ["@k%d" % h] + wr, [])
+
+    def dup(bank, bname, src, sname):
+        mm([(bank[:, i:128 * DUP:DUP], T.idb[:, :], src, True, True, 128) for i in range(DUP)], ["idb", sname], [bname, "@" + bname])
+
+    for t in range(RO):
+        lastv = t == RO - 1
+        times.clear(); visit[0] = t
+        xo = 48 * t
+        gxu, xu, xtu = T.XU[:, xo:xo + 16], T.XU[:, xo + 16:xo + 32], T.XU[:, xo + 32:xo + 48]
+        XR = ["XU0", "XU0b", "XU0c"] if t == 0 else ["XU%d" % t]
+        zo = R + L * t
+        def zz(h): return T.win[:, zo + 128 * h:zo + 128 * h + 128]
+        def hs(buf, h): return buf[:, 128 * h:128 * h + 128]
+        ZR = ["z%d_%d" % (t, h) for h in (0, 1)]
+        cp(T.Au[:, :], Pw.indirect(gxu), L, ["P"] + XR, ["Au"], GA)
+        ac(T.rm[:, :], T.rmt[:, :].indirect(xtu), L, ["rmt"] + XR, ["rm"], f=Act.Copy, per=GA)
+        tt(T.yv[:, :], Pw.indirect(gxu), T.rm[:, :], Alu.mult, L, ["P", "rm"] + XR, ["yv"], GA)
+        mm([(T.m1[:, 0:16], T.fs[:, 15 - j:143 - j], T.yv[:, j:L:16], j == 0, j == 15, 256) for j in range(16)], ["fs", "yv"], ["yl", "@m1"])
+        ts(T.YU[:, 0:16], T.m1[:, 0:16], 0.5, -0.25, Alu.mult, Alu.add, 16, ["yl"], ["gyu", "@m1"])
+        cp(T.YU[:, 16:32], T.m1[:, 0:16], 16, ["yl"], ["yu", "@m1"])
+        ac(T.YS[:, 16:32], T.m1[:, 0:16], 16, ["yl"], ["ys1", "@m1"], f=Act.Copy)
+        gyu, yu = T.YU[:, 0:16], T.YU[:, 16:32]
+        cp(T.Bu[:, :], Pw.indirect(gyu), L, ["P", "gyu"], ["Bu"], GA)
+        ac(T.pp[:, :], prof.indirect(yu), L, ["prof", "yu"], ["pp"], f=Act.Copy, per=GA)
+        ac(T.Af[:, :], Pw.indirect(gxu), L, ["P"] + XR, ["Af"], f=Act.Copy, per=GA)
+        ac(T.Bf[:, :], Pw.indirect(gyu), L, ["P", "gyu"], ["Bf"], f=Act.Copy, per=GA)
+        tt(T.eqab[:, :], Pw.indirect(gyu), T.Af[:, :], Alu.is_equal, L, ["P", "gyu", "Af"], ["eqab"], GA)
+        ac(T.nrm[:, :], T.rm[:, :], L, ["rm"], ["nrm"], bias=1.0, scale=-1.0)
+        mm([(T.m0[:, 0:L], T.ipen[:, :], T.rm[:, :], True, False, 256), (T.m0[:, 0:L], T.idf[:, 0:128], T.Af[:, :], False, True, 1024)],
+           ["ipen", "rm", "idf0", "Af"], ["ab", "@m0"])
+        ac(T.Ab[:, :], T.m0[:, 0:L], L, ["ab"], ["Ab", "@m0"], f=Act.Relu)
+        ac(T.YS[:, 0:16], T.dum[:, 0:16], 16, ["dum"], ["ys0"], bias=float(zo - V))
+        ts(T.GL[:, 0:16], gxu, 4096.0, None, Alu.add, None, 16, XR, ["gl0"])
+        ts(T.GL[:, 16:32], gyu, 4096.0, None, Alu.add, None, 16, ["gyu"], ["gl1"])
+        ac(T.gbc[:, 0:L], T.cnt4k[:, 0:V].indirect(gxu), L, ["cnt_lo"] + XR, ["gbc0"], bias=4096.0, per=GA)
+        ac(T.gbc[:, L:2 * L], T.cnt4k[:, 0:V].indirect(gyu), L, ["cnt_lo", "gyu"], ["gbc1"], bias=4096.0, per=GA)
+        scol = T.thf[:, 0:1] if t == 0 else T.cf[:, 4:5]
+        ac(T.SD[:, 0:256], T.negi[:, :], 256, ["negi0", "negi128", "thf", "scol"], ["SD"], scale=scol)
+        for h in HS:
+            K = KB[h]; kb = "@k%d" % h; M = MB[h]; mb = "@m%d" % h; H = str(h)
+            if not P16:
+                dup(PZ[h], "pz" + H, zz(h), ZR[h]); dup(PQ[h], "pq" + H, hs(T.pp, h), "pp")
+            elif h == HS[0]:
+                for i in range(DUP):
+                    cp(T.pq0[:, i:L * DUP:DUP], T.win[:, zo:zo + L], L, ZR + ["@pq0"], ["pq0_%d" % i], 0.5)
+                    cp(T.pq1[:, i:L * DUP:DUP], T.pp[:, :], L, ["pp", "@pq1"], ["pq1_%d" % i], 0.5)
+            mm([(K[:, 0:384], T.ones[:, :], T.SD[:, 0:384], True, False, 384)], ["ones", "SD", "cd256"], ["K" + H, kb])
+            o24 = lambda k, K=K: K[:, k:384:16]
+            o16 = lambda k, K=K: K[:, k:256:16]
+            wm = lambda nm, n: T.W[:, WOF[nm]:WOF[nm] + n]
+            gather(T.wa, T.Au, "wa", "Au", h)
+            mins(T.wa, "wa", "mzA", PZ[h], "pz" + H, h, o24, wm("mzA", 24), WR["mzA"])
+            sums(T.wa, "wa", h, o16, wm("wa", 16), WR["wa"])
+            mins(T.wa, "wa", "mpA", PQ[h], "pq" + H, h, o24, wm("mpA", 24), WR["mpA"])
+            gather(T.wb, T.Bu, "wb", "Bu", h)
+            if ("mzB", h) in ABS:
+                sums(T.wb, "wb", h, o24, wm("wb2", 24), WR["wb2"])
+                mm([(K[:, 0:128], zz(h), T.bon[:, :], False, False, 128), (K[:, 256:384], zz(h), T.boh[:, :], False, False, 128)], [ZR[h], "bon", "boh", kb], [])
+            else:
+                sums(T.wb, "wb", h, o16, wm("wb", 16), WR["wb"])
+            mm([(K[:, 0:128], hs(T.eqab, h), T.i512[:, :], False, False, 128), (K[:, 0:128], hs(T.rm, h), T.i512[:, :], False, False, 128)],
+               ["eqab", "rm", "i512", kb], [])
+            if ("mzB", h) in ABS: dists(T.wb, "wb", "mzB", zz(h), ZR[h], DB[("mzB", h)], h, o24, wm("dB", 24), WR["dB"])
+            else: mins(T.wb, "wb", "mzB", PZ[h], "pz" + H, h, o24, wm("mzB", 24), WR["mzB"])
+            mins(T.wb, "wb", "mpB", PQ[h], "pq" + H, h, o24, wm("mpB", 24), WR["mpB"])
+            so = 256 * h
+            mm([(K[:, 256:384], hs(T.Bf, h), T.idf[:, 0:128], False, True, 512)], ["Bf", "idf0"], ["K" + H, kb])
+            ac(hs(T.Xb, h), K[:, 0:128], 128, ["K" + H], ["Xb" + H, kb], f=Act.Relu, scale=-1024.0)
+            tt(hs(T.wt, h), K[:, 128:256], hs(T.Xb, h), Alu.is_ge, 128, ["K" + H, "Xb" + H], ["wt" + H, kb])
+            tt(hs(T.wk, h), K[:, 256:384], hs(T.wt, h), Alu.mult, 128, ["K" + H, "wt" + H], ["wk" + H, kb])
+            V_(128, 1.0, lambda h=h, so=so: vec.tensor_tensor_scan(T.sc[:, so:so + 128], T.rsa[:, 0:128], hs(T.wk, h), 0.0, Alu.add, Alu.max),
+               ["rsa", "wk" + H], ["sc" + H])
+            V_(128, 0.5, lambda h=h: vec.tensor_tensor_scan(hs(T.cs, h), T.rsm[:, :], hs(T.wt, h), 0.0, Alu.mult, Alu.add), ["rsm", "wt" + H], ["cs" + H])
+            ko, vo, bo_ = 16 * h, 32 * h, 48 * h
+            cp(T.ki[:, ko:ko + 8], T.sc[:, so + 15:so + 128:16], 8, ["sc" + H], ["ki" + H])
+            ts(T.vi[:, vo:vo + 16:2], T.ki[:, ko:ko + 8], 1, 0x7C0, Alu.logical_shift_right, Alu.bitwise_and, 8, ["ki" + H], ["vh" + H])
+            ts(T.vi[:, vo + 1:vo + 16:2], T.ki[:, ko:ko + 8], 1, 63, Alu.logical_shift_right, Alu.bitwise_and, 8, ["ki" + H], ["vl" + H])
+            ac(T.VV[:, bo_ + 32:bo_ + 40], T.cs[:, 128 * h + 15:128 * h + 128:16], 8, ["cs" + H], ["vn" + H], f=Act.Relu, bias=24576.0, scale=-8192.0)
+            cp(T.VV[:, bo_ + 16:bo_ + 32], T.vi[:, vo:vo + 16], 16, ["vh" + H, "vl" + H], ["vv" + H])
+            to = 384 * h
+            mm([(M[0:24, 0:128], T.VV[:, bo_ + 16:bo_ + 40], T.idb[:, :], True, True, 128)], ["vv" + H, "vn" + H, "idb"], ["vt" + H, mb])
+            ac(T.vts[0:24, to:to + 128], M[0:24, 0:128], 128, ["vt" + H], ["vts" + H, mb], f=Act.Copy)
+            mm([(M[:, 384:392], T.ff[0:24, 15 - j:143 - j], T.vts[0:24, to + j:to + 128:16], j == 0, j == 15, 64) for j in range(16)],
+               ["ff", "vts" + H], ["li" + H, mb])
+            ts(T.GC[:, 8 * h:8 * h + 8], M[:, 384:392], float(V - 1), None, Alu.min, None, 8, ["li" + H], ["gc" + H, mb])
+            ac(T.NS[:, 8 * h:8 * h + 8], M[:, 384:392], 8, ["li" + H], ["ns" + H, mb], f=Act.Copy)
+            gcu = T.GC[:, 8 * h:8 * h + 8]
+            cp(hs(T.Cu, h), Pw.indirect(gcu), 128, ["P", "gc" + H], ["Cu" + H], GA)
+            ac(hs(T.Cf, h), Pw.indirect(gcu), 128, ["P", "gc" + H], ["Cf" + H], f=Act.Copy, per=GA)
+        ac(T.NS[:, 16:32], T.NS[:, 0:16], 16, ["ns0", "ns1"], ["ns2"], f=Act.Copy)
+        ac(T.BS[:, :], T.NS[:, :], 32, ["ns0", "ns1", "ns2"], ["BS"], bias=16384.0, scale=-2.0)
+        tt(T.KE[:, :], T.GL[:, :], T.NS[:, :], Alu.max, 32, ["gl0", "gl1", "ns0", "ns1", "ns2"], ["KE"])
+        tt(T.YB[:, :], T.YS[:, :], T.BS[:, :], Alu.max, 32, ["ys0", "ys1", "BS"], ["YB"])
+        ac(T.gbc[:, 512:16 * NE], T.gbc[:, 0:512].indirect(T.cdu[:, 96:64 + NE]), 16 * NE - 512, ["gbc0", "gbc1", "cdv"], ["gbc2"], f=Act.Copy, per=GA)
+        tt(T.eqd[:, :], T.KE[:, :].indirect(T.cdu[:, 0:NE]), T.gbc[:, :], Alu.is_equal, 16 * NE, ["KE", "cdu", "gbc0", "gbc1", "gbc2"], ["eqd"], GA)
+        if not lastv:
+            ac(T.sg[:, :], T.NS[:, 0:16], 16, ["ns0", "ns1"], ["sg"], f=Act.Sign, bias=-4096.0)
+            mm([(T.m0[:, 440:456], T.ones[:, :], T.sg[:, :], True, True, 64)], ["ones", "sg"], ["cn", "@m0"])
+            A_(16, 1.0, lambda: act.activation(T.cj[:, :], T.m0[:, 440:456], Act.Identity, bias=64.0, scale=-0.5, accum_out=T.cf[:, 0:1]),
+               ["cn"], ["cf", "cj", "@m0"])
+            ac(T.cf[:, 1:2], T.cf[:, 0:1], 1, ["cf"], ["cf1"], bias=-0.46875, scale=0.0625)
+            ac(T.cf[:, 2:3], T.cf[:, 1:2], 1, ["cf1"], ["cf2"], bias=12582912.0)
+            ac(T.cf[:, 3:4], T.cf[:, 2:3], 1, ["cf2"], ["cf3"], bias=16 * 12582912.0, scale=-16.0)
+            ac(T.cf[:, 5:6], T.cf[:, 0:1], 1, ["cf", "cf3"], ["cf5"], bias=T.cf[:, 3:4])
+            ac(T.cf[:, 4:5], T.cf[:, 5:6], 1, ["cf5", "thf"], ["scol"], bias=T.thf[:, t + 1:t + 2])
+        mm([(T.m1[:, 432:400 + NE], T.f4k[:, 15 - j:143 - j], T.eqd[:, 512 + j:16 * NE:16], j == 0, j == 15, 64) for j in range(16)],
+           ["eqd", "f4k"], ["dx", "@m1"])
+        ac(T.dxs[:, 0:NE - 32], T.m1[:, 432:400 + NE], NE - 32, ["dx"], ["dxs", "@m1"], f=Act.Copy)
+        mm([(T.m1[:, 400:432], T.tri[:, 128 * j:128 * j + 128], T.eqd[:, j:512:16], j == 0, False, 64) for j in range(16)]
+           + [(T.m1[:, 400:432], T.idf[:, 0:128], T.GL[:, :], False, False, 256)]
+           + [(T.m1[:, 400 + i:432:BM], T.idb[:, :], T.dxs[:, NB * s:NB * (s + 1)], False, s == len(PAIRS) - 1, 64) for s, (d, i) in enumerate(PAIRS)],
+           ["eqd", "dxs", "idb", "gl0", "gl1", "idf0"] + ["tri%d" % j for j in range(16)], ["dd", "@m1"])
+        tt(T.OF[:, :], T.m1[:, 400:432], T.dum[:, :], Alu.min, 32, ["dd", "dum"], ["OF", "@m1"])
+        cp(T.OU[:, 0:32], T.OF[:, :], 32, ["OF"], ["OU"])
+        for h in HS:
+            K = KB[h]; kb = "@k%d" % h; M = MB[h]; mb = "@m%d" % h; H = str(h)
+            far = ("mzC", h) in ABS
+            mm([(K[:, 0:256], T.ones[:, :], T.SD[:, 256:512], True, False, 256), (K[:, 0:128], hs(T.pp, h), T.boz[:, :], False, False, 128)]
+               + ([] if far else [(K[:, 128:256], zz(h), T.boz[:, :], False, False, 128)]),
+               ["ones", "cd256", "cd384", "pp", ZR[h], "boz"], ["K" + H, kb])
+            gather(T.wc, T.Cu, "wc", "Cu" + H, h)
+            tt(hs(T.nex, h), T.cnt4k[:, :].indirect(T.XU[:, xo + 16 + 8 * h:xo + 24 + 8 * h]), hs(T.Cf, h), Alu.not_equal, 128, ["cnt_lo", "cnt_hi", "Cf" + H] + XR, ["nex" + H], GA)
+            tt(hs(T.ney, h), T.cnt4k[:, :].indirect(T.YU[:, 16 + 8 * h:24 + 8 * h]), hs(T.Cf, h), Alu.not_equal, 128, ["cnt_lo", "cnt_hi", "Cf" + H, "yu"], ["ney" + H], GA)
+            mm([(K[:, 0:128], hs(T.nex, h), T.i241[:, :], False, False, 128), (K[:, 128:256], hs(T.ney, h), T.i241[:, :], False, False, 128)],
+               ["nex" + H, "ney" + H, "i241", kb], [])
+            if far:
+                sums(T.wc, "wc", h, lambda k, K=K: K[:, k:128:16], T.W[:, 144:152], WR["wc"])
+                dists(T.wc, "wc", "mzC", zz(h), ZR[h], DB[("mzC", h)], h, lambda k, K=K: K[:, 128 + k:256:16], T.W[:, 144:152], WR["wc"])
+            else:
+                sums(T.wc, "wc", h, lambda k, K=K: K[:, k:256:16], T.W[:, 144:160], WR["wc"])
+                mins(T.wc, "wc", "mzC", PZ[h], "pz" + H, h, lambda k, K=K: K[:, 128 + k:256:16], T.W[:, 160:168], WR["mC"])
+            mins(T.wc, "wc", "mpC", PQ[h], "pq" + H, h, lambda k, K=K: K[:, k:128:16], T.W[:, 160:168], WR["mC"])
+            mm([(K[:, 0:256], hs(T.Cf, h), T.idf[:, :], False, True, 1024)], ["Cf" + H, "idf0", "idf128"], ["K" + H, kb])
+            so, ko, vo, bo_, to = 256 * h, 16 * h, 32 * h, 48 * h, 384 * h
+            V_(256, 1.0, lambda K=K, so=so: vec.tensor_tensor_scan(T.sc[:, so:so + 256], T.rsa[:, :], K[:, 0:256], 0.0, Alu.add, Alu.max),
+               ["rsa", "K" + H], ["sc" + H, kb])
+            cp(T.ki[:, ko:ko + 16], T.sc[:, so + 15:so + 256:16], 16, ["sc" + H], ["ki" + H])
+            ts(T.vi[:, vo:vo + 32:2], T.ki[:, ko:ko + 16], 0xFC0, None, Alu.bitwise_and, None, 16, ["ki" + H], ["vh" + H])
+            ts(T.vi[:, vo + 1:vo + 32:2], T.ki[:, ko:ko + 16], 63, None, Alu.bitwise_and, None, 16, ["ki" + H], ["vl" + H])
+            cp(T.VV[:, bo_:bo_ + 32], T.vi[:, vo:vo + 32], 32, ["vh" + H, "vl" + H], ["vv" + H])
+            mm([(M[0:24, 0:128], T.VV[:, bo_ + 16:bo_ + 40], T.idb[:, :], True, True, 128),
+                (M[0:24, 128:256], T.VV[:, bo_ + 16:bo_ + 40], T.idb[:, :], True, True, 128),
+                (M[0:16, 256:384], T.VV[:, bo_:bo_ + 16], T.idb[:, :], True, True, 128)], ["vv" + H, "vn" + H, "idb"], ["vt" + H, mb])
+            ac(T.vts[0:24, to:to + 256], M[0:24, 0:256], 256, ["vt" + H], ["vts" + H, mb], f=Act.Copy)
+            ac(T.vts[0:16, to + 256:to + 384], M[0:16, 256:384], 128, ["vt" + H], ["vtx" + H, mb], f=Act.Copy)
+            mm([(K[:, 384:400], T.ff[0:24, 15 - j:143 - j], T.vts[0:24, to + j:to + 256:16], j == 0, j == 15, 64) for j in range(16)],
+               ["ff", "vts" + H], ["lj" + H, kb])
+            mm([(M[:, 0:128], T.eb[0:24, :], T.vts[0:24, to:to + 128], True, False, 128), (M[:, 0:128], T.ipen[:, :], hs(T.nrm, h), False, True, 128),
+                  (M[:, 128:256], T.eb[0:16, :], T.vts[0:16, to + 256:to + 384], True, False, 128), (M[:, 128:256], T.ipen[:, :], hs(T.nrm, h), False, True, 128)],
+               ["eb", "ipen", "nrm", "vts" + H, "vtx" + H], ["vt" + H, mb])
+            tt(T.XN[:, 8 * h:8 * h + 8], K[:, 384:392], T.YB[:, 8 * h:8 * h + 8], Alu.min, 8, ["lj" + H, "YB"], ["qf" + H, kb])
+            cp(T.QU[:, 8 * h:8 * h + 8], T.XN[:, 8 * h:8 * h + 8], 8, ["qf" + H], ["qu" + H])
+            tt(T.XN[:, 16 + 8 * h:24 + 8 * h], K[:, 392:400], T.YB[:, 16 + 8 * h:24 + 8 * h], Alu.min, 8, ["lj" + H, "YB"], ["xn" + H, kb])
+            ac(T.yx[:, so:so + 256], M[:, 0:256], 256, ["vt" + H], ["yx" + H, mb], f=Act.Relu)
+            ac(hs(T.qh, h), T.win[:, 0:zo + L].indirect(T.QU[:, 8 * h:8 * h + 8]), 128, ["prof", "qu" + H] + ["z%d_%d" % (u, v) for u in range(t + 1) for v in (0, 1)],
+               ["qh" + H], scale=0.5, per=GA)
+            mm([(K[:, 256:384], T.idb[:, :], hs(T.qh, h), True, False, 128), (K[:, 256:384], T.ih[:, :], zz(h), False, True, 128)],
+               ["idb", "ih", "qh" + H, ZR[h]], ["zp" + H, kb])
+            ac(hs(T.zt, h), K[:, 256:384], 128, ["zp" + H], ["zt" + H, kb], bias=127.75)
+            zs = T.ZS[:, L * t + 128 * h:L * t + 128 * h + 128]
+            ac(zs, hs(T.zt, h), 128, ["zt" + H], ["zs%d_%d" % (t, h)], bias=-128.0)
+            if not lastv:
+                send(T.win[:, zo + L + 128 * h:zo + L + 128 * h + 128], zs, "az%d_%d" % (t + 1, h), ["zs%d_%d" % (t, h)], "z%d_%d" % (t + 1, h))
+            for m in range(8 * h + 8 - BM, 8 * h - 1, -BM):
+                tt(Pall.indirect(T.OU[:, m:m + BM]), T.Ab[:, 16 * m:16 * (m + BM)], T.yx[:, 128 * h + 16 * m:128 * h + 16 * (m + BM)], Alu.add, 16 * BM,
+                   ["OU", "Ab", "yx" + H], ["P"], SCA)
+        if not lastv:
+            xn = T.XN[:, 16:32]
+            ac(T.XV[:, 0:16], xn, 16, ["xn0", "xn1"], ["xv0"], bias=-0.25, scale=0.5)
+            ac(T.XV[:, 16:32], xn, 16, ["xn0", "xn1"], ["xv1"], f=Act.Copy)
+            ac(T.XV[:, 32:48], xn, 16, ["xn0", "xn1"], ["xv2"], bias=float(t + 1))
+            cp(T.XS[:, xo:xo + 48], T.XV[:, :], 48, ["xv0", "xv1", "xv2"], ["xs%d" % t])
+            send(T.XU[:, xo + 48:xo + 96], T.XS[:, xo:xo + 48], "ax%d" % (t + 1), ["xs%d" % t], "XU%d" % (t + 1))
+        tt(T.bb[:, :], Pw.indirect(gyu), T.nrm[:, :], Alu.mult, L, ["P", "gyu", "nrm"], ["bb"], GA)
+        for m in range(16 - BM, -1, -BM):
+            a = 128 * (m // 8) + 128 + 16 * m
+            tt(Pall.indirect(T.OU[:, 16 + m:16 + m + BM]), T.bb[:, 16 * m:16 * (m + BM)], T.yx[:, a:a + 16 * BM], Alu.add, 16 * BM,
+               ["OU", "bb", "yx%d" % (m // 8)], ["P"], SCA)
+    t = RO - 1
+    dma("S", T.yrec[:, :], T.XN[:, 16:32], "st0", 2000.0, ["xn0", "xn1"], [])
+    dma("S", T.yz[:, :], T.ZS[:, L * t:L * t + L], "st1", 2000.0, ["zs%d_0" % t, "zs%d_1" % t], [])
+    dma("S", T.ypar[:, 0:1024], T.P[:, 0:1024], "st2", 4000.0, ["P"], [])
+    dma("A", T.ypar[:, 1024:V], T.P[:, 1024:V], "st3", 4000.0, ["P"], [])
+    return ops, nsent[0]
+
+
+def schedule(ops):
+    n = len(ops)
+    busy = [o["busy"] for o in ops]; eng = [o["eng"] for o in ops]
+    pre = [[] for _ in range(n)]; suc = [[] for _ in range(n)]
+    for i, o in enumerate(ops):
+        for j in list(o["deps"]) + o["after"]:
+            d = ops[j]
+            same = d["eng"] == o["eng"] and not o["deps"].get(j, False) and d["sem"] is None
+            gap = 0.0 if same else d["lat"] + WAKE
+            pre[i].append((j, gap)); suc[j].append((i, gap))
+
+    def place(seq, edges, base):
+        end = [0.0] * n; line = {}
+        for i in seq:
+            t = base[i]
+            for j, gap in edges[i]:
+                if end[j] + gap > t: t = end[j] + gap
+            if eng[i] is not None:
+                ln = line.setdefault(eng[i], []); k = len(ln)
+                while k > 0 and ln[k - 1][1] > t: k -= 1
+                while k < len(ln) and ln[k][0] < t + busy[i]:
+                    t = max(t, ln[k][1]); k += 1
+                ln.insert(k, (t, t + busy[i]))
+            end[i] = t + busy[i]
+        return end
+
+    lat = [o["lat"] for o in ops]; zero = [0.0] * n
+    rng = np.random.default_rng(SEED)
+    tail = [0.0] * n
+    for i in range(n - 1, -1, -1): tail[i] = busy[i] + max([tail[s] + gp for s, gp in suc[i]] + [lat[i]])
+    key = [-tail[i] for i in range(n)]
+    best = None
+    for rnd in range(ROUNDS):
+        for i in range(n):
+            for j, gap in pre[i]:
+                if key[i] <= key[j]: key[i] = key[j] + 1e-3
+        end = place(sorted(range(n), key=lambda i: key[i]), pre, zero)
+        span = max(end[i] + lat[i] for i in range(n))
+        if best is None or span < best[0]: best = (span, end)
+        use = end if rnd % 4 else best[1]
+        noise = rng.random(n) * NOISE
+        key = [-use[i] - float(noise[i]) for i in range(n)]
+        for i in range(n - 1, -1, -1):
+            for s, gap in suc[i]:
+                if key[i] <= key[s]: key[i] = key[s] + 1e-3
+        back = place(sorted(range(n), key=lambda i: key[i]), suc, lat)
+        key = [-back[i] for i in range(n)]
+    kin = {}
+    for i, o in enumerate(ops): kin.setdefault(o["kin"], []).append(i)
+    kins = list(kin.values())
+    vis = [o["vis"] for o in ops]
+    sub = [i for i in range(n) if vis[i] in (1, 2)]
+    per = best[0] / RO
+    off = {ops[i]["kin"]: best[1][i] - busy[i] - per * vis[i] for i in range(n) if vis[i] <= 2}
+    for i in range(n): off.setdefault(ops[i]["kin"], per)
+    names = sorted(set(ops[i]["kin"] for i in sub))
+    spre = [[e for e in pre[i] if vis[e[0]] in (1, 2)] for i in range(n)]
+    ssuc = [[e for e in suc[i] if vis[e[0]] in (1, 2)] for i in range(n)]
+
+    def keys(o, idx, p, s, back):
+        key = [0.0] * n
+        for i in idx: key[i] = o[ops[i]["kin"]] + per * max(vis[i], 0)
+        if back:
+            for i in idx[::-1]:
+                for j, gap in s[i]:
+                    if key[i] >= key[j]: key[i] = key[j] - 1e-3
+        else:
+            for i in idx:
+                for j, gap in p[i]:
+                    if key[i] <= key[j]: key[i] = key[j] + 1e-3
+        return sorted(idx, key=lambda i: key[i])
+
+    now = None; top = None
+    for rnd in range(STEADY):
+        o = dict(off)
+        for u in range(int(rng.integers(1, 4)) if rnd else 0):
+            o[names[int(rng.integers(len(names)))]] += float(rng.normal()) * (3000.0 if rng.random() < 0.5 else 800.0)
+        if rng.random() < 0.3:
+            key = {}
+            for i in sub[::-1]:
+                k = o[ops[i]["kin"]] + per * vis[i]
+                for j, gap in ssuc[i]: k = min(k, key[j] - 1e-3)
+                key[i] = k
+                if vis[i] == 1: o[ops[i]["kin"]] = k - per
+        end = place(keys(o, sub, spre, ssuc, False), spre, zero)
+        span = max(end)
+        if now is None or span <= now + TEMP * (1.0 - rnd / STEADY) * float(rng.random()): now = span; off = o
+        if top is None or span < top[0]: top = (span, o)
+    if top is not None:
+        end = place(keys(top[1], list(range(n)), pre, suc, False), pre, zero)
+        span = max(end[i] + lat[i] for i in range(n))
+        if span < best[0]: best = (span, end)
+    cur = best
+    for rnd in range(MOVES):
+        key = [cur[1][i] - busy[i] for i in range(n)]
+        for u in range(int(rng.integers(1, 4))):
+            d = float(rng.normal()) * (3000.0 if rng.random() < 0.5 else 800.0)
+            for i in kins[int(rng.integers(len(kins)))]: key[i] += d
+        if rng.random() < 0.5:
+            for i in range(n):
+                for j, gap in pre[i]:
+                    if key[i] <= key[j]: key[i] = key[j] + 1e-3
+        else:
+            for i in range(n - 1, -1, -1):
+                for s, gap in suc[i]:
+                    if key[i] >= key[s]: key[i] = key[s] - 1e-3
+        end = place(sorted(range(n), key=lambda i: key[i]), pre, zero)
+        span = max(end[i] + lat[i] for i in range(n))
+        if span <= cur[0] + TEMP * (1.0 - rnd / MOVES) * float(rng.random()): cur = (span, end)
+        if span < best[0]: best = (span, end)
+    end = best[1]; order = {}
+    for i in sorted(range(n), key=lambda i: (end[i] - busy[i], i)):
+        if eng[i] is not None: order.setdefault(eng[i], []).append(i)
+    return order, [end[i] + lat[i] for i in range(n)]
+
+
+def rank_program(g, core, T, topo):
+    if T.rank_of(core) is None:
+        return
+    ops, nsent = build(g, T, topo, core)
+    if not ORDER: ORDER.append(schedule(ops)[0])
+    order = ORDER[0]
+    queue = {"V": g.vector, "A": g.scalar, "P": g.tensor, "G": g, "S": g.sync}
+    pos = {}
+    for e in order:
+        for k, i in enumerate(order[e]): pos[i] = k
+    waits = {}; marked = set()
+    for e in order:
+        seen = {}
+        for i in order[e]:
+            need = {}; ws = []
+            for j, raw in ops[i]["deps"].items():
+                d = ops[j]
+                if d["sem"] is not None:
+                    if d["sem"] not in seen: seen[d["sem"]] = 1; ws.append(d["sem"])
+                elif d["eng"] != e or (raw and e != "P"):
+                    if pos[j] > seen.get(d["eng"], -1) and pos[j] > need.get(d["eng"], (-1, 0))[0]: need[d["eng"]] = (pos[j], j)
+            for q in need:
+                seen[q] = need[q][0]; marked.add(need[q][1]); ws.append(need[q][1])
+            waits[i] = ws
+    count = {}
+    for e in order:
+        c = 0
+        for i in order[e]:
+            if i in marked: c += 1; count[i] = c
+    for e in order:
+        for i in order[e]:
+            for w in waits[i]:
+                if isinstance(w, tuple): queue[e].wait_ge(T.sem[w[0]], w[1])
+                else: queue[e].wait_ge(T.sem["s" + ops[w]["eng"]], count[w])
+            ins = ops[i]["fn"]()
+            if i in marked: ins.then_inc(T.sem["s" + e], 1)
+    for s in ("st0", "st1", "st2", "st3"): g.sync.wait_ge(T.sem[s], 16)
+    g.wait_ge(T.sem.sent, nsent)

@@ -6,10 +6,10 @@ DUP = 4
 GCH = 2
 WARQ = False
 BM = 4
-ABS = (("mzB", 0), ("mzC", 1), ("mzC", 0))
-VG = (("wa", 1, 1), ("wc", 0, 1))
-P16 = False
-MINC = 1.0
+ABS = ()
+VG = (("wa", 1, 1), ("wc", 0, 1), ("wb", 1, 1))
+P16 = True
+MINC = 0.5
 PAIRS = [(d, i) for d in range(1, BM) for i in range(d, BM)]
 NB = 32 // BM
 NE = 32 + NB * len(PAIRS)
@@ -52,10 +52,10 @@ SCRATCH = {
     "vts": ("sbuf", [128, 768], "bfloat16"), "ym": ("sbuf", [128, L], "float32"), "xm": ("sbuf", [128, L], "float32"),
     "bb": ("sbuf", [128, L], "float32"), "qh": ("sbuf", [128, L], "bfloat16"), "zt": ("sbuf", [128, L], "bfloat16"),
     "cj": ("sbuf", [128, 16], "float32"), "cf": ("sbuf", [128, 8], "float32"), "ci": ("sbuf", [128, 8], "int32"),
-    "pz0": ("psum", [128, 512], "float32"), "pz1": ("psum", [128, 512], "float32"),
-    "pq0": ("psum", [128, 1024], "bfloat16") if P16 else ("psum", [128, 512], "float32"),
-    "pq1": ("psum", [128, 1024], "bfloat16") if P16 else ("psum", [128, 512], "float32"),
+    "rz0": ("psum", [128, 64, 16], "bfloat16"), "rz1": ("psum", [128, 64, 16], "bfloat16"),
+    "rp0": ("psum", [128, 64, 16], "bfloat16"), "rp1": ("psum", [128, 64, 16], "bfloat16"),
     "ipen": ("sbuf", [128, 128], "bfloat16"), "yx": ("sbuf", [128, 2 * L], "float32"), "Ab": ("sbuf", [128, L], "float32"),
+    "zd": ("sbuf", [128, 1024], "bfloat16"), "pd": ("sbuf", [128, 1024], "bfloat16"),
     "sg": ("sbuf", [128, 16], "bfloat16"), "dxs": ("sbuf", [128, 64], "bfloat16"),
     "k0": ("psum", [128, 512], "float32"), "k1": ("psum", [128, 512], "float32"),
     "m0": ("psum", [128, 512], "float32"), "m1": ("psum", [128, 512], "float32"),
@@ -64,7 +64,7 @@ SEMAPHORES = (["sV", "sA", "sP", "sG", "sent", "ld0", "ld1", "ld2", "ld3", "ld4"
               + ["ax%d" % t for t in range(1, RO)] + ["az%d_%d" % (t, h) for t in range(1, RO) for h in (0, 1)])
 
 CY, PCY, GA, SCA, CALL, WAKE = 1.0, 0.5, 1.56, 3.8, 60.0, 120.0
-SEED, ROUNDS, NOISE, STEADY, MOVES, TEMP = 1, 12, 600.0, 20000, 3000, 500.0
+SEED, ROUNDS, NOISE, STEADY, MOVES, TEMP = 1, 12, 600.0, 14000, 1500, 500.0
 ORDER = []
 
 
@@ -210,9 +210,10 @@ def build(g, T, topo, core):
     cp(T.XU[:, 32:48], T.reci[:, :], 16, ["reci"], ["XU0c"])
 
     Pw, Pall, prof = T.P[:, 0:V], T.P[:, 0:V + L], T.win[:, 0:R]
-    PZ, PQ, KB, MB = [T.pz0, T.pz1], [T.pq0, T.pq1], [T.k0, T.k1], [T.m0, T.m1]
+    PZ, PQ, KB, MB = [T.rz0, T.rz1], [T.rp0, T.rp1], [T.k0, T.k1], [T.m0, T.m1]
     HS = (1, 0)
     NQ = 16 // DUP
+    HC = (None,)
     DB = {}; seq = [("mzB", 1), ("mzB", 0), ("mzC", 1), ("mzC", 0)]
     for n, e in enumerate(seq):
         DB[e] = [b for b in (1, 0) if P16 or all(u in ABS for u in seq[n:] if u[1] == b) and not (b == 0 and n == 0)]
@@ -229,14 +230,39 @@ def build(g, T, topo, core):
     def wres(name, h): return ["%s%d_%d" % (name, h, c) for c in range(GCH)]
 
     def mins(w, wname, mname, bank, bname, h, outs, wmat, wr):
+        m = T[mname]; s = mname[1]
+        for c in range(2):
+            a = 2048 * h + 1024 * c; bn = "r%s%d" % (s, c)
+            tt(m[:, a:a + 1024], w[:, a:a + 1024], T[bn][:, :, :], Alu.min, 1024, ["%s%d_%d" % (wname, h, c), bn, "@" + bn], ["%s%d_%d" % (mname, h, c)], MINC)
+        mm([(outs(k), m[:, 2048 * h + k:2048 * (h + 1):16], wmat, False, False, 64) for k in range(16)],
+           ["%s%d_0" % (mname, h), "%s%d_1" % (mname, h), "@k%d" % h] + wr, [])
+
+    def turn(s, h, src, sname):
+        bn = "r%s0" % s; o = 512 * (s == "p") + 256 * h; two = ["%sd%d_%d" % (s, h, i) for i in (0, 1)]
+        for i in (0, 1): ac(T.pd[:, o + i:o + 256:2], src, 128, [sname], [two[i]], f=Act.Copy)
+        def fn():
+            for c in (0, 1): ins = pe.transpose(T[bn][:, 8 * c:8 * c + 8, :], T.pd[:, o + 128 * c:o + 128 * c + 128], T.idb[:, :])
+            return ins
+        op("P", 256 * PCY, fn, two + ["idb"], [bn, "@" + bn], lat=60.0)
+        ac(T.zd[:, o:o + 256], T[bn][:, 0:16, :], 256, [bn], ["%sT%d" % (s, h), "@" + bn], f=Act.Copy)
+
+    def fill(s, h):
+        for c in range(2):
+            bn = "r%s%d" % (s, c); o = 512 * (s == "p") + 256 * h + 128 * c
+            def fn(o=o, bn=bn):
+                for k in range(0, 16, 2): ins = pe.transpose(T[bn][:, :, k:k + 2], T.zd[:, o:o + 128], T.idb[:, :])
+                return ins
+            op("P", 1024 * PCY, fn, ["%sT%d" % (s, h), "idb"], [bn, "@" + bn], lat=60.0)
+
+    def mins4(w, wname, mname, bank, bname, h, outs, wmat, wr):
         m = T[mname]; n = 128 * DUP; c0 = 0; br = [bname]
         if P16:
             bank, bname, c0 = (T.pq0, "pq0", n * h) if mname[1] == "z" else (T.pq1, "pq1", n * h)
             br = ["%s_%d" % (bname, i) for i in range(DUP)]
         for q in range(NQ):
             a = 2048 * h + n * q; r = "%s%d_%d" % (mname, h, q)
-            tt(m[:, a:a + n], w[:, 2048 * h + q:2048 * (h + 1):NQ], bank[:, c0:c0 + n], Alu.min, n, wres(wname, h) + br + ["@" + bname], [r], MINC)
-            mm([(outs(NQ * i + q), m[:, a + i:a + n:DUP], wmat, False, False, 64) for i in range(DUP)], [r, "@k%d" % h] + wr, [])
+            tt(m[:, a:a + n], w[:, 128 * h:128 * h + 128, DUP * q:DUP * q + DUP], bank[:, c0:c0 + n], Alu.min, n, wres(wname, h) + br + ["@" + bname], [r], MINC)
+            mm([(outs(DUP * q + i), m[:, a + i:a + n:DUP], wmat, False, False, 64) for i in range(DUP)], [r, "@k%d" % h] + wr, [])
 
     def dists(w, wname, mname, src, sname, banks, h, outs, wmat, wr):
         m = T[mname]
@@ -292,12 +318,10 @@ def build(g, T, topo, core):
         ac(T.SD[:, 0:256], T.negi[:, :], 256, ["negi0", "negi128", "thf", "scol"], ["SD"], scale=scol)
         for h in HS:
             K = KB[h]; kb = "@k%d" % h; M = MB[h]; mb = "@m%d" % h; H = str(h)
-            if not P16:
-                dup(PZ[h], "pz" + H, zz(h), ZR[h]); dup(PQ[h], "pq" + H, hs(T.pp, h), "pp")
-            elif h == HS[0]:
-                for i in range(DUP):
-                    cp(T.pq0[:, i:L * DUP:DUP], T.win[:, zo:zo + L], L, ZR + ["@pq0"], ["pq0_%d" % i], 0.5)
-                    cp(T.pq1[:, i:L * DUP:DUP], T.pp[:, :], L, ["pp", "@pq1"], ["pq1_%d" % i], 0.5)
+            if h == HS[0]:
+                for u in HS: turn("z", u, zz(u), ZR[u])
+                for u in HS: turn("p", u, hs(T.pp, u), "pp")
+            fill("z", h); fill("p", h)
             mm([(K[:, 0:384], T.ones[:, :], T.SD[:, 0:384], True, False, 384)], ["ones", "SD", "cd256"], ["K" + H, kb])
             o24 = lambda k, K=K: K[:, k:384:16]
             o16 = lambda k, K=K: K[:, k:256:16]
@@ -369,6 +393,7 @@ def build(g, T, topo, core):
         for h in HS:
             K = KB[h]; kb = "@k%d" % h; M = MB[h]; mb = "@m%d" % h; H = str(h)
             far = ("mzC", h) in ABS
+            if h != HC[0]: fill("z", h); fill("p", h)
             mm([(K[:, 0:256], T.ones[:, :], T.SD[:, 256:512], True, False, 256), (K[:, 0:128], hs(T.pp, h), T.boz[:, :], False, False, 128)]
                + ([] if far else [(K[:, 128:256], zz(h), T.boz[:, :], False, False, 128)]),
                ["ones", "cd256", "cd384", "pp", ZR[h], "boz"], ["K" + H, kb])

@@ -2,69 +2,41 @@ import numpy as np
 from concourse.mybir import AluOpType as Alu, ActivationFunctionType as Act
 
 V, R, L, RO = 2048, 4096, 256, 5
-DUP = 4
-GCH = 2
-WARQ = False
-BM = 4
-ABS = ()
-VG = (("wa", 1, 1), ("wc", 0, 1), ("wb", 1, 1))
-P16 = True
-MINC = 0.5
-PAIRS = [(d, i) for d in range(1, BM) for i in range(d, BM)]
-NB = 32 // BM
-NE = 32 + NB * len(PAIRS)
-KW = 65536.0
+CUT = tuple((w, h, c) for w in ("wa", "wb", "wc") for h in (0, 1) for c in (0, 1))
+APART = (0,)
+SPLIT = "A"
+VG = (("wa", 1, 1, 0), ("wa", 1, 1, 1), ("wb", 1, 1, 1), ("wb", 0, 1, 1))
+ONV = ("pT", "zT0", "Bh")
+KW = 131072.0
+BIG = 67108864.0
+MG = 1.5 * 2.0 ** 36
 
-SCRATCH = {
-    "win": ("sbuf", [128, R + RO * L], "bfloat16"), "pari": ("sbuf", [128, V], "int32"),
-    "P": ("sbuf", [128, V + L], "float32"), "cnt4k": ("sbuf", [128, R], "float32"),
-    "rmt": ("sbuf", [128, R + 16], "bfloat16"), "tri": ("sbuf", [128, 2048], "bfloat16"),
-    "reci": ("sbuf", [128, 16], "int32"), "thi": ("sbuf", [128, 8], "int32"), "thf": ("sbuf", [128, 8], "float32"),
-    "XU": ("sbuf", [128, RO * 48], "uint16"), "XS": ("sbuf", [128, RO * 48], "uint16"),
-    "ZS": ("sbuf", [128, RO * L], "bfloat16"), "XV": ("sbuf", [128, 48], "float32"),
-    "ones": ("sbuf", [128, 128], "bfloat16"), "idb": ("sbuf", [128, 128], "bfloat16"),
-    "bo": ("sbuf", [128, 128], "bfloat16"), "tt0": ("sbuf", [128, 128], "bfloat16"),
-    "idf": ("sbuf", [128, 256], "float32"), "bof": ("sbuf", [128, 128], "float32"), "fs": ("sbuf", [128, 144], "float32"),
-    "negi": ("sbuf", [128, 256], "bfloat16"), "i512": ("sbuf", [128, 128], "bfloat16"), "ih": ("sbuf", [128, 128], "bfloat16"),
-    "i241": ("sbuf", [128, 128], "bfloat16"), "boz": ("sbuf", [128, 128], "bfloat16"),
-    "eb": ("sbuf", [128, 128], "bfloat16"), "ff": ("sbuf", [128, 144], "bfloat16"),
-    "W": ("sbuf", [128, 232], "bfloat16"), "SD": ("sbuf", [128, 512], "bfloat16"),
-    "rsa": ("sbuf", [128, 256], "float32"), "rsm": ("sbuf", [128, 128], "bfloat16"),
-    "pmi": ("sbuf", [128, 8], "int32"), "pmf": ("sbuf", [128, 8], "float32"), "jrow": ("sbuf", [128, 64], "float32"),
-    "cdi": ("sbuf", [128, 160], "int32"), "cdu": ("sbuf", [128, 160], "uint16"), "f4k": ("sbuf", [128, 144], "bfloat16"),
-    "bon": ("sbuf", [128, 128], "bfloat16"), "boh": ("sbuf", [128, 128], "bfloat16"), "dum": ("sbuf", [128, 32], "float32"),
-    "Au": ("sbuf", [128, L], "uint16"), "Bu": ("sbuf", [128, L], "uint16"), "Cu": ("sbuf", [128, L], "uint16"),
-    "Af": ("sbuf", [128, L], "float32"), "Bf": ("sbuf", [128, L], "float32"), "Cf": ("sbuf", [128, L], "float32"),
-    "yv": ("sbuf", [128, L], "float32"), "rm": ("sbuf", [128, L], "bfloat16"), "nrm": ("sbuf", [128, L], "bfloat16"),
-    "eqab": ("sbuf", [128, L], "bfloat16"), "nex": ("sbuf", [128, L], "bfloat16"), "ney": ("sbuf", [128, L], "bfloat16"),
-    "pp": ("sbuf", [128, L], "bfloat16"), "YU": ("sbuf", [128, 32], "uint16"), "GC": ("sbuf", [128, 16], "uint16"),
-    "QU": ("sbuf", [128, 16], "uint16"), "GL": ("sbuf", [128, 32], "float32"), "YS": ("sbuf", [128, 32], "float32"),
-    "NS": ("sbuf", [128, 32], "float32"), "BS": ("sbuf", [128, 32], "float32"), "KE": ("sbuf", [128, 32], "float32"),
-    "YB": ("sbuf", [128, 32], "float32"), "XN": ("sbuf", [128, 32], "float32"), "OF": ("sbuf", [128, 32], "float32"),
-    "OU": ("sbuf", [128, 64], "uint16"), "gbc": ("sbuf", [128, 16 * NE], "float32"), "eqd": ("sbuf", [128, 16 * NE], "bfloat16"),
-    "wa": ("sbuf", [128, 4096], "bfloat16"), "wb": ("sbuf", [128, 4096], "bfloat16"), "wc": ("sbuf", [128, 4096], "bfloat16"),
-    "mzA": ("sbuf", [128, 4096], "bfloat16"), "mpA": ("sbuf", [128, 4096], "bfloat16"),
-    "mzB": ("sbuf", [128, 4096], "bfloat16"), "mpB": ("sbuf", [128, 4096], "bfloat16"),
-    "mzC": ("sbuf", [128, 4096], "bfloat16"), "mpC": ("sbuf", [128, 4096], "bfloat16"),
-    "Xb": ("sbuf", [128, L], "bfloat16"), "wt": ("sbuf", [128, L], "bfloat16"), "wk": ("sbuf", [128, L], "float32"),
-    "sc": ("sbuf", [128, 512], "float32"), "cs": ("sbuf", [128, L], "bfloat16"),
-    "ki": ("sbuf", [128, 32], "int32"), "vi": ("sbuf", [128, 64], "int32"), "VV": ("sbuf", [128, 96], "bfloat16"),
-    "vts": ("sbuf", [128, 768], "bfloat16"), "ym": ("sbuf", [128, L], "float32"), "xm": ("sbuf", [128, L], "float32"),
-    "bb": ("sbuf", [128, L], "float32"), "qh": ("sbuf", [128, L], "bfloat16"), "zt": ("sbuf", [128, L], "bfloat16"),
-    "cj": ("sbuf", [128, 16], "float32"), "cf": ("sbuf", [128, 8], "float32"), "ci": ("sbuf", [128, 8], "int32"),
-    "rz0": ("psum", [128, 64, 16], "bfloat16"), "rz1": ("psum", [128, 64, 16], "bfloat16"),
-    "rp0": ("psum", [128, 64, 16], "bfloat16"), "rp1": ("psum", [128, 64, 16], "bfloat16"),
-    "ipen": ("sbuf", [128, 128], "bfloat16"), "yx": ("sbuf", [128, 2 * L], "float32"), "Ab": ("sbuf", [128, L], "float32"),
-    "zd": ("sbuf", [128, 1024], "bfloat16"), "pd": ("sbuf", [128, 1024], "bfloat16"),
-    "sg": ("sbuf", [128, 16], "bfloat16"), "dxs": ("sbuf", [128, 64], "bfloat16"),
-    "k0": ("psum", [128, 512], "float32"), "k1": ("psum", [128, 512], "float32"),
-    "m0": ("psum", [128, 512], "float32"), "m1": ("psum", [128, 512], "float32"),
-}
-SEMAPHORES = (["sV", "sA", "sP", "sG", "sent", "ld0", "ld1", "ld2", "ld3", "ld4", "ld5", "st0", "st1", "st2", "st3"]
-              + ["ax%d" % t for t in range(1, RO)] + ["az%d_%d" % (t, h) for t in range(1, RO) for h in (0, 1)])
+BF, HF, F32, I32, U16 = "bfloat16", "float16", "float32", "int32", "uint16"
+SCRATCH = {name: ("sbuf", [128] + list(shape), kind) for kind, bufs in (
+    (BF, {"win": [R + RO * 2 * L], "rmt": [R + 16], "SJ": [2048], "MK": [256], "ZS": [RO * 2 * L], "ones": [128], "idb": [128], "negi": [256],
+          "bo": [128], "fs": [144], "ih": [128], "iq": [128], "ie": [128], "ic": [128], "ig": [128], "I17": [408], "E17": [408], "B17": [408],
+          "KB": [512], "KC": [408], "FB": [144], "FX": [144], "FQ": [144], "EB": [384], "W": [160], "SD": [256], "rsm": [128], "rm": [L],
+          "dab": [L], "eq": [2 * L], "pp": [2 * L], "zT": [2 * L], "pT": [2 * L], "EC": [512], "eqd": [1024], "dxs": [64], "SH": [512],
+          "wa": [2048, 2], "wb": [2048, 2], "wc": [2048, 2], "mzA": [4096], "mpA": [4096], "mzB": [4096], "mpB": [4096], "mzC": [4096],
+          "mpC": [4096], "Xb": [L], "nw": [L], "cs": [L], "qh": [L], "zt": [L]}),
+    (HF, {"XB": [RO * L], "XN": [RO * L], "VV": [RO * 64], "LQ": [80], "Ah": [L], "Bh": [L], "Ch": [L], "yv": [L], "KT": [128], "KX": [96],
+          "GX": [96], "vts": [512]}),
+    (F32, {"P": [V + L], "PO": [V], "thf": [16], "XO": [16], "xl": [16], "wk": [L], "rsb": [128], "rsc": [408], "pmf": [8], "jrow": [16], "dum": [16],
+           "LF": [80], "Ab": [L], "bb": [L], "yx": [2 * L], "GL": [32], "BR": [16], "VR": [192], "OF": [32], "sb": [L], "sc": [816], "tb": [64],
+           "cj": [8], "cf": [8]}),
+    (I32, {"pari": [V], "reci": [16], "thi": [8], "pmi": [8]}),
+    (U16, {"XU": [RO * 48], "XS": [RO * 32], "cl": [16], "ju": [16], "Au": [L], "Bu": [L], "Cu": [L], "YU": [16], "GC": [16], "QU": [16], "OU": [32]}),
+) for name, shape in bufs.items()}
+SCRATCH.update({name: ("psum", [128, 128, 8], BF) for name in ("rz0", "rz1", "rp0", "rp1")})
+SCRATCH.update({name: ("psum", [128, 512], F32) for name in ("k0", "k1", "m0", "m1")})
+SEMAPHORES = (["sV", "sA", "sP", "sG", "sent"] + ["ld%d" % i for i in range(8)] + ["st%d" % i for i in range(6)]
+              + ["ax%d" % t for t in range(1, RO)] + ["a%s%d_%d" % (s, t, h) for s in "zt" for t in range(1, RO) for h in (0, 1)])
 
 CY, PCY, GA, SCA, CALL, WAKE = 1.0, 0.5, 1.56, 3.8, 60.0, 120.0
-SEED, ROUNDS, NOISE, STEADY, MOVES, TEMP = 1, 12, 600.0, 14000, 1500, 500.0
+SEED, STEADY, MOVES, HOT, COLD, PERIOD = 1, 20000, 40000, 60.0, 10.0, 35100.0
+EARLY = {"V": 3000.0, "A": 9000.0, "P": 0.0}
+PLAN = """rz1:-173 zT1:-120 Ah:-108 rm:-62 sh0:-50 rz1':-37 Au1:-19 SD:-16 yv:0 sh0':14 wa1_0b:16 Au0:46 yl:58 wa1_1:65 wa0_1b:102 K0:109 ones':128 K1:148 gyu:151 yu:163 rz0:167 Bh:175 pp0:188 wa1_1b:221 sh1:233 pp1:234 ab:246 sh1':272 wa1_0:280 ones:285 Bu0:307 wa1_1':319 zT0:339 rp0:345 wb1_1b:358 wb1_0:365 wa1_0':377 pT0:443 wb1_1:451 mzA1_1:475 rp1:487 mzA1_0:532 wb1_0b:537 rp0':538 rz0':589 mpA1_1:589 dab:623 wb1_1':641 mzB1_1:647 wa0_1:655 wb1_0':666 mzA1_1':692 mpB1_0:704 mzA1_0':717 wa0_0:741 mpA1_1':743 mzB1_0:761 mzB1_1':769 mpB1_0':794 mpB1_1:818 wa0_0b:826 mzB1_0':830 mpA1_0:875 mpB1_1':887 wb0_0b:912 mpA0_0:933 mpA1_0':945 K1':970 ab':983 mzA0_0:990 Xb1:1001 wb0_1:1020 mpA0_0':1021 nw1:1047 mzA0_0':1059 wk1:1078 GL:1097 Xb1':1106 sb1:1109 GX:1125 cs1:1137 tb1:1149 vn1:1161 Ab:1173 vr1:1173 wb0_1b:1186 vt1:1198 K1'':1204 vtb1:1222 wb0_0:1241 li1:1253 mzA0_1:1272 wa0_1':1304 gc1:1329 wb0_0':1339 mpB0_0:1341 Ch1:1353 wa0_0':1364 BR1:1379 sh1'':1404 KX1:1404 wb0_1':1416 Cu1:1434 mpA0_1:1453 kt:1465 mpB0_0':1472 KT:1490 mzA0_1':1497 wc1_0b:1508 mzB0_1:1510 df1:1523 mzB0_0:1568 mpA0_1':1587 wc1_1:1594 df1':1612 mpB0_1:1625 mzB0_1':1638 mzB0_0':1664 wc1_0:1680 eq1:1452 mpB0_1':1694 K0':1720 K1''':1732 eqd1:1734 eq1':1746 eq1'':1750 Xb0:1766 wc1_0':1778 wc1_1b:1785 nw0:1797 dx1:1804 wk0:1828 sb0:1858 Xb0':1871 tb0:1889 dxs1:1889 cs0:1902 vr0:1914 dd1:1914 vn0:1926 mzC1_1:1926 vt0:1950 K0'':1957 vtb0:1975 mzC1_0:1984 li0:2006 OF1:2041 mzC1_1':2057 gc0:2075 OU1:2087 BR0:2099 Ch0:2112 KX0:2124 sh0'':2150 kt':2162 Cu0:2180 mzC1_0':2182 KT':2187 eq0:2199 wc1_1':2208 wc0_1b:2211 mpC1_1:2225 df0:2234 mpC1_0:2282 wc0_0:2297 df0':2298 X0:2323 mpC1_1':2337 eqd0:2341 mpC1_0':2362 wc0_1:2383 K1'''':2388 eq0':2408 eq0'':2415 dx0:2418 sc1:2426 wc0_0b:2469 wc0_1':2481 tc1:2485 wc0_1'':2506 vy1:2510 vt1':2534 vtc1:2558 wc0_0':2567 mzC0_1:2567 dxs0:2577 vt1'':2592 mzC0_0:2624 dd0:2631 y01:2636 xs1:2670 xs1':2700 mzC0_1':2654 xn1:2679 mpC0_1:2681 mzC0_0':2731 mpC0_0:2738 K0''':2756 ql1:2770 sc0:2795 wc0_0'':2821 OF0:2829 tc0:2841 mpC0_1':2847 qu1:2853 vy0:2866 qh1:2878 P:2878 vt0':2890 mpC0_0':2897 P':2908 vtc0:2915 zp1:2922 OU0:2927 X0':2935 P'':2939 vt0'':2945 zt1:2953 scx0:2960 y00:2976 P''':2979 xn0:2984 zsb1:2995 tcx0:2998 P'''':3010 zsa1:3014 vr0':3028 cn:3035 ql0:3041 P''''':3041 zsa1':3045 cf:3059 xs:3059 xt:3071 cf1:3084 xs0:3040 xs0':3200 vtx0:3093 cf3:3096 P'''''':3096 xs':3108 qu0:3114 vtb0':3117 P''''''':3127 cf2:3136 vtx0':3148 qh0:3148 bb:3157 zp0:3186 P'''''''':3215 zt0:3217 y10:3190 zsa0:3255 P''''''''':3257 zsb0:3273 scol:3292 P'''''''''':3299 zsa0':3304 P''''''''''':3342"""
+PLAN = """rm:-58 Ah:-12 rz1:-8 yv:0 zT1:34 sh0:46 yl:59 SD:66 Au1:77 wa1_0:108 wa1_1b:108 sh0':110 K0:123 rz0:162 rz1':175 gyu:193 wa1_0b:193 yu:206 Bh:218 K1:226 ones:246 Au0:264 sh1:276 pp0:279 wa1_1:283 sh1':289 pp1:325 Bu0:369 wa0_0b:371 rp0:383 GL:400 ones':409 mzA1_0:413 ab:428 wa1_0':454 wb1_0:457 pT0:470 wa1_1':479 wb1_1b:502 mzA1_0':505 rp1:530 wb1_0b:543 rp0':582 mzA1_1:587 wb1_1:629 mpA1_0:645 mpA1_1:702 wa0_1:715 wb1_1':727 mzA1_1':752 zT0:759 wb1_0':778 mzB1_1:778 wa0_0:801 mpA1_0':803 mpA1_1':829 mpB1_0:835 rz0':855 wa0_1b:886 mpB1_1:892 mzB1_1':906 mpB1_0':931 mzB1_0:949 mpB1_1':961 dab:972 wb0_0b:1004 mzA0_0:1007 mzB1_0':1019 K1':1044 mpA0_0:1064 mzA0_0':1076 Xb1:1090 ab':1101 wb0_1:1109 nw1:1121 wk1:1152 sb1:1183 Xb1':1194 tb1:1213 cs1:1226 vr1:1238 vn1:1250 mpA0_1:1251 vt1:1275 vtb1:1299 wb0_1b:1308 wb0_0:1318 li1:1330 wa0_0':1381 gc1:1399 GX:1404 K1'':1407 mzA0_1:1411 Ch1:1425 K1''':1447 BR1:1451 wa0_1':1463 mpB0_1:1469 sh1'':1489 mzA0_1':1502 Cu1:1526 mpB0_1':1538 KX1:1545 wc1_0:1557 mzB0_1:1558 de1:1563 mpA0_0':1595 eq1:1615 mpA0_1':1621 wc1_1:1643 wb0_0':1647 mzB0_0:1647 mzB0_1':1672 kt:1698 mpB0_0:1704 eq1':1704 wb0_1':1718 KT:1728 mzB0_0':1743 wc1_0b:1747 mpB0_0':1773 K0':1799 df1:1812 Xb0:1833 nw0:1864 wk0:1895 Xb0':1895 wc1_0':1901 Ab:1914 eqd1:1919 wc1_1b:1945 sb0:1977 dx1:1989 cs0:1995 tb0:2008 vn0:2031 vr0:2032 mzC1_0:2045 vt0:2057 K0'':2063 vtb0:2081 dxs1:2100 mzC1_1:2102 li0:2112 eq1'':2163 dd1:2170 gc0:2181 mzC1_0':2192 BR0:2205 OF1:2210 Ch0:2218 wc1_1':2218 KX0:2230 sh0'':2256 kt':2269 mzC1_1':2275 Cu0:2287 KT':2293 mpC1_0:2305 wc0_0b:2317 df0:2324 mpC1_1:2363 wc0_0:2403 mpC1_0':2413 eqd0:2431 de0:2439 mpC1_1':2471 eq0:2489 wc0_1b:2489 K1'''':2497 wc0_0':2517 sc1:2535 dx0:2543 wc0_1:2575 tc1:2594 X0:2594 eq0'':2611 wc0_0'':2617 vy1:2618 OU1:2631 vt1':2643 eq0':2649 vtc1:2667 wc0_1':2673 mzC0_0:2673 dxs0:2686 vt1'':2698 dd0:2730 mzC0_1:2730 y01:2748 mzC0_0':2753 mpC0_0:2787 xn1:2792 mzC0_1':2843 OF0:2844 mpC0_1:2857 K0''':2869 ql1:2882 sc0:2914 mpC0_0':2934 qu1:2952 mpC0_1':2959 tc0:2964 xs1:2976 wc0_1'':2985 vy0:2988 qh1:2995 P:3001 X0':3010 vt0':3017 P':3031 zp1:3033 vtc0:3042 cn:3046 scx0:3049 zt1:3064 P'':3069 vt0'':3072 tcx0:3087 zsa1:3094 xn0:3094 P''':3099 y00:3113 OU0:3117 vr0':3130 zsb1:3132 P'''':3144 ql0:3146 cf:3151 xs:3164 cf1:3175 xt:3176 P''''':3188 vtx0:3197 cf2:3200 xs':3200 qu0:3215 vtb0':3221 P'''''':3227 xs0:3240 zsa1':3250 vtx0':3252 P''''''':3257 qh0:3259 XU:3262 y10:3285 bb:3288 zp0:3297 xs0':3300 cf3:3304 z1:3312 scol:3328 zt0:3340 P'''''''':3345 xs1':3350 xb0:3362 zsa0:3371 P''''''''':3388 zsb0:3390 xb1:3412 zsa0':3421 P'''''''''':3430 P''''''''''':3472 z0:3483"""
 ORDER = []
 
 
@@ -78,15 +50,14 @@ def build(g, T, topo, core):
         for r in rd:
             if r in last_w: deps[last_w[r]] = deps.get(last_w[r], False) or not r.startswith("@")
         for r in wr:
-            for j in readers.get(r, []):
-                deps[j] = deps.get(j, False) or (WARQ and not r.startswith("@"))
+            for j in readers.get(r, []): deps[j] = deps.get(j, False)
             if r in last_w: deps[last_w[r]] = deps.get(last_w[r], False) or not r.startswith("@")
         for r in rd: readers.setdefault(r, []).append(i)
         for r in wr: last_w[r] = i; readers[r] = []
-        nm = (list(wr) + list(rd) + ["-"])[0]
-        if nm[0] in "zxX" and nm[1] not in "btpnmv": nm = nm[0:2] + nm[-2:] if "_" in nm else nm[0:2]
+        name = (list(wr) + list(rd) + ["-"])[0]; nm = name.split("#")[0]
         times[nm] = times.get(nm, 0) + 1
-        ops.append({"kin": (nm, times[nm], visit[0] < 0), "vis": visit[0], "eng": eng, "busy": busy, "lat": lat, "fn": fn, "deps": deps, "sem": sem, "name": (list(wr) + list(rd) + ["-"])[0], "after": list(after)})
+        ops.append({"kin": (nm, times[nm], visit[0] < 0), "vis": visit[0], "eng": eng, "busy": busy, "lat": lat, "fn": fn, "deps": deps,
+                    "sem": sem, "name": name, "after": list(after)})
         return i
 
     def vcost(n, per=1.0): return CALL + max(64.0, n * per) * CY
@@ -100,14 +71,26 @@ def build(g, T, topo, core):
             return ins
         return op("P", sum(max(64, it[5]) for it in items) * PCY, fn, rd, wr, lat=60.0)
 
+    def turn(items, rd, wr):
+        def fn():
+            for o, a in items: ins = pe.transpose(o, a, T.idb[:, :])
+            return ins
+        return op("P", 128 * len(items) * PCY, fn, rd + ["idb"], wr, lat=60.0)
+
     def ts(out, in0, s1, s2, o0, o1, n, rd, wr, per=1.0):
         if s2 is None: return V_(n, per, lambda: vec.tensor_scalar(out, in0, s1, None, o0), rd, wr)
         return V_(n, per, lambda: vec.tensor_scalar(out, in0, s1, s2, o0, o1), rd, wr)
+    def add(out, in0, c, n, rd, wr, per=1.0): return ts(out, in0, c, None, Alu.add, None, n, rd, wr, per)
     def tt(out, a, b, o, n, rd, wr, per=1.0): return V_(n, per, lambda: vec.tensor_tensor(out, a, b, o), rd, wr)
     def cp(out, a, n, rd, wr, per=1.0): return V_(n, per, lambda: vec.tensor_copy(out, a), rd, wr)
     def ms(out, c, n, wr): return V_(n, 0.5, lambda: vec.memset(out, c), [], wr)
+    def scan(out, a, b, o0, o1, n, rd, wr, per=1.0): return V_(n, per, lambda: vec.tensor_tensor_scan(out, a, b, 0.0, o0, o1), rd, wr)
     def ac(out, a, n, rd, wr, f=Act.Identity, bias=0.0, scale=1.0, per=1.0):
         return A_(n, per, lambda: act.activation(out, a, f, bias=bias, scale=scale), rd, wr)
+    def move(tag, out, a, n, rd, wr, per=1.0, fast=0.5):
+        if tag in ONV or tag in VG: return cp(out, a, n, rd, wr, per if per > 1 else fast)
+        return ac(out, a, n, rd, wr, f=Act.Copy, per=per)
+    def fl(out, c, n, wr, p=(0, 128)): return ac(out, T.ones[p[0]:p[1], 0:n], n, ["ones"], wr, bias=float(c), scale=0.0)
     def sel(out, a, pat, cmp, fill, base, cm, n, rd, wr):
         return G_(n, lambda: g.affine_select(out, a, pat, cmp, fill, base, cm), rd, wr)
     def io(out, pat, base, cm, n, wr, flt=True):
@@ -116,6 +99,7 @@ def build(g, T, topo, core):
     def dma(eng, out, a, sem, lat, rd, wr):
         q = g.sync if eng == "S" else act
         return op(eng, 60.0, lambda: q.dma_start(out, a).then_inc(T.sem[sem], 16), rd, wr, lat=lat, sem=(sem, 16))
+    def hs(buf, h): return buf[:, 128 * h:128 * h + 128]
 
     rank = T.rank_of(core)
     nxt = T.cores[(rank + 1) % len(T.cores)]
@@ -133,450 +117,442 @@ def build(g, T, topo, core):
         s = op("G", 500.0, fn, rd, [])
         return op(None, 0.0, None, [], [landed], lat=2000.0, sem=(sem, nin), after=[s])
 
-    dma("S", T.pari[:, 0:1024], T.par[:, 0:1024], "ld0", 4000.0, [], ["pari0"])
-    dma("S", T.pari[:, 1024:V], T.par[:, 1024:V], "ld1", 5500.0, [], ["pari1"])
-    dma("S", T.win[:, 0:R], T.prof[:, :], "ld2", 8000.0, [], ["prof"])
-    dma("A", T.reci[:, :], T.rec[:, :], "ld3", 2500.0, [], ["reci"])
-    dma("A", T.win[:, R:R + L], T.zf[:, :], "ld4", 3000.0, [], ["z0_0", "z0_1"])
-    dma("A", T.thi[:, 0:RO], T.th[:, :], "ld5", 2500.0, [], ["thi"])
+    dma("A", T.reci[:, :], T.rec[:, :], "ld5", 2500.0, [], ["reci"])
+    for q in range(4):
+        dma("S", T.pari[:, 512 * q:512 * q + 512], T.par[:, 512 * q:512 * q + 512], "ld%d" % q, 3000.0 + 800.0 * q, [], ["pari%d" % q])
+    dma("S", T.win[:, 0:R], T.prof[:, :], "ld4", 8000.0, [], ["prof"])
+    dma("A", T.zt[:, :], T.zf[:, :], "ld6", 3000.0, [], ["zt0", "zt1"])
+    dma("A", T.thi[:, 0:RO], T.th[:, :], "ld7", 2500.0, [], ["thi"])
     ms(T.ones[:, :], 1.0, 128, ["ones"])
+    io(T.pmi[:, 0:1], [[0, 1]], 0, 1, 1, ["pmi"], False)
+    io(T.jrow[:, :], [[1, 16]], 0, 0, 16, ["jrow"])
     sel(T.idb[:, :], T.ones[:, :], [[-1, 128]], Alu.is_equal, 0.0, 0, 1, 128, ["ones"], ["idb"])
     sel(T.bo[:, :], T.ones[:, :], [[-16, 8], [0, 16]], Alu.is_ge, 0.0, 0, 1, 128, ["ones"], ["bo"])
     sel(T.bo[:, :], T.bo[:, :], [[16, 8], [0, 16]], Alu.is_ge, 0.0, 15, -1, 128, ["bo"], ["bo"])
-    io(T.pmi[:, 0:1], [[0, 1]], 0, 1, 1, ["pmi"], False)
-    io(T.jrow[:, 0:16], [[1, 16]], 0, 0, 16, ["jrow"])
-    io(T.jrow[:, 16:48], [[0, 2], [16, 16]], V, 0, 32, ["jrow2"])
-    io(T.cdi[:, 0:32], [[1, 32]], 0, 0, 32, ["cdi"], False)
-    for s, (d, i) in enumerate(PAIRS):
-        io(T.cdi[:, 32 + NB * s:32 + NB * s + NB], [[BM, NB]], i - d, 0, NB, ["cdi%d" % s], False)
-        io(T.cdi[:, 96 + NB * s:96 + NB * s + NB], [[16 * BM, NB]], 16 * i, 0, NB, ["cdj%d" % s], False)
     ts(T.pmi[:, 4:5], T.pmi[:, 0:1], 15, None, Alu.bitwise_and, None, 1, ["pmi"], ["pmi2"])
     cp(T.pmf[:, 0:1], T.pmi[:, 4:5], 1, ["pmi2"], ["pmf"])
-    ts(T.rmt[:, 0:16], T.jrow[:, 0:16], T.pmf[:, 0:1], None, Alu.is_equal, None, 16, ["jrow", "pmf"], ["rmt"])
+    pj = T.pmf[:, 0:1]
+    ts(T.rmt[:, 0:16], T.jrow[:, :], pj, 4096.0, Alu.is_equal, Alu.mult, 16, ["jrow", "pmf"], ["rmt"])
+    add(T.rmt[:, 0:16], T.rmt[:, 0:16], -2048.0, 16, ["rmt"], ["rmt"])
     n = 16
-    while n < R:
-        ac(T.rmt[:, n:2 * n], T.rmt[:, 0:n], n, ["rmt"], ["rmt"], f=Act.Copy); n *= 2
-    ac(T.rmt[:, R:R + 16], T.rmt[:, 0:16], 16, ["rmt"], ["rmt"], f=Act.Copy)
-    ts(T.dum[:, :], T.jrow[:, 16:48], T.pmf[:, 0:1], None, Alu.add, None, 32, ["jrow2", "pmf"], ["dum"])
-    cp(T.cdu[:, 0:NE], T.cdi[:, 0:NE], NE, ["cdi"] + ["cdi%d" % s for s in range(len(PAIRS))], ["cdu"])
-    ts(T.cdu[:, 96:64 + NE], T.cdi[:, 96:64 + NE], T.pmf[:, 0:1], None, Alu.add, None, NE, ["pmf"] + ["cdj%d" % s for s in range(len(PAIRS))], ["cdv"])
-    ts(T.pmf[:, 4:5], T.pmf[:, 0:1], -4096.0, 61440.0, Alu.mult, Alu.add, 1, ["pmf"], ["pmf2"])
-    for c in (256, 384):
-        ac(T.SD[:, c:c + 128], T.idb[:, :], 128, ["idb", "pmf2"], ["cd%d" % c], scale=T.pmf[:, 4:5])
-    for c in (0, 128):
-        ac(T.idf[:, c:c + 128], T.idb[:, :], 128, ["idb"], ["idf%d" % c], f=Act.Copy)
-        ac(T.negi[:, c:c + 128], T.idb[:, :], 128, ["idb"], ["negi%d" % c], scale=-1.0)
-    ac(T.i512[:, :], T.idb[:, :], 128, ["idb"], ["i512"], scale=-512.0)
-    ac(T.ih[:, :], T.idb[:, :], 128, ["idb"], ["ih"], scale=0.5)
-    ac(T.i241[:, :], T.idb[:, :], 128, ["idb"], ["i241"], scale=241.0 * KW)
-    ac(T.boz[:, :], T.bo[:, :], 128, ["bo"], ["boz"], scale=-KW)
-    ac(T.ipen[:, :], T.idb[:, :], 128, ["idb"], ["ipen"], scale=-8192.0)
-    ms(T.fs[:, :], 0.0, 288, ["fs"])
-    cp(T.fs[:, 15:143:16], T.bo[:, 0:128:16], 8, ["bo", "fs"], ["fs"])
-    ac(T.f4k[:, :], T.fs[:, :], 144, ["fs"], ["f4k"], scale=4096.0)
-    ac(T.bon[:, :], T.bo[:, :], 128, ["bo"], ["bon"], scale=-1.0)
-    ac(T.boh[:, :], T.bo[:, :], 128, ["bo"], ["boh"], scale=-KW / 2)
-    ms(T.W[:, :], 0.0, 232, ["W"])
-    WOF = {"mzA": 0, "mpA": 24, "mzB": 48, "mpB": 72, "wa": 96, "wb": 120, "wc": 144, "mC": 160, "dB": 168, "wb2": 192}
-    for name, cs in (("mzA", (2, 0, KW)), ("mpA", (0, -2, -KW)), ("mzB", (-2, 0, -KW)), ("mpB", (0, 2, KW)),
-                     ("wa", (-1, 1)), ("wb", (1, -1)), ("wc", (-KW, -KW)), ("mC", (2 * KW,)),
-                     ("dB", (1, 0, KW / 2)), ("wb2", (0, -1, -KW / 2))):
-        for b, c in enumerate(cs):
-            if c:
-                o = WOF[name] + 8 * b
-                ts(T.W[:, o:o + 8], T.bo[:, 0:128:16], float(c), None, Alu.mult, None, 8, ["bo", "W"], ["W%d" % o])
-    WR = {k: ["W%d" % (o + 8 * b) for b in range(3)] + ["W"] for k, o in WOF.items()}
-    sel(T.eb[0:24, :], T.ones[0:24, :], [[-2, 8], [0, 16]], Alu.is_ge, 0.0, 0, 1, 128, ["ones"], ["eb"])
-    sel(T.eb[0:24, :], T.eb[0:24, :], [[2, 8], [0, 16]], Alu.is_ge, 0.0, 1, -1, 128, ["eb"], ["eb"])
-    sel(T.eb[0:24, :], T.eb[0:24, :], [[-1, 8], [0, 16]], Alu.not_equal, 1.0, -16, 1, 128, ["eb"], ["eb"])
-    ms(T.ff[:, :], 0.0, 144, ["ff"])
-    cp(T.ff[0:24, 15:143:16], T.eb[0:24, 0:128:16], 8, ["eb", "ff"], ["ff"])
-    ms(T.rsa[:, :], 0.0, 512, ["rsa"])
-    V_(16, 1.0, lambda: vec.memset(T.rsa[:, 0:256:16], -67108864.0), ["rsa"], ["rsa"])
-    ms(T.rsm[:, :], 1.0, 128, ["rsm"])
-    V_(8, 1.0, lambda: vec.memset(T.rsm[:, 0:128:16], 0.0), ["rsm"], ["rsm"])
-    io(T.cnt4k[:, 0:V], [[1, V]], 0, 0, V, ["cnt_lo"])
-    io(T.cnt4k[:, V:R], [[1, V]], V, 0, V, ["cnt_hi"])
-    ac(T.tt0[:, :], T.bo[:, :], 128, ["bo"], ["tt0"], scale=4096.0)
-    sel(T.tt0[:, :], T.tt0[:, :], [[1, 128]], Alu.is_ge, 0.0, 0, -1, 128, ["tt0"], ["tt0"])
-    sel(T.tt0[:, :], T.tt0[:, :], [[1, 128]], Alu.not_equal, -4096.0, 0, -1, 128, ["tt0"], ["tt0"])
+    while n < 1024:
+        cp(T.rmt[:, n:2 * n], T.rmt[:, 0:n], n, ["rmt"], ["rmt"], 0.5); n *= 2
+    cp(T.rmt[:, 1024:2048], T.rmt[:, 0:1024], 1024, ["rmt"], ["rmt1"], 0.5)
+    cp(T.rmt[:, 2048:3072], T.rmt[:, 0:1024], 1024, ["rmt"], ["rmt2"], 0.5)
+    ac(T.rmt[:, 3072:R], T.rmt[:, 0:1024], 1024, ["rmt"], ["rmt3"], f=Act.Copy)
+    ac(T.rmt[:, R:R + 16], T.rmt[:, 0:16], 16, ["rmt"], ["rmt4"], f=Act.Copy)
+    bo8 = T.bo[:, 0:128:16]
+    for q in (0, 1):
+        for c in (0, 1):
+            S = hs(T.SH, 2 * q + c)
+            sel(S, T.ones[:, :], [[-16, 8], [0, 2], [-1, 8]], Alu.is_equal, 0.0, -8 * q, 1, 128, ["ones"], ["SH%d%d" % (q, c)])
+            sel(S, S, [[0, 8], [1, 2], [0, 8]], Alu.is_equal, 0.0, -c, 0, 128, ["SH%d%d" % (q, c)], ["SH%d%d" % (q, c)])
+    SH = ["SH00", "SH01", "SH10", "SH11"]
+    ms(T.fs[:, :], 0.0, 144, ["fs"])
+    ac(T.fs[:, 15:143:16], bo8, 8, ["bo", "fs"], ["fs"], f=Act.Copy)
+    ac(T.win[:, R:R + 2 * L:2], T.zt[:, :], L, ["zt0", "zt1"], ["z0#0", "z1#0"], f=Act.Copy)
+    ac(T.win[:, R + 1:R + 2 * L:2], T.zt[:, :], L, ["zt0", "zt1"], ["zd#0"], f=Act.Copy)
+    for q in range(4):
+        add(T.P[:, 512 * q:512 * q + 512], T.pari[:, 512 * q:512 * q + 512], -2048.0, 512, ["pari%d" % q], ["P%d" % q])
+    cp(T.XU[:, 0:16], T.reci[:, :], 16, ["reci"], ["XT#0"])
+    ts(T.XU[:, 16:32], T.reci[:, :], 0.5, -0.25, Alu.mult, Alu.add, 16, ["reci"], ["XU#0"])
+    cp(T.thf[:, 8:8 + RO], T.thi[:, 0:RO], RO, ["thi"], ["thf0"])
+    for c, s in ((0, -1.0), (128, -BIG)): ac(T.negi[:, c:c + 128], T.idb[:, :], 128, ["idb"], ["negi%d" % c], scale=s)
+    WOF = {"mzA": 0, "mpA": 24, "wa": 48, "mzB": 64, "mpB": 88, "wb": 112}
+    ms(T.W[:, :], 0.0, 160, ["W"])
+    WS = ((0, 1, 2.0), (16, 1, KW), (32, 1, -2 * BIG), (40, 1, -KW), (48, 1, -1.0), (56, 1, BIG), (128, 2, -KW), (144, 1, -KW), (152, 1, 2 * KW))
+    for o, s, c in WS: ac(T.W[:, o:o + 8 * s:s], bo8, 8, ["bo", "W"], ["W%d" % o], scale=c)
+    ac(T.W[:, 64:128], T.W[:, 0:64], 64, ["W%d" % o for o, s, c in WS[:6]], ["W64"], scale=-1.0)
+    WR = ["W64"] + ["W%d" % o for o, s, c in WS]
+    ms(T.KB[0:64, :], 0.0, 512, ["KB"])
+    io(T.KB[0:1, 256:384], [[0, 8], [-8192, 16]], 122880, 0, 128, ["KB"])
+    for o, c in ((0, -512.0), (128, BIG / 2), (256, -120.0 * KW), (384, 30720.0)): fl(T.KB[32:33, o:o + 128], c, 128, ["KB"], (32, 33))
+    for nm, c in (("iq", -0.25), ("ie", 2.0 ** -13), ("ic", 125.0 * KW), ("ig", 126.0 * KW), ("ih", 0.5)):
+        ac(T[nm][:, :], T.idb[:, :], 128, ["idb"], [nm], scale=c)
+    fl(T.rsb[:, :], 0.0, 128, ["rsb"]); fl(T.rsb[:, 0:128:16], -4 * BIG, 8, ["rsb"])
+    sel(T.rsm[:, :], T.ones[:, :], [[0, 8], [1, 16]], Alu.is_gt, 0.0, 0, 0, 128, ["ones"], ["rsm"])
+
+    def shifts(nm, rows, c, flag):
+        F = T[nm]
+        io(F[0:32, :], [[0, 144]], 0, 0, 144, [nm])
+        ac(F[0:32, 15:143:16], rows, 8, ["idb", nm], [nm], scale=c)
+        if flag: sel(F[0:32, 15:143:16], F[0:32, 15:143:16], [[-1, 8]], Alu.not_equal, 2048.0, -flag, 1, 8, [nm], [nm])
+    shifts("FB", T.idb[0:32, 0:8], 0.5, 8)
+    for o, w in ((0, 0), (48, 16)):
+        for a, pat, base in ((0, [[w, 2], [1, 8]], 0), (16, [[w, 2], [2, 4]], 1), (24, [[0, 2], [4, 2], [1, 2]], w + 2),
+                             (32, [[w, 2], [2, 4]], 0), (40, [[4, 2], [1, 2]], w), (44, [[4, 2], [-1, 2]], w + 1)):
+            n = int(np.prod([p[1] for p in pat]))
+            io(T.VR[:, o + a:o + a + n], pat, base, 0, n, ["VR%d" % (o + a)])
+    tt(T.VR[:, 0:96], T.VR[:, 0:96], T.rmt[:, 0:96], Alu.min, 96, ["rmt"], ["VR"] + ["VR%d" % (o + a) for o in (0, 48) for a in (0, 16, 24, 32, 40, 44)])
+    scan(T.VR[:, 96:192], T.rsb[:, 0:96], T.VR[:, 0:96], Alu.add, Alu.max, 96, ["VR", "rsb"], ["VS"])
+    for o, a, c in ((0, 144, 0.0), (3, 144, 8.0), (6, 96, 0.0)): add(T.cl[:, o:o + 3], T.VR[:, a + 15:a + 48:16], c, 3, ["VS"], ["cl%d" % o])
+    ms(T.I17[:, :], 1.0, 408, ["I17"])
+    for a, b, w in ((0, 272, 34), (272, 408, 17)):
+        I = T.I17[:, a:b]
+        sel(I, I, [[0, 8], [-1, w]], Alu.is_ge, 0.0, 15, 0, b - a, ["I17"], ["I17"])
+        sel(I, I, [[-16, 8], [-1, w]], Alu.is_equal, 0.0, 0, 1, b - a, ["I17"], ["I17"])
+    mm([(T.k0[:, 0:408], T.bo[:, :], T.I17[:, :], True, True, 408)], ["bo", "I17"], ["K0", "@k0"])
+    ac(T.B17[:, :], T.k0[:, 0:408], 408, ["K0"], ["B17", "@k0"], scale=-KW)
+    ac(T.E17[:, :], T.I17[:, :], 408, ["I17"], ["E17"], scale=-BIG)
+    ms(T.KC[0:64, :], 0.0, 408, ["KC"])
+    io(T.KC[0:1, :], [[0, 24], [-8192, 17]], 122880, 0, 408, ["KC"])
+    ms(T.KC[32:33, :], 120 * KW, 408, ["KC"])
+    sel(T.KC[0:33, 0:272], T.KC[0:33, 0:272], [[0, 8], [-1, 34]], Alu.is_ge, -127.0 * KW, 15 + 32 * 64, -64, 272, ["KC"], ["KC"])
+    fl(T.KC[0:64, 16:408:17], 0.0, 24, ["KC"], (0, 64))
+    fl(T.KC[32:33, 288:408:17], -125.0 * KW, 8, ["KC"], (32, 33))
+    fl(T.KC[32:33, 16:272:34], 30720.0, 8, ["KC"], (32, 33))
+    io(T.LF[:, :], [[256, 10], [0, 8]], -2048, 2, 80, ["LF"])
+    ac(T.LQ[:, :], T.LF[:, :], 80, ["LF"], ["LQ"], f=Act.Copy)
+    add(T.xl[:, :], T.reci[:, :], -2048.0, 16, ["reci"], ["xl"])
+    cp(T.ju[:, :], T.jrow[:, :], 16, ["jrow"], ["ju"])
+    tt(T.XN[:, 0:L], T.xl[:, :].indirect(T.ju[:, :]), T.rmt[:, 0:L], Alu.min, L, ["xl", "ju", "rmt"], ["xv"], GA)
+    mm([(T.k1[:, 0:L], T.bo[:, :], T.XN[:, 0:L], True, True, L)], ["bo", "xv"], ["K1", "@k1"])
+    ac(T.XB[:, 0:L], T.k1[:, 0:L], L, ["K1"], ["xb0#0", "xb1#0", "@k1"], bias=30720.0)
+    io(T.MK[:, :], [[0, 16], [1, 16]], 0, 0, 256, ["MK"])
+    ts(T.MK[:, :], T.MK[:, :], pj, 131072.0, Alu.is_le, Alu.mult, 256, ["MK", "pmf"], ["MK"], 0.5)
     for j in range(16):
-        sel(T.tri[:, 128 * j:128 * j + 128], T.tt0[:, :], [[0, 8], [1, 16]], Alu.is_equal, 0.0, -j, 0, 128, ["tt0"], ["tri%d" % j])
-    cp(T.P[:, 0:1024], T.pari[:, 0:1024], 1024, ["pari0"], ["P"])
-    cp(T.P[:, 1024:V], T.pari[:, 1024:V], 1024, ["pari1"], ["P"])
-    cp(T.thf[:, 0:RO], T.thi[:, 0:RO], RO, ["thi"], ["thf"])
-    ts(T.XU[:, 0:16], T.reci[:, :], 0.5, -0.25, Alu.mult, Alu.add, 16, ["reci"], ["XU0"])
-    cp(T.XU[:, 16:32], T.reci[:, :], 16, ["reci"], ["XU0b"])
-    cp(T.XU[:, 32:48], T.reci[:, :], 16, ["reci"], ["XU0c"])
+        sel(hs(T.SJ, j), T.ones[:, :], [[-16, 8], [0, 16]], Alu.is_equal, 0.0, -j, 1, 128, ["ones"], ["SJ%d" % j])
+    ms(T.EC[:, :], -1.0, 512, ["EC"])
+    sel(T.EC[:, :], T.EC[:, :], [[-32, 2], [-1, 16], [0, 16]], Alu.is_equal, 0.0, 0, 1, 512, ["EC"], ["EC"])
+    ac(T.pmf[:, 2:3], pj, 1, ["pmf"], ["pmf2"], bias=float(V))
+    ac(T.dum[:, :], T.jrow[:, :], 16, ["jrow", "pmf2"], ["dum"], bias=T.pmf[:, 2:3], scale=16.0)
+    io(T.rsc[:, :], [[0, 408]], 0, 0, 408, ["rsc"]); fl(T.rsc[:, 0:272:34], -4 * BIG, 8, ["rsc"]); fl(T.rsc[:, 272:408:17], -4 * BIG, 8, ["rsc"])
+    io(T.EB[0:32, :], [[0, 384]], -1, 0, 384, ["EB"])
+    sel(T.EB[0:32, 0:128], T.EB[0:32, 0:128], [[-2, 8], [0, 16]], Alu.is_equal, 0.0, 0, 1, 128, ["EB"], ["EB"])
+    sel(T.EB[0:32, 128:384], T.EB[0:32, 128:384], [[16, 2], [-1, 8], [0, 16]], Alu.is_equal, 0.0, -16, 1, 256, ["EB"], ["EB"])
+    shifts("FX", T.idb[0:32, 0:16:2], 1.0, 0)
+    shifts("FQ", T.idb[0:32, 1:16:2], 1.0, 24)
+    add(T.thf[:, 0:RO], T.thi[:, 0:RO], 7.5, RO, ["thi"], ["thf"])
 
     Pw, Pall, prof = T.P[:, 0:V], T.P[:, 0:V + L], T.win[:, 0:R]
-    PZ, PQ, KB, MB = [T.rz0, T.rz1], [T.rp0, T.rp1], [T.k0, T.k1], [T.m0, T.m1]
+    KK, MM = [T.k0, T.k1], [T.m0, T.m1]
     HS = (1, 0)
-    NQ = 16 // DUP
-    HC = (None,)
-    DB = {}; seq = [("mzB", 1), ("mzB", 0), ("mzC", 1), ("mzC", 0)]
-    for n, e in enumerate(seq):
-        DB[e] = [b for b in (1, 0) if P16 or all(u in ABS for u in seq[n:] if u[1] == b) and not (b == 0 and n == 0)]
 
-    def gather(w, U, name, uname, h):
-        m = 128 // GCH
-        for c in range(GCH):
-            a = 128 * h + m * c
-            if (name, h, c) in VG:
-                cp(w[:, 16 * a:16 * (a + m)], prof.indirect(U[:, a:a + m]), 16 * m, ["prof", uname], ["%s%d_%d" % (name, h, c)], GA)
-            else:
-                ac(w[:, 16 * a:16 * (a + m)], prof.indirect(U[:, a:a + m]), 16 * m, ["prof", uname], ["%s%d_%d" % (name, h, c)], f=Act.Copy, per=GA)
+    def gather(name, U, uname, h):
+        for c in (0, 1):
+            n = 2 if (name, h, c) in CUT else 1
+            for u in range(n):
+                a = 128 * h + 64 * c + 32 * u; o = 1024 * h + 512 * u; r = "%s%d_%d" % (name, h, c)
+                move((name, h, c, u) if n > 1 else (name, h, c), T[name][:, o:o + 1024 // n, c], prof.indirect(U[:, a:a + 64 // n]), 1024 // n,
+                     ["prof", uname], [r + "b"] if u else [r] + [r + "b"] * (n == 1), GA)
 
-    def wres(name, h): return ["%s%d_%d" % (name, h, c) for c in range(GCH)]
+    def sums(name, h, outs, wmat, bank):
+        for u in (0, 1):
+            mm([(outs(k + 8 * u), T[name][:, 1024 * h + k:1024 * h + 1024:8, u], wmat, False, False, 64) for k in range(8)],
+               ["%s%d_%d" % (name, h, u), "%s%d_%db" % (name, h, u), bank] + WR, [])
 
-    def mins(w, wname, mname, bank, bname, h, outs, wmat, wr):
-        m = T[mname]; s = mname[1]
-        for c in range(2):
-            a = 2048 * h + 1024 * c; bn = "r%s%d" % (s, c)
-            tt(m[:, a:a + 1024], w[:, a:a + 1024], T[bn][:, :, :], Alu.min, 1024, ["%s%d_%d" % (wname, h, c), bn, "@" + bn], ["%s%d_%d" % (mname, h, c)], MINC)
-        mm([(outs(k), m[:, 2048 * h + k:2048 * (h + 1):16], wmat, False, False, 64) for k in range(16)],
-           ["%s%d_0" % (mname, h), "%s%d_1" % (mname, h), "@k%d" % h] + wr, [])
+    def mins(name, mname, h, outs, wmat, bank):
+        m = T[mname]; bn = "r%s%d" % (mname[1], h)
+        for q in (0, 1):
+            a = 2048 * h + 1024 * q; r = "%s%d_%d" % (mname, h, q)
+            tt(m[:, a:a + 1024], T[name][:, 1024 * h + q:1024 * h + 1024:2, :], T[bn][:, :, :], Alu.min, 1024,
+               ["%s%d_%s" % (name, h, u) for u in ("0", "0b", "1", "1b")] + [bn, "@" + bn], [r], 0.5)
+            mm([(outs(2 * (e // 2) + q + 8 * (e % 2)), m[:, a + e:a + 1024:8], wmat, False, False, 64) for e in range(8)], [r, bank] + WR, [])
 
-    def turn(s, h, src, sname):
-        bn = "r%s0" % s; o = 512 * (s == "p") + 256 * h; two = ["%sd%d_%d" % (s, h, i) for i in (0, 1)]
-        for i in (0, 1): ac(T.pd[:, o + i:o + 256:2], src, 128, [sname], [two[i]], f=Act.Copy)
-        def fn():
-            for c in (0, 1): ins = pe.transpose(T[bn][:, 8 * c:8 * c + 8, :], T.pd[:, o + 128 * c:o + 128 * c + 128], T.idb[:, :])
-            return ins
-        op("P", 256 * PCY, fn, two + ["idb"], [bn, "@" + bn], lat=60.0)
-        ac(T.zd[:, o:o + 256], T[bn][:, 0:16, :], 256, [bn], ["%sT%d" % (s, h), "@" + bn], f=Act.Copy)
+    def lists(nm, hh, b, o, rd, more=()):
+        for i, h in enumerate(hh):
+            a = o + 128 * i
+            its = [(MM[b][:, a + 64 * q:a + 64 * q + 64], hs(T.SH, 2 * q + c), T[nm + "h"][:, 128 * h + c:128 * h + 128:2], 64) for q in (0, 1) for c in (0, 1)]
+            its += list(more)
+            mm([it[0:3] + (k == 0, k == len(its) - 1, it[3]) for k, it in enumerate(its)], SH + rd, ["sh%d" % b, "@m%d" % b])
+        add(T[nm + "u"][:, 128 * hh[0]:128 * hh[-1] + 128], MM[b][:, o:o + 128 * len(hh)], 2048.0, 128 * len(hh),
+            ["sh%d" % b], ["%su%d" % (nm, h) for h in hh] + ["@m%d" % b])
 
     def fill(s, h):
-        for c in range(2):
-            bn = "r%s%d" % (s, c); o = 512 * (s == "p") + 256 * h + 128 * c
-            def fn(o=o, bn=bn):
-                for k in range(0, 16, 2): ins = pe.transpose(T[bn][:, :, k:k + 2], T.zd[:, o:o + 128], T.idb[:, :])
-                return ins
-            op("P", 1024 * PCY, fn, ["%sT%d" % (s, h), "idb"], [bn, "@" + bn], lat=60.0)
+        bn = "r%s%d" % (s, h); o = 256 * h
+        turn([(T[bn][:, 64 * c:64 * c + 64, k:k + 2], T[s + "T"][:, o + 128 * c:o + 128 * c + 128]) for c in (0, 1) for k in range(0, 8, 2)],
+             ["%sT%d" % (s, h)], [bn, "@" + bn])
 
-    def mins4(w, wname, mname, bank, bname, h, outs, wmat, wr):
-        m = T[mname]; n = 128 * DUP; c0 = 0; br = [bname]
-        if P16:
-            bank, bname, c0 = (T.pq0, "pq0", n * h) if mname[1] == "z" else (T.pq1, "pq1", n * h)
-            br = ["%s_%d" % (bname, i) for i in range(DUP)]
-        for q in range(NQ):
-            a = 2048 * h + n * q; r = "%s%d_%d" % (mname, h, q)
-            tt(m[:, a:a + n], w[:, 128 * h:128 * h + 128, DUP * q:DUP * q + DUP], bank[:, c0:c0 + n], Alu.min, n, wres(wname, h) + br + ["@" + bname], [r], MINC)
-            mm([(outs(DUP * q + i), m[:, a + i:a + n:DUP], wmat, False, False, 64) for i in range(DUP)], [r, "@k%d" % h] + wr, [])
-
-    def dists(w, wname, mname, src, sname, banks, h, outs, wmat, wr):
-        m = T[mname]
-        for q in range(4):
-            b = banks[q % len(banks)]; bank = PZ[b]; bn = "pz%d" % b
-            a = 2048 * h + 512 * q; r = "%s%d_%d" % (mname, h, q); its = []
-            for i in range(4):
-                its += [(bank[:, 128 * i:128 * i + 128], T.idb[:, :], w[:, 2048 * h + 4 * q + i:2048 * (h + 1):16], True, False, 128),
-                        (bank[:, 128 * i:128 * i + 128], T.negi[:, 0:128], src, False, True, 128)]
-            mm(its, wres(wname, h) + ["idb", "negi0", sname], [bn, "@" + bn])
-            ac(m[:, a:a + 512], bank[:, :], 512, [bn], [r, "@" + bn], f=Act.Abs)
-            mm([(outs(4 * q + i), m[:, a + 128 * i:a + 128 * i + 128], wmat, False, False, 64) for i in range(4)], [r, "@k%d" % h] + wr, [])
-
-    def sums(w, wname, h, outs, wmat, wr):
-        mm([(outs(k), w[:, 2048 * h + k:2048 * (h + 1):16], wmat, False, False, 64) for k in range(16)], wres(wname, h) + ["@k%d" % h] + wr, [])
-
-    def dup(bank, bname, src, sname):
-        mm([(bank[:, i:128 * DUP:DUP], T.idb[:, :], src, True, True, 128) for i in range(DUP)], ["idb", sname], [bname, "@" + bname])
+    def column(nm, genes, rd, b):
+        move(nm + "h", T[nm + "h"][:, :], Pw.indirect(genes), L, rd, [nm + "h"], GA)
+        for hh in (((1,), (0,)) if nm in SPLIT else ((0, 1),)): lists(nm, hh, b, 128 + 128 * hh[0], [nm + "h"])
 
     for t in range(RO):
         lastv = t == RO - 1
         times.clear(); visit[0] = t
-        xo = 48 * t
-        gxu, xu, xtu = T.XU[:, xo:xo + 16], T.XU[:, xo + 16:xo + 32], T.XU[:, xo + 32:xo + 48]
-        XR = ["XU0", "XU0b", "XU0c"] if t == 0 else ["XU%d" % t]
-        zo = R + L * t
-        def zz(h): return T.win[:, zo + 128 * h:zo + 128 * h + 128]
-        def hs(buf, h): return buf[:, 128 * h:128 * h + 128]
-        ZR = ["z%d_%d" % (t, h) for h in (0, 1)]
-        cp(T.Au[:, :], Pw.indirect(gxu), L, ["P"] + XR, ["Au"], GA)
-        ac(T.rm[:, :], T.rmt[:, :].indirect(xtu), L, ["rmt"] + XR, ["rm"], f=Act.Copy, per=GA)
-        tt(T.yv[:, :], Pw.indirect(gxu), T.rm[:, :], Alu.mult, L, ["P", "rm"] + XR, ["yv"], GA)
-        mm([(T.m1[:, 0:16], T.fs[:, 15 - j:143 - j], T.yv[:, j:L:16], j == 0, j == 15, 256) for j in range(16)], ["fs", "yv"], ["yl", "@m1"])
-        ts(T.YU[:, 0:16], T.m1[:, 0:16], 0.5, -0.25, Alu.mult, Alu.add, 16, ["yl"], ["gyu", "@m1"])
-        cp(T.YU[:, 16:32], T.m1[:, 0:16], 16, ["yl"], ["yu", "@m1"])
-        ac(T.YS[:, 16:32], T.m1[:, 0:16], 16, ["yl"], ["ys1", "@m1"], f=Act.Copy)
-        gyu, yu = T.YU[:, 0:16], T.YU[:, 16:32]
-        cp(T.Bu[:, :], Pw.indirect(gyu), L, ["P", "gyu"], ["Bu"], GA)
-        ac(T.pp[:, :], prof.indirect(yu), L, ["prof", "yu"], ["pp"], f=Act.Copy, per=GA)
-        ac(T.Af[:, :], Pw.indirect(gxu), L, ["P"] + XR, ["Af"], f=Act.Copy, per=GA)
-        ac(T.Bf[:, :], Pw.indirect(gyu), L, ["P", "gyu"], ["Bf"], f=Act.Copy, per=GA)
-        tt(T.eqab[:, :], Pw.indirect(gyu), T.Af[:, :], Alu.is_equal, L, ["P", "gyu", "Af"], ["eqab"], GA)
-        ac(T.nrm[:, :], T.rm[:, :], L, ["rm"], ["nrm"], bias=1.0, scale=-1.0)
-        mm([(T.m0[:, 0:L], T.ipen[:, :], T.rm[:, :], True, False, 256), (T.m0[:, 0:L], T.idf[:, 0:128], T.Af[:, :], False, True, 1024)],
-           ["ipen", "rm", "idf0", "Af"], ["ab", "@m0"])
-        ac(T.Ab[:, :], T.m0[:, 0:L], L, ["ab"], ["Ab", "@m0"], f=Act.Relu)
-        ac(T.YS[:, 0:16], T.dum[:, 0:16], 16, ["dum"], ["ys0"], bias=float(zo - V))
-        ts(T.GL[:, 0:16], gxu, 4096.0, None, Alu.add, None, 16, XR, ["gl0"])
-        ts(T.GL[:, 16:32], gyu, 4096.0, None, Alu.add, None, 16, ["gyu"], ["gl1"])
-        ac(T.gbc[:, 0:L], T.cnt4k[:, 0:V].indirect(gxu), L, ["cnt_lo"] + XR, ["gbc0"], bias=4096.0, per=GA)
-        ac(T.gbc[:, L:2 * L], T.cnt4k[:, 0:V].indirect(gyu), L, ["cnt_lo", "gyu"], ["gbc1"], bias=4096.0, per=GA)
-        scol = T.thf[:, 0:1] if t == 0 else T.cf[:, 4:5]
-        ac(T.SD[:, 0:256], T.negi[:, :], 256, ["negi0", "negi128", "thf", "scol"], ["SD"], scale=scol)
+        xo = 48 * t; tg = "#%d" % t; nt = "#%d" % (t + 1)
+        xtu, gxu, gyu, yu = T.XU[:, xo:xo + 16], T.XU[:, xo + 16:xo + 32], T.XU[:, xo + 32:xo + 48], T.YU[:, :]
+        XR = ["XU#0", "XT#0"] if t == 0 else ["XU" + tg]
+        PR = ["P%d" % q for q in range(4)] if t == 0 else ["P"]
+        zo = R + 2 * L * t
+        def zz(h): return T.win[:, zo + 256 * h:zo + 256 * h + 256:2]
+        ZR = ["z%d%s" % (h, tg) for h in (0, 1)]
+        def vv(h, a, b): return T.VV[:, 64 * t + 32 * h + a:64 * t + 32 * h + b]
+        def xb(h): return T.XB[:, L * t + 128 * h:L * t + 128 * h + 128]
+        ac(T.rm[:, :], T.rmt[:, :].indirect(xtu), L, ["rmt", "rmt1", "rmt2", "rmt3", "rmt4"] + XR, ["rm"], f=Act.Copy, per=GA)
+        tt(T.yv[:, :], Pw.indirect(gxu), T.rm[:, :], Alu.min, L, PR + ["rm"] + XR, ["yv"], GA)
+        column("A", gxu, PR + XR, 0)
+        mm([(T.m1[:, 0:16], T.fs[:, 15 - j:143 - j], T.yv[:, j:L:16], j == 0, j == 15, 64) for j in range(16)], ["fs", "yv"], ["yl", "@m1"])
+        ts(gyu, T.m1[:, 0:16], 0.5, 16383.75, Alu.mult, Alu.add, 16, ["yl"], ["gyu" + tg, "@m1"])
+        add(yu, T.m1[:, 0:16], 32768.0, 16, ["yl"], ["yu", "@m1"])
+        column("B", gyu, PR + ["gyu" + tg], 1)
+        for c in (0, 1): move("pp%d" % c, T.pp[:, c:2 * L:2], prof.indirect(yu), L, ["prof", "yu"], ["pp%d" % c], GA)
         for h in HS:
-            K = KB[h]; kb = "@k%d" % h; M = MB[h]; mb = "@m%d" % h; H = str(h)
-            if h == HS[0]:
-                for u in HS: turn("z", u, zz(u), ZR[u])
-                for u in HS: turn("p", u, hs(T.pp, u), "pp")
-            fill("z", h); fill("p", h)
-            mm([(K[:, 0:384], T.ones[:, :], T.SD[:, 0:384], True, False, 384)], ["ones", "SD", "cd256"], ["K" + H, kb])
-            o24 = lambda k, K=K: K[:, k:384:16]
-            o16 = lambda k, K=K: K[:, k:256:16]
+            bn = "rz%d" % h; o = zo + 256 * h
+            turn([(T[bn][:, 16 * c:16 * c + 16, :], T.win[:, o + 128 * c:o + 128 * c + 128]) for c in (0, 1)], [ZR[h], "zd#0"], [bn, "@" + bn])
+            move("zT%d" % h, T.zT[:, 256 * h:256 * h + 256], T[bn][:, 0:32, :], 256, [bn], ["zT%d" % h, "@" + bn])
+            fill("z", h)
+        turn([(T.rp0[:, 16 * c:16 * c + 16, :], hs(T.pp, c)) for c in range(4)], ["pp0", "pp1"], ["rp0", "@rp0"])
+        move("pT", T.pT[:, :], T.rp0[:, 0:64, :], 512, ["rp0"], ["pT0", "pT1", "@rp0"])
+        for h in HS: fill("p", h)
+        mm([(T.m0[:, 0:L], T.idb[:, :], T.Ah[:, :], True, False, 256), (T.m0[:, 0:L], T.negi[:, 0:128], T.Bh[:, :], False, True, 256)],
+           ["idb", "negi0", "Ah", "Bh"], ["ab", "@m0"])
+        ac(T.dab[:, :], T.m0[:, 0:L], L, ["ab"], ["dab", "@m0"], f=Act.Abs)
+        mm([(T.m0[:, L:2 * L], T.idb[:, :], T.Ah[:, :], True, False, 256), (T.m0[:, L:2 * L], T.idb[:, :], T.rm[:, :], False, False, 256),
+            (T.m0[:, L:2 * L], T.negi[:, 0:128], T.yv[:, :], False, True, 256)], ["idb", "negi0", "Ah", "rm", "yv"], ["ab", "@m0"])
+        ac(T.Ab[:, :], T.m0[:, L:2 * L], L, ["ab"], ["Ab", "@m0"], f=Act.Copy)
+        cp(T.GL[:, :], T.XU[:, xo + 16:xo + 48], 32, XR + ["gyu" + tg], ["GL"])
+        move("GX", T.GX[:, :], T.GL[:, :].indirect(T.cl[:, 0:6]), 96, ["GL", "cl0", "cl3"], ["GX"], GA)
+        scol = T.thf[:, 8:9] if t == 0 else T.cf[:, 2:3]
+        ac(T.SD[:, :], T.negi[:, :], 256, ["negi0", "negi128", "thf0", "scol"], ["SD"], scale=scol)
+        for h in HS:
+            K = KK[h]; kb = "@k%d" % h; M = MM[h]; mb = "@m%d" % h; H = str(h)
+            mm([(K[:, 0:384], T.ones[0:33, :], T.KB[0:33, 0:384], True, False, 384)], ["ones", "KB"], ["K" + H, kb])
             wm = lambda nm, n: T.W[:, WOF[nm]:WOF[nm] + n]
-            gather(T.wa, T.Au, "wa", "Au", h)
-            mins(T.wa, "wa", "mzA", PZ[h], "pz" + H, h, o24, wm("mzA", 24), WR["mzA"])
-            sums(T.wa, "wa", h, o16, wm("wa", 16), WR["wa"])
-            mins(T.wa, "wa", "mpA", PQ[h], "pq" + H, h, o24, wm("mpA", 24), WR["mpA"])
-            gather(T.wb, T.Bu, "wb", "Bu", h)
-            if ("mzB", h) in ABS:
-                sums(T.wb, "wb", h, o24, wm("wb2", 24), WR["wb2"])
-                mm([(K[:, 0:128], zz(h), T.bon[:, :], False, False, 128), (K[:, 256:384], zz(h), T.boh[:, :], False, False, 128)], [ZR[h], "bon", "boh", kb], [])
-            else:
-                sums(T.wb, "wb", h, o16, wm("wb", 16), WR["wb"])
-            mm([(K[:, 0:128], hs(T.eqab, h), T.i512[:, :], False, False, 128), (K[:, 0:128], hs(T.rm, h), T.i512[:, :], False, False, 128)],
-               ["eqab", "rm", "i512", kb], [])
-            if ("mzB", h) in ABS: dists(T.wb, "wb", "mzB", zz(h), ZR[h], DB[("mzB", h)], h, o24, wm("dB", 24), WR["dB"])
-            else: mins(T.wb, "wb", "mzB", PZ[h], "pz" + H, h, o24, wm("mzB", 24), WR["mzB"])
-            mins(T.wb, "wb", "mpB", PQ[h], "pq" + H, h, o24, wm("mpB", 24), WR["mpB"])
-            so = 256 * h
-            mm([(K[:, 256:384], hs(T.Bf, h), T.idf[:, 0:128], False, True, 512)], ["Bf", "idf0"], ["K" + H, kb])
-            ac(hs(T.Xb, h), K[:, 0:128], 128, ["K" + H], ["Xb" + H, kb], f=Act.Relu, scale=-1024.0)
-            tt(hs(T.wt, h), K[:, 128:256], hs(T.Xb, h), Alu.is_ge, 128, ["K" + H, "Xb" + H], ["wt" + H, kb])
-            tt(hs(T.wk, h), K[:, 256:384], hs(T.wt, h), Alu.mult, 128, ["K" + H, "wt" + H], ["wk" + H, kb])
-            V_(128, 1.0, lambda h=h, so=so: vec.tensor_tensor_scan(T.sc[:, so:so + 128], T.rsa[:, 0:128], hs(T.wk, h), 0.0, Alu.add, Alu.max),
-               ["rsa", "wk" + H], ["sc" + H])
-            V_(128, 0.5, lambda h=h: vec.tensor_tensor_scan(hs(T.cs, h), T.rsm[:, :], hs(T.wt, h), 0.0, Alu.mult, Alu.add), ["rsm", "wt" + H], ["cs" + H])
-            ko, vo, bo_ = 16 * h, 32 * h, 48 * h
-            cp(T.ki[:, ko:ko + 8], T.sc[:, so + 15:so + 128:16], 8, ["sc" + H], ["ki" + H])
-            ts(T.vi[:, vo:vo + 16:2], T.ki[:, ko:ko + 8], 1, 0x7C0, Alu.logical_shift_right, Alu.bitwise_and, 8, ["ki" + H], ["vh" + H])
-            ts(T.vi[:, vo + 1:vo + 16:2], T.ki[:, ko:ko + 8], 1, 63, Alu.logical_shift_right, Alu.bitwise_and, 8, ["ki" + H], ["vl" + H])
-            ac(T.VV[:, bo_ + 32:bo_ + 40], T.cs[:, 128 * h + 15:128 * h + 128:16], 8, ["cs" + H], ["vn" + H], f=Act.Relu, bias=24576.0, scale=-8192.0)
-            cp(T.VV[:, bo_ + 16:bo_ + 32], T.vi[:, vo:vo + 16], 16, ["vh" + H, "vl" + H], ["vv" + H])
-            to = 384 * h
-            mm([(M[0:24, 0:128], T.VV[:, bo_ + 16:bo_ + 40], T.idb[:, :], True, True, 128)], ["vv" + H, "vn" + H, "idb"], ["vt" + H, mb])
-            ac(T.vts[0:24, to:to + 128], M[0:24, 0:128], 128, ["vt" + H], ["vts" + H, mb], f=Act.Copy)
-            mm([(M[:, 384:392], T.ff[0:24, 15 - j:143 - j], T.vts[0:24, to + j:to + 128:16], j == 0, j == 15, 64) for j in range(16)],
-               ["ff", "vts" + H], ["li" + H, mb])
-            ts(T.GC[:, 8 * h:8 * h + 8], M[:, 384:392], float(V - 1), None, Alu.min, None, 8, ["li" + H], ["gc" + H, mb])
-            ac(T.NS[:, 8 * h:8 * h + 8], M[:, 384:392], 8, ["li" + H], ["ns" + H, mb], f=Act.Copy)
+            for nm in "AB":
+                w = "w" + nm.lower()
+                gather(w, T[nm + "u"], nm + "u" + H, h)
+                sums(w, h, lambda k: K[:, k:256:16], wm(w, 16), kb)
+                for s in "zp": mins(w, "m" + s + nm, h, lambda k: K[:, k:384:16], wm("m" + s + nm, 24), kb)
+            mm([(K[:, 0:256], T.ones[:, :], T.SD[:, :], False, False, 256), (K[:, 0:128], hs(T.rm, h), T.iq[:, :], False, False, 128)],
+               ["ones", "SD", "rm", "iq", kb], [])
+            mm([(K[:, 0:128], hs(T.dab, h), T.ie[:, :], False, False, 128), (K[:, 256:384], hs(T.Bh, h), T.idb[:, :], False, True, 128)],
+               ["dab", "ie", "Bh", "idb"], ["K" + H, kb])
+            ac(hs(T.Xb, h), K[:, 0:128], 128, ["K" + H], ["Xb" + H, kb], bias=-BIG / 2, scale=BIG * 8192)
+            tt(hs(T.nw, h), K[:, 128:256], hs(T.Xb, h), Alu.min, 128, ["K" + H, "Xb" + H], ["nw" + H, kb])
+            tt(hs(T.wk, h), K[:, 256:384], hs(T.nw, h), Alu.min, 128, ["K" + H, "nw" + H], ["wk" + H, kb])
+            ac(hs(T.Xb, h), hs(T.nw, h), 128, ["nw" + H], ["Xb" + H], f=Act.Sign)
+            scan(hs(T.sb, h), T.rsb[:, :], hs(T.wk, h), Alu.add, Alu.max, 128, ["rsb", "wk" + H], ["sb" + H])
+            scan(hs(T.cs, h), T.rsm[:, :], hs(T.Xb, h), Alu.mult, Alu.add, 128, ["rsm", "Xb" + H], ["cs" + H], 0.5)
+            top = T.sb[:, 128 * h + 15:128 * h + 128:16]; tb = T.tb[:, 32 * h:32 * h + 8]
+            ts(tb, top, MG, MG, Alu.add, Alu.subtract, 8, ["sb" + H], ["tb" + H])
+            tt(vv(h, 16, 24), top, tb, Alu.subtract, 8, ["sb" + H, "tb" + H], ["vr" + H + tg])
+            ac(vv(h, 24, 32), T.cs[:, 128 * h + 15:128 * h + 128:16], 8, ["cs" + H], ["vn" + H + tg], f=Act.Sign, bias=-11.0, scale=-1.0)
+            mm([(M[0:16, 0:128], vv(h, 16, 32), T.idb[:, :], True, True, 128)], ["vr" + H + tg, "vn" + H + tg, "idb"], ["vt" + H, mb])
+            move("vtb", T.vts[0:16, 256 * h:256 * h + 128], M[0:16, 0:128], 128, ["vt" + H], ["vtb" + H, mb], fast=1.0)
+            mm([(M[:, 384:392], T.FB[0:16, 15 - j:143 - j], T.vts[0:16, 256 * h + j:256 * h + 128:16], j == 0, j == 15, 64) for j in range(16)],
+               ["FB", "vtb" + H], ["li" + H, mb])
             gcu = T.GC[:, 8 * h:8 * h + 8]
-            cp(hs(T.Cu, h), Pw.indirect(gcu), 128, ["P", "gc" + H], ["Cu" + H], GA)
-            ac(hs(T.Cf, h), Pw.indirect(gcu), 128, ["P", "gc" + H], ["Cf" + H], f=Act.Copy, per=GA)
-        ac(T.NS[:, 16:32], T.NS[:, 0:16], 16, ["ns0", "ns1"], ["ns2"], f=Act.Copy)
-        ac(T.BS[:, :], T.NS[:, :], 32, ["ns0", "ns1", "ns2"], ["BS"], bias=16384.0, scale=-2.0)
-        tt(T.KE[:, :], T.GL[:, :], T.NS[:, :], Alu.max, 32, ["gl0", "gl1", "ns0", "ns1", "ns2"], ["KE"])
-        tt(T.YB[:, :], T.YS[:, :], T.BS[:, :], Alu.max, 32, ["ys0", "ys1", "BS"], ["YB"])
-        ac(T.gbc[:, 512:16 * NE], T.gbc[:, 0:512].indirect(T.cdu[:, 96:64 + NE]), 16 * NE - 512, ["gbc0", "gbc1", "cdv"], ["gbc2"], f=Act.Copy, per=GA)
-        tt(T.eqd[:, :], T.KE[:, :].indirect(T.cdu[:, 0:NE]), T.gbc[:, :], Alu.is_equal, 16 * NE, ["KE", "cdu", "gbc0", "gbc1", "gbc2"], ["eqd"], GA)
-        if not lastv:
-            ac(T.sg[:, :], T.NS[:, 0:16], 16, ["ns0", "ns1"], ["sg"], f=Act.Sign, bias=-4096.0)
-            mm([(T.m0[:, 440:456], T.ones[:, :], T.sg[:, :], True, True, 64)], ["ones", "sg"], ["cn", "@m0"])
-            A_(16, 1.0, lambda: act.activation(T.cj[:, :], T.m0[:, 440:456], Act.Identity, bias=64.0, scale=-0.5, accum_out=T.cf[:, 0:1]),
-               ["cn"], ["cf", "cj", "@m0"])
-            ac(T.cf[:, 1:2], T.cf[:, 0:1], 1, ["cf"], ["cf1"], bias=-0.46875, scale=0.0625)
-            ac(T.cf[:, 2:3], T.cf[:, 1:2], 1, ["cf1"], ["cf2"], bias=12582912.0)
-            ac(T.cf[:, 3:4], T.cf[:, 2:3], 1, ["cf2"], ["cf3"], bias=16 * 12582912.0, scale=-16.0)
-            ac(T.cf[:, 5:6], T.cf[:, 0:1], 1, ["cf", "cf3"], ["cf5"], bias=T.cf[:, 3:4])
-            ac(T.cf[:, 4:5], T.cf[:, 5:6], 1, ["cf5", "thf"], ["scol"], bias=T.thf[:, t + 1:t + 2])
-        mm([(T.m1[:, 432:400 + NE], T.f4k[:, 15 - j:143 - j], T.eqd[:, 512 + j:16 * NE:16], j == 0, j == 15, 64) for j in range(16)],
-           ["eqd", "f4k"], ["dx", "@m1"])
-        ac(T.dxs[:, 0:NE - 32], T.m1[:, 432:400 + NE], NE - 32, ["dx"], ["dxs", "@m1"], f=Act.Copy)
-        mm([(T.m1[:, 400:432], T.tri[:, 128 * j:128 * j + 128], T.eqd[:, j:512:16], j == 0, False, 64) for j in range(16)]
-           + [(T.m1[:, 400:432], T.idf[:, 0:128], T.GL[:, :], False, False, 256)]
-           + [(T.m1[:, 400 + i:432:BM], T.idb[:, :], T.dxs[:, NB * s:NB * (s + 1)], False, s == len(PAIRS) - 1, 64) for s, (d, i) in enumerate(PAIRS)],
-           ["eqd", "dxs", "idb", "gl0", "gl1", "idf0"] + ["tri%d" % j for j in range(16)], ["dd", "@m1"])
-        tt(T.OF[:, :], T.m1[:, 400:432], T.dum[:, :], Alu.min, 32, ["dd", "dum"], ["OF", "@m1"])
-        cp(T.OU[:, 0:32], T.OF[:, :], 32, ["OF"], ["OU"])
+            ts(gcu, M[:, 384:392], 3071.75, 2047.25, Alu.add, Alu.min, 8, ["li" + H], ["gc" + H, mb])
+            ac(T.BR[:, 8 * h:8 * h + 8], M[:, 384:392], 8, ["li" + H], ["BR" + H, mb], bias=4096.0, scale=8.0)
+            move("Ch%d" % h, hs(T.Ch, h), Pw.indirect(gcu), 128, PR + ["gc" + H], ["Ch" + H], GA)
+            lists("C", (h,), h, 128, ["Ch" + H])
+            mm([(M[:, 256:384], T.bo[:, :], hs(T.yv, h), True, False, 128), (M[:, 256:384], T.ones[0:33, :], T.KB[0:33, 384:512], False, False, 128),
+                (M[:, 384:512], T.idb[:, :], xb(h), False, False, 128), (M[:, 256:384], T.negi[:, 0:128], hs(T.Ch, h), False, False, 128),
+                (M[:, 384:512], T.negi[:, 0:128], hs(T.Ch, h), False, True, 128)],
+               ["Ch" + H, "negi0", "bo", "yv", "ones", "KB", "idb", "xb" + H + tg], ["de" + H, mb])
+            ts(T.eq[:, 256 * h:256 * h + 256], M[:, 256:512], 0.0, None, Alu.is_equal, None, 256, ["de" + H], ["eq" + H, mb])
         for h in HS:
-            K = KB[h]; kb = "@k%d" % h; M = MB[h]; mb = "@m%d" % h; H = str(h)
-            far = ("mzC", h) in ABS
-            if h != HC[0]: fill("z", h); fill("p", h)
-            mm([(K[:, 0:256], T.ones[:, :], T.SD[:, 256:512], True, False, 256), (K[:, 0:128], hs(T.pp, h), T.boz[:, :], False, False, 128)]
-               + ([] if far else [(K[:, 128:256], zz(h), T.boz[:, :], False, False, 128)]),
-               ["ones", "cd256", "cd384", "pp", ZR[h], "boz"], ["K" + H, kb])
-            gather(T.wc, T.Cu, "wc", "Cu" + H, h)
-            tt(hs(T.nex, h), T.cnt4k[:, :].indirect(T.XU[:, xo + 16 + 8 * h:xo + 24 + 8 * h]), hs(T.Cf, h), Alu.not_equal, 128, ["cnt_lo", "cnt_hi", "Cf" + H] + XR, ["nex" + H], GA)
-            tt(hs(T.ney, h), T.cnt4k[:, :].indirect(T.YU[:, 16 + 8 * h:24 + 8 * h]), hs(T.Cf, h), Alu.not_equal, 128, ["cnt_lo", "cnt_hi", "Cf" + H, "yu"], ["ney" + H], GA)
-            mm([(K[:, 0:128], hs(T.nex, h), T.i241[:, :], False, False, 128), (K[:, 128:256], hs(T.ney, h), T.i241[:, :], False, False, 128)],
-               ["nex" + H, "ney" + H, "i241", kb], [])
-            if far:
-                sums(T.wc, "wc", h, lambda k, K=K: K[:, k:128:16], T.W[:, 144:152], WR["wc"])
-                dists(T.wc, "wc", "mzC", zz(h), ZR[h], DB[("mzC", h)], h, lambda k, K=K: K[:, 128 + k:256:16], T.W[:, 144:152], WR["wc"])
-            else:
-                sums(T.wc, "wc", h, lambda k, K=K: K[:, k:256:16], T.W[:, 144:160], WR["wc"])
-                mins(T.wc, "wc", "mzC", PZ[h], "pz" + H, h, lambda k, K=K: K[:, 128 + k:256:16], T.W[:, 160:168], WR["mC"])
-            mins(T.wc, "wc", "mpC", PQ[h], "pq" + H, h, lambda k, K=K: K[:, k:128:16], T.W[:, 160:168], WR["mC"])
-            mm([(K[:, 0:256], hs(T.Cf, h), T.idf[:, :], False, True, 1024)], ["Cf" + H, "idf0", "idf128"], ["K" + H, kb])
-            so, ko, vo, bo_, to = 256 * h, 16 * h, 32 * h, 48 * h, 384 * h
-            V_(256, 1.0, lambda K=K, so=so: vec.tensor_tensor_scan(T.sc[:, so:so + 256], T.rsa[:, :], K[:, 0:256], 0.0, Alu.add, Alu.max),
-               ["rsa", "K" + H], ["sc" + H, kb])
-            cp(T.ki[:, ko:ko + 16], T.sc[:, so + 15:so + 256:16], 16, ["sc" + H], ["ki" + H])
-            ts(T.vi[:, vo:vo + 32:2], T.ki[:, ko:ko + 16], 0xFC0, None, Alu.bitwise_and, None, 16, ["ki" + H], ["vh" + H])
-            ts(T.vi[:, vo + 1:vo + 32:2], T.ki[:, ko:ko + 16], 63, None, Alu.bitwise_and, None, 16, ["ki" + H], ["vl" + H])
-            cp(T.VV[:, bo_:bo_ + 32], T.vi[:, vo:vo + 32], 32, ["vh" + H, "vl" + H], ["vv" + H])
-            mm([(M[0:24, 0:128], T.VV[:, bo_ + 16:bo_ + 40], T.idb[:, :], True, True, 128),
-                (M[0:24, 128:256], T.VV[:, bo_ + 16:bo_ + 40], T.idb[:, :], True, True, 128),
-                (M[0:16, 256:384], T.VV[:, bo_:bo_ + 16], T.idb[:, :], True, True, 128)], ["vv" + H, "vn" + H, "idb"], ["vt" + H, mb])
-            ac(T.vts[0:24, to:to + 256], M[0:24, 0:256], 256, ["vt" + H], ["vts" + H, mb], f=Act.Copy)
-            ac(T.vts[0:16, to + 256:to + 384], M[0:16, 256:384], 128, ["vt" + H], ["vtx" + H, mb], f=Act.Copy)
-            mm([(K[:, 384:400], T.ff[0:24, 15 - j:143 - j], T.vts[0:24, to + j:to + 256:16], j == 0, j == 15, 64) for j in range(16)],
-               ["ff", "vts" + H], ["lj" + H, kb])
-            mm([(M[:, 0:128], T.eb[0:24, :], T.vts[0:24, to:to + 128], True, False, 128), (M[:, 0:128], T.ipen[:, :], hs(T.nrm, h), False, True, 128),
-                  (M[:, 128:256], T.eb[0:16, :], T.vts[0:16, to + 256:to + 384], True, False, 128), (M[:, 128:256], T.ipen[:, :], hs(T.nrm, h), False, True, 128)],
-               ["eb", "ipen", "nrm", "vts" + H, "vtx" + H], ["vt" + H, mb])
-            tt(T.XN[:, 8 * h:8 * h + 8], K[:, 384:392], T.YB[:, 8 * h:8 * h + 8], Alu.min, 8, ["lj" + H, "YB"], ["qf" + H, kb])
-            cp(T.QU[:, 8 * h:8 * h + 8], T.XN[:, 8 * h:8 * h + 8], 8, ["qf" + H], ["qu" + H])
-            tt(T.XN[:, 16 + 8 * h:24 + 8 * h], K[:, 392:400], T.YB[:, 16 + 8 * h:24 + 8 * h], Alu.min, 8, ["lj" + H, "YB"], ["xn" + H, kb])
-            ac(T.yx[:, so:so + 256], M[:, 0:256], 256, ["vt" + H], ["yx" + H, mb], f=Act.Relu)
-            ac(hs(T.qh, h), T.win[:, 0:zo + L].indirect(T.QU[:, 8 * h:8 * h + 8]), 128, ["prof", "qu" + H] + ["z%d_%d" % (u, v) for u in range(t + 1) for v in (0, 1)],
-               ["qh" + H], scale=0.5, per=GA)
-            mm([(K[:, 256:384], T.idb[:, :], hs(T.qh, h), True, False, 128), (K[:, 256:384], T.ih[:, :], zz(h), False, True, 128)],
-               ["idb", "ih", "qh" + H, ZR[h]], ["zp" + H, kb])
-            ac(hs(T.zt, h), K[:, 256:384], 128, ["zp" + H], ["zt" + H, kb], bias=127.75)
-            zs = T.ZS[:, L * t + 128 * h:L * t + 128 * h + 128]
-            ac(zs, hs(T.zt, h), 128, ["zt" + H], ["zs%d_%d" % (t, h)], bias=-128.0)
-            if not lastv:
-                send(T.win[:, zo + L + 128 * h:zo + L + 128 * h + 128], zs, "az%d_%d" % (t + 1, h), ["zs%d_%d" % (t, h)], "z%d_%d" % (t + 1, h))
-            for m in range(8 * h + 8 - BM, 8 * h - 1, -BM):
-                tt(Pall.indirect(T.OU[:, m:m + BM]), T.Ab[:, 16 * m:16 * (m + BM)], T.yx[:, 128 * h + 16 * m:128 * h + 16 * (m + BM)], Alu.add, 16 * BM,
-                   ["OU", "Ab", "yx" + H], ["P"], SCA)
+            H = str(h); M = T.m1; eq = 512 * h
+            kx = lambda a, b: T.KX[:, 48 * h + a:48 * h + b]
+            dx = lambda a, b, c=1: T.dxs[:, 32 * h + a:32 * h + b:c]
+            tt(kx(0, 48), T.BR[:, 8 * h:8 * h + 8].indirect(T.cl[:, 6:9]), T.GX[:, 48 * h:48 * h + 48], Alu.max, 48, ["BR" + H, "GX", "cl6"], ["KX" + H], GA)
+            mm([(M[0:48, 0:128], kx(0, 48), T.idb[:, :], True, True, 128)], ["KX" + H, "idb"], ["kt", "@m1"])
+            move("KT", T.KT[0:48, :], M[0:48, 0:128], 128, ["kt"], ["KT", "@m1"], fast=1.0)
+            mm([(M[:, 0:512], T.KT[0:48, :], T.EC[0:48, :], True, False, 512), (M[:, 0:256], T.idb[:, :], T.MK[:, :], False, False, 256)]
+               + [(M[:, j:512:16], hs(T.SJ, j), kx(0, 32), False, j == 15, 64) for j in range(16)],
+               ["SJ%d" % j for j in range(16)] + ["KX" + H, "idb", "MK", "KT", "EC"], ["df" + H, "@m1"])
+            ts(T.eqd[:, eq:eq + 512], M[:, 0:512], 0.0, None, Alu.is_equal, None, 512, ["df" + H], ["eqd" + H, "@m1"])
+            mm([(M[:, 0:32], T.fs[:, 15 - j:143 - j], T.eqd[:, eq + j:eq + 512:16], j == 0, j == 15, 64) for j in range(16)], ["fs", "eqd" + H], ["dx" + H, "@m1"])
+            ac(dx(0, 32), M[:, 0:32], 32, ["dx" + H], ["dxs" + H, "@m1"], scale=4096.0)
+            its = [(M[:, 64:80], kx(0, 16)), (M[:, 64:80], dx(0, 16)), (M[:, 65:80:2], dx(16, 24))]
+            its += [(M[:, 74 + s:80:4], dx(a + s, a + 4, 2)) for a in (24, 28) for s in (0, 1)]
+            mm([(o, T.idb[:, :], r, i == 0, i == len(its) - 1, 64) for i, (o, r) in enumerate(its)], ["idb", "KX" + H, "dxs" + H], ["dd" + H, "@m1"])
+            tt(T.OF[:, 16 * h:16 * h + 16], M[:, 64:80], T.dum[:, :], Alu.min, 16, ["dd" + H, "dum"], ["OF" + H, "@m1"])
+            cp(T.OU[:, 16 * h:16 * h + 16], T.OF[:, 16 * h:16 * h + 16], 16, ["OF" + H], ["OU" + H])
         if not lastv:
-            xn = T.XN[:, 16:32]
-            ac(T.XV[:, 0:16], xn, 16, ["xn0", "xn1"], ["xv0"], bias=-0.25, scale=0.5)
-            ac(T.XV[:, 16:32], xn, 16, ["xn0", "xn1"], ["xv1"], f=Act.Copy)
-            ac(T.XV[:, 32:48], xn, 16, ["xn0", "xn1"], ["xv2"], bias=float(t + 1))
-            cp(T.XS[:, xo:xo + 48], T.XV[:, :], 48, ["xv0", "xv1", "xv2"], ["xs%d" % t])
-            send(T.XU[:, xo + 48:xo + 96], T.XS[:, xo:xo + 48], "ax%d" % (t + 1), ["xs%d" % t], "XU%d" % (t + 1))
-        tt(T.bb[:, :], Pw.indirect(gyu), T.nrm[:, :], Alu.mult, L, ["P", "gyu", "nrm"], ["bb"], GA)
-        for m in range(16 - BM, -1, -BM):
-            a = 128 * (m // 8) + 128 + 16 * m
-            tt(Pall.indirect(T.OU[:, 16 + m:16 + m + BM]), T.bb[:, 16 * m:16 * (m + BM)], T.yx[:, a:a + 16 * BM], Alu.add, 16 * BM,
-               ["OU", "bb", "yx%d" % (m // 8)], ["P"], SCA)
+            mm([(T.m1[:, 400:408], T.ones[:, :], vv(h, 24, 32), h == 1, h == 0, 64) for h in HS], ["ones", "vn0" + tg, "vn1" + tg], ["cn", "@m1"])
+            A_(8, 1.0, lambda: act.activation(T.cj[:, :], T.m1[:, 400:408], Act.Identity, bias=127.0625, scale=-0.5, accum_out=T.cf[:, 0:1]),
+               ["cn"], ["cf", "cj", "@m1"])
+            ac(T.cf[:, 1:2], T.cf[:, 0:1], 1, ["cf"], ["cf1"], bias=201326592.0)
+            ac(T.cf[:, 3:4], T.cf[:, 1:2], 1, ["cf1"], ["cf2"], bias=201326592.0, scale=-1.0)
+            ac(T.cf[:, 4:5], T.cf[:, 0:1], 1, ["cf", "thf"], ["cf3"], bias=T.thf[:, t + 1:t + 2])
+            ac(T.cf[:, 2:3], T.cf[:, 3:4], 1, ["cf2", "cf3"], ["scol"], bias=T.cf[:, 4:5])
+        for h in HS:
+            K = KK[h]; kb = "@k%d" % h; H = str(h)
+            two = h in APART
+            X, xk, xn_ = (MM[h], "@m" + H, "X" + H) if two else (K, kb, "K" + H)
+            mm([(K[:, 0:272], T.ones[0:33, :], T.KC[0:33, 0:272], True, False, 272),
+                (K[:, 0:272], zz(h), T.B17[:, 0:272], False, False, 272), (K[:, 16:272:34], hs(T.yv, h), bo8, False, False, 64),
+                (K[:, 16:272:34], T.ic[:, :], vv(h, 24, 32), False, False, 64), (K[:, 33:272:34], T.ig[:, :], vv(h, 24, 32), False, False, 64),
+                (K[:, 33:272:34], T.idb[:, :], T.LQ[:, 16 * t + 8 * h:16 * t + 8 * h + 8], False, False, 64)],
+               ["ones", "KC", ZR[h], "B17", "yv", "bo", "ic", "ig", "vn" + H + tg, "idb", "LQ"], ["K" + H, kb])
+            mm([(X[:, 272:408], T.ones[0:33, :], T.KC[0:33, 272:408], two, False, 136),
+                (X[:, 272:408], T.pp[:, 256 * h:256 * h + 256:2], T.B17[:, 272:408], False, False, 136),
+                (X[:, 288:408:17], xb(h), T.idb[:, 0:128:16], False, False, 64)], ["ones", "KC", "pp0", "B17", "idb", "xb" + H + tg], [xn_, xk])
+            gather("wc", T.Cu, "Cu" + H, h)
+            mm([(K[:, 0:272], hs(T.eq, 2 * h), T.E17[:, 0:272], False, False, 272)], ["eq" + H, "E17", kb], [])
+            mm([(X[:, 272:408], hs(T.eq, 2 * h + 1), T.E17[:, 272:408], False, False, 136)], ["eq" + H, "E17", xk], [])
+            if two:
+                sums("wc", h, lambda k: K[:, k:272:34], T.W[:, 144:152], kb)
+                sums("wc", h, lambda k: X[:, 272 + k:408:17], T.W[:, 144:152], xk)
+            else: sums("wc", h, lambda k: K[:, k:408:17], T.W[:, 128:152], kb)
+            mins("wc", "mzC", h, lambda k: K[:, k:272:34], T.W[:, 152:160], kb)
+            mins("wc", "mpC", h, lambda k: X[:, 272 + k:408:17], T.W[:, 152:160], xk)
+            so = 408 * h; vt = T.vts[0:32, 256 * h + 128:256 * h + 256]
+            for B, bn, nm, a, b, s in ((K, kb, "K" + H, 0, 272, ""), (X, xk, xn_, 272, 408, "x")) if two else ((K, kb, "K" + H, 0, 408, ""),):
+                mm([(B[:, a:b], hs(T.Ch, h), T.I17[:, a:b], False, True, b - a)], ["Ch" + H, "I17"], [nm, bn])
+                scan(T.sc[:, so + a:so + b], T.rsc[:, a:b], B[:, a:b], Alu.add, Alu.max, b - a, ["rsc", nm], ["sc" + s + H, bn])
+                top = T.sc[:, so + a + 16:so + b:17]; tb = T.tb[:, 32 * h + 8 + a // 17:32 * h + 8 + b // 17]
+                ts(tb, top, MG, MG, Alu.add, Alu.subtract, 24, ["sc" + s + H], ["tc" + s + H])
+                tt(vv(h, a // 17, b // 17), top, tb, Alu.subtract, 24, ["sc" + s + H, "tc" + s + H],
+                   ["vy" + H + tg] * (not s) + ["vr" + H + tg] * (s == "x" or not two))
+                rows, src, dst = (8, vv(h, 16, 24), T.vts[0:8, 256 * h:256 * h + 128]) if s else (32, vv(h, 0, 32), vt)
+                mm([(B[0:rows, 0:128], src, T.idb[:, :], True, True, 128)], ["vy" + H + tg, "vr" + H + tg, "vn" + H + tg, "idb"], ["vt" + s + H, bn])
+                move("vtc", dst, B[0:rows, 0:128], 128, ["vt" + s + H], ["vtb" + H if s else "vtc" + H, bn], fast=1.0)
+                parts = [(1, T.EB[0:8, 256:384])] if s else [(0, T.EB[0:32, 0:128])] + ([] if two else [(1, T.EB[0:32, 128:256])])
+                its = []
+                for w, E in parts: its += [(B[:, 128 + 128 * w:256 + 128 * w], T.idb[:, :], hs(T.rm, h)), (B[:, 128 + 128 * w:256 + 128 * w], E, dst)]
+                if not (s or lastv): its += [(B[:, 0:128], T.EB[0:32, 0:128], dst)]
+                mm([it + (k == 0, k == len(its) - 1, 128) for k, it in enumerate(its)], ["idb", "rm", "EB", "vtb" + H if s else "vtc" + H], ["vt" + s + H, bn])
+                a, b = 128 * parts[0][0], 128 * parts[-1][0] + 128
+                ac(T.yx[:, 256 * h + a:256 * h + b], B[:, 128 + a:128 + b], b - a, ["vt" + s + H], ["y%d%s" % (w, H) for w, E in parts] + [bn], f=Act.Relu)
+            for F, o, nm, bank in ((T.FX, T.k1[:, 408 + 8 * h:416 + 8 * h], "xn", "@k1"), (T.FQ, K[:, 424:432], "ql", kb)):
+                mm([(o, F[0:32, 15 - j:143 - j], T.vts[0:32, 256 * h + 128 + j:256 * h + 256:16], j == 0, j == 15, 64) for j in range(16)],
+                   ["FX", "FQ", "vtc" + H], [nm + H, bank])
+            add(T.QU[:, 8 * h:8 * h + 8], K[:, 424:432], 4096.0, 8, ["ql" + H], ["qu" + H, kb])
+            if not lastv:
+                o = L * (t + 1) + 128 * h
+                ac(T.XN[:, o:o + 128], K[:, 0:128], 128, ["vt" + H], ["xs" + H + tg, kb], scale=-1.0)
+                send(T.XB[:, o:o + 128], T.XN[:, o:o + 128], "at%d_%d" % (t + 1, h), ["xs" + H + tg], "xb" + H + nt)
+            ac(hs(T.qh, h), T.win[:, 0:zo + 2 * L].indirect(T.QU[:, 8 * h:8 * h + 8]), 128,
+               ["prof", "qu" + H, "zd#0"] + ["z%d#%d" % (v, u) for u in range(t + 1) for v in (0, 1)], ["qh" + H], bias=-0.25, scale=0.5, per=GA)
+            mm([(K[:, 0:128], T.idb[:, :], hs(T.qh, h), True, False, 128), (K[:, 0:128], T.ih[:, :], zz(h), False, True, 128)],
+               ["idb", "ih", "qh" + H, ZR[h]], ["zp" + H, kb])
+            o = 2 * L * t + 256 * h
+            zs = [T.ZS[:, o - 128 * h:o - 128 * h + 128]] if lastv else [T.ZS[:, o + c:o + 256:2] for c in (0, 1)]
+            ac(hs(T.zt, h), K[:, 0:128], 128, ["zp" + H], ["zt" + H, kb], bias=128.0)
+            for c, out in enumerate(zs): ac(out, hs(T.zt, h), 128, ["zt" + H], ["zs" + "ab"[c] + H + tg], bias=-128.0)
+            if not lastv:
+                send(T.win[:, R + 2 * L + o:R + 2 * L + o + 256], T.ZS[:, o:o + 256], "az%d_%d" % (t + 1, h), ["zsa" + H + tg, "zsb" + H + tg], "z" + H + nt)
+            for m in (6, 4, 2, 0):
+                a = 128 * h + 16 * m
+                tt(Pall.indirect(T.OU[:, 16 * h + m:16 * h + m + 2]), T.Ab[:, a:a + 32], T.yx[:, 128 * h + a:128 * h + a + 32], Alu.subtract, 32,
+                   ["OU" + H, "Ab", "y0" + H], PR + ["P"], SCA)
+        xn = T.k1[:, 408:424]; so = 32 * t
+        if not lastv:
+            ts(T.XS[:, so + 16:so + 32], xn, 0.5, 1023.75, Alu.mult, Alu.add, 16, ["xn0", "xn1"], ["xs" + tg, "@k1"])
+            add(T.XS[:, so:so + 16], xn, 2049.0 + t, 16, ["xn0", "xn1"], ["xt" + tg, "@k1"])
+            send(T.XU[:, xo + 48:xo + 80], T.XS[:, so:so + 32], "ax%d" % (t + 1), ["xs" + tg, "xt" + tg], "XU" + nt)
+        else:
+            ac(T.XO[:, :], xn, 16, ["xn0", "xn1"], ["XO", "@k1"], bias=2048.0)
+        tt(T.bb[:, :], Pw.indirect(gyu), T.rm[:, :], Alu.max, L, ["P", "gyu" + tg, "rm"], ["bb"], GA)
+        for h, m in ((1, 4), (1, 0), (0, 4), (0, 0)):
+            a = 128 * h + 16 * m; o = 128 * h + 128 + a
+            tt(Pall.indirect(T.OU[:, 16 * h + 8 + m:16 * h + 12 + m]), T.bb[:, a:a + 64], T.yx[:, o:o + 64], Alu.subtract, 64,
+               ["OU%d" % h, "bb", "y1%d" % h], ["P"], SCA)
     t = RO - 1
-    dma("S", T.yrec[:, :], T.XN[:, 16:32], "st0", 2000.0, ["xn0", "xn1"], [])
-    dma("S", T.yz[:, :], T.ZS[:, L * t:L * t + L], "st1", 2000.0, ["zs%d_0" % t, "zs%d_1" % t], [])
-    dma("S", T.ypar[:, 0:1024], T.P[:, 0:1024], "st2", 4000.0, ["P"], [])
-    dma("A", T.ypar[:, 1024:V], T.P[:, 1024:V], "st3", 4000.0, ["P"], [])
+    dma("S", T.yrec[:, :], T.XO[:, :], "st4", 2000.0, ["XO"], [])
+    dma("S", T.yz[:, :], T.ZS[:, 2 * L * t:2 * L * t + L], "st5", 2000.0, ["zsa0#%d" % t, "zsa1#%d" % t], [])
+    for q in range(4):
+        a, o = T.P[:, 512 * q:512 * q + 512], T.PO[:, 512 * q:512 * q + 512]
+        if q % 2: ac(o, a, 512, ["P"], ["out%d" % q], bias=2048.0)
+        else: add(o, a, 2048.0, 512, ["P"], ["out%d" % q])
+        dma("SA"[q % 2], T.ypar[:, 512 * q:512 * q + 512], o, "st%d" % q, 3000.0, ["out%d" % q], [])
     return ops, nsent[0]
 
 
 def schedule(ops):
-    n = len(ops)
-    busy = [o["busy"] for o in ops]; eng = [o["eng"] for o in ops]
-    pre = [[] for _ in range(n)]; suc = [[] for _ in range(n)]
-    for i, o in enumerate(ops):
-        for j in list(o["deps"]) + o["after"]:
-            d = ops[j]
-            same = d["eng"] == o["eng"] and not o["deps"].get(j, False) and d["sem"] is None
-            gap = 0.0 if same else d["lat"] + WAKE
-            pre[i].append((j, gap)); suc[j].append((i, gap))
-
-    def place(seq, edges, base):
-        end = [0.0] * n; line = {}
-        for i in seq:
-            t = base[i]
-            for j, gap in edges[i]:
-                if end[j] + gap > t: t = end[j] + gap
-            if eng[i] is not None:
-                ln = line.setdefault(eng[i], []); k = len(ln)
-                while k > 0 and ln[k - 1][1] > t: k -= 1
-                while k < len(ln) and ln[k][0] < t + busy[i]:
-                    t = max(t, ln[k][1]); k += 1
-                ln.insert(k, (t, t + busy[i]))
-            end[i] = t + busy[i]
-        return end
-
-    lat = [o["lat"] for o in ops]; zero = [0.0] * n
     rng = np.random.default_rng(SEED)
-    tail = [0.0] * n
-    for i in range(n - 1, -1, -1): tail[i] = busy[i] + max([tail[s] + gp for s, gp in suc[i]] + [lat[i]])
-    key = [-tail[i] for i in range(n)]
-    best = None
-    for rnd in range(ROUNDS):
-        for i in range(n):
-            for j, gap in pre[i]:
-                if key[i] <= key[j]: key[i] = key[j] + 1e-3
-        end = place(sorted(range(n), key=lambda i: key[i]), pre, zero)
-        span = max(end[i] + lat[i] for i in range(n))
-        if best is None or span < best[0]: best = (span, end)
-        use = end if rnd % 4 else best[1]
-        noise = rng.random(n) * NOISE
-        key = [-use[i] - float(noise[i]) for i in range(n)]
-        for i in range(n - 1, -1, -1):
-            for s, gap in suc[i]:
-                if key[i] <= key[s]: key[i] = key[s] + 1e-3
-        back = place(sorted(range(n), key=lambda i: key[i]), suc, lat)
-        key = [-back[i] for i in range(n)]
-    kin = {}
-    for i, o in enumerate(ops): kin.setdefault(o["kin"], []).append(i)
-    kins = list(kin.values())
-    vis = [o["vis"] for o in ops]
-    sub = [i for i in range(n) if vis[i] in (1, 2)]
-    per = best[0] / RO
-    off = {ops[i]["kin"]: best[1][i] - busy[i] - per * vis[i] for i in range(n) if vis[i] <= 2}
-    for i in range(n): off.setdefault(ops[i]["kin"], per)
-    names = sorted(set(ops[i]["kin"] for i in sub))
-    spre = [[e for e in pre[i] if vis[e[0]] in (1, 2)] for i in range(n)]
-    ssuc = [[e for e in suc[i] if vis[e[0]] in (1, 2)] for i in range(n)]
+    num = {"V": 0, "A": 1, "P": 2, "G": 3, "S": 4, None: -1}
 
-    def keys(o, idx, p, s, back):
-        key = [0.0] * n
-        for i in idx: key[i] = o[ops[i]["kin"]] + per * max(vis[i], 0)
-        if back:
-            for i in idx[::-1]:
-                for j, gap in s[i]:
-                    if key[i] >= key[j]: key[i] = key[j] - 1e-3
-        else:
-            for i in idx:
-                for j, gap in p[i]:
-                    if key[i] <= key[j]: key[i] = key[j] + 1e-3
-        return sorted(idx, key=lambda i: key[i])
+    def improve(idx, kin, base, off, rounds, hot, mark, free):
+        n = len(idx); at = {x: i for i, x in enumerate(idx)}; every = range(n)
+        busy = [ops[x]["busy"] for x in idx]; eng = [num[ops[x]["eng"]] for x in idx]; vis = [ops[x]["vis"] for x in idx]
+        lat = [ops[x]["lat"] if ops[x]["sem"] else 0.0 for x in idx]; pre = []; anc = []
+        for x in idx:
+            o = ops[x]; l = []; a = 0
+            for j in list(o["deps"]) + o["after"]:
+                if j in at:
+                    d = ops[j]
+                    same = d["eng"] == o["eng"] and (not o["deps"].get(j, False) or d["eng"] == "P") and d["sem"] is None
+                    l.append((at[j], 0.0 if same else d["lat"] + WAKE)); a |= anc[at[j]] | (1 << at[j])
+            anc.append(a)
+            pre.append([(j, gp) for j, gp in l if not any(k != j and anc[k] >> j & 1 and busy[k] + g2 >= gp for k, g2 in l)])
 
-    now = None; top = None
-    for rnd in range(STEADY):
-        o = dict(off)
-        for u in range(int(rng.integers(1, 4)) if rnd else 0):
-            o[names[int(rng.integers(len(names)))]] += float(rng.normal()) * (3000.0 if rng.random() < 0.5 else 800.0)
-        if rng.random() < 0.3:
-            key = {}
-            for i in sub[::-1]:
-                k = o[ops[i]["kin"]] + per * vis[i]
-                for j, gap in ssuc[i]: k = min(k, key[j] - 1e-3)
+        def decode(o):
+            key = [0.0] * n; end = [0.0] * n; why = [-1] * n; last = [-1] * 5; idle = [0.0] * 5
+            for i in every:
+                k = o[kin[i]] + base[i]
+                for j, gp in pre[i]:
+                    if k <= key[j]: k = key[j] + 1e-3
                 key[i] = k
-                if vis[i] == 1: o[ops[i]["kin"]] = k - per
-        end = place(keys(o, sub, spre, ssuc, False), spre, zero)
-        span = max(end)
-        if now is None or span <= now + TEMP * (1.0 - rnd / STEADY) * float(rng.random()): now = span; off = o
-        if top is None or span < top[0]: top = (span, o)
-    if top is not None:
-        end = place(keys(top[1], list(range(n)), pre, suc, False), pre, zero)
-        span = max(end[i] + lat[i] for i in range(n))
-        if span < best[0]: best = (span, end)
-    cur = best
-    for rnd in range(MOVES):
-        key = [cur[1][i] - busy[i] for i in range(n)]
-        for u in range(int(rng.integers(1, 4))):
-            d = float(rng.normal()) * (3000.0 if rng.random() < 0.5 else 800.0)
-            for i in kins[int(rng.integers(len(kins)))]: key[i] += d
-        if rng.random() < 0.5:
-            for i in range(n):
-                for j, gap in pre[i]:
-                    if key[i] <= key[j]: key[i] = key[j] + 1e-3
-        else:
-            for i in range(n - 1, -1, -1):
-                for s, gap in suc[i]:
-                    if key[i] >= key[s]: key[i] = key[s] - 1e-3
-        end = place(sorted(range(n), key=lambda i: key[i]), pre, zero)
-        span = max(end[i] + lat[i] for i in range(n))
-        if span <= cur[0] + TEMP * (1.0 - rnd / MOVES) * float(rng.random()): cur = (span, end)
-        if span < best[0]: best = (span, end)
-    end = best[1]; order = {}
-    for i in sorted(range(n), key=lambda i: (end[i] - busy[i], i)):
-        if eng[i] is not None: order.setdefault(eng[i], []).append(i)
-    return order, [end[i] + lat[i] for i in range(n)]
+            seq = sorted(every, key=lambda i: key[i]); span = 0.0
+            for i in seq:
+                e = eng[i]
+                if e >= 0: t = idle[e]; w = -2 - last[e]
+                else: t = 0.0; w = -1
+                for j, gp in pre[i]:
+                    if end[j] + gp >= t: t = end[j] + gp; w = j
+                t += busy[i]; end[i] = t; why[i] = w
+                if e >= 0: idle[e] = t; last[e] = i
+                if t + lat[i] > span: span = t + lat[i]; z = i
+            return span, end, key, why, z, seq
+
+        def arcs(now):
+            i = now[4]; why = now[3]; out = []
+            while why[i] != -1:
+                if why[i] <= -2:
+                    if free[i] or free[-2 - why[i]]: out.append((-2 - why[i], i))
+                    i = -2 - why[i]
+                else: i = why[i]
+            return out
+
+        now = decode(off); top = (now, off); ar = arcs(now); loose = [i for i in every if free[i]]
+        for it in range(1, rounds + 1):
+            o = off[:]; end, key = now[1], now[2]; r = rng.random(6)
+            if it % 64 == 0:
+                zero = min(end[i] - busy[i] - key[i] for i in mark)
+                for i in mark: o[kin[i]] = end[i] - busy[i] - base[i] - zero
+            elif r[0] < 0.8 and ar:
+                a = int(r[1] * len(ar)); u, v = ar[a]
+                if r[2] < 0.5:
+                    while a + 1 < len(ar) and ar[a + 1][1] == ar[a][0] and rng.random() < 0.6: a += 1
+                    u = ar[a][0]
+                if free[v] and (r[3] < 0.5 or not free[u]):
+                    todo = [(v, key[u] - 1e-2)]
+                    while todo:
+                        x, k = todo.pop(); o[kin[x]] = min(o[kin[x]], k - base[x])
+                        todo += [(j, k - 1e-2) for j, gp in pre[x] if key[j] >= k and vis[j] == vis[x]]
+                else: o[kin[u]] = key[v] + 1e-2 - base[u] + (r[4] * 1500.0 if r[5] < 0.3 else 0.0)
+            else: o[kin[loose[int(r[1] * len(loose))]]] += float(rng.normal()) * (2000.0 if r[2] < 0.3 else 500.0)
+            new = decode(o)
+            if new[0] <= now[0] or rng.random() < np.exp((now[0] - new[0]) / (hot * (COLD / hot) ** (it / rounds))):
+                now, off = new, o; ar = arcs(now)
+                if new[0] < top[0][0]: top = (new, o)
+        now = top[0]
+        return now[0], {x: now[1][i] - busy[i] for i, x in enumerate(idx)}, [idx[i] for i in now[5]]
+
+    def calls(idx, key, rounds, hot, free):
+        n = len(idx)
+        return improve(idx, list(range(n)), [0.0] * n, [key[x] for x in idx], rounds, hot, list(range(n)), [free(ops[x]["vis"]) for x in idx])
+
+    n = len(ops); vis = [o["vis"] for o in ops]; kin = [o["kin"] for o in ops]
+    plan = {k: 10.0 * int(v) for k, v in (e.split(":") for e in PLAN.split())}
+    sub = [i for i in range(n) if vis[i] in (1, 2)]; names = sorted(set(kin[i] for i in sub))
+    span, start, seq = improve(sub, [names.index(kin[i]) for i in sub], [PERIOD * vis[i] for i in sub],
+                               [plan.get(k[0] + "'" * (k[1] - 1), -2000.0) for k in names], STEADY, HOT,
+                               [i for i, x in enumerate(sub) if vis[x] == 2], [True] * len(sub))
+    first = {v: min(start[i] for i in sub if vis[i] == v and kin[i][0] == "yv") for v in (1, 2)}
+    per = first[2] - first[1]; off = {kin[i]: start[i] - first[2] for i in sub if vis[i] == 2}; key = [0.0] * n
+    for i in range(n - 1, -1, -1):
+        if kin[i] in off: key[i] = off[kin[i]] + per * vis[i]
+        else: key[i] = min([key[s] - ops[i]["busy"] - WAKE for s in range(i + 1, n) if i in ops[s]["deps"]] + [per * RO])
+    for i in range(n):
+        if vis[i] < 0 and ops[i]["eng"] in "GS": key[i] = i - 2 * per
+        elif vis[i] < 0 and key[i] < EARLY[ops[i]["eng"]]: key[i] -= per
+    span, start, seq = calls([i for i in range(n) if vis[i] <= 1], key, MOVES, HOT, lambda v: v < 1)
+    at = {kin[i]: start[i] for i in start if vis[i] == 1}
+    for i in range(n): key[i] = start[i] if vis[i] <= 1 else at.get(kin[i], max(at.values())) + per * (vis[i] - 1)
+    rear = [i for i in range(n) if vis[i] >= RO - 2]
+    span, start, seq = calls(rear, key, MOVES // 2, HOT / 2, lambda v: v == RO - 1)
+    i = min(rear, key=lambda i: key[i]); zero = key[i] - start[i]
+    for i in rear: key[i] = start[i] + zero
+    span, start, seq = calls(list(range(n)), key, MOVES // 8, HOT / 4, lambda v: True)
+    order = {}
+    for i in seq:
+        if ops[i]["eng"] is not None: order.setdefault(ops[i]["eng"], []).append(i)
+    return order, [start[i] + ops[i]["busy"] + ops[i]["lat"] for i in range(n)]
 
 
 def rank_program(g, core, T, topo):
@@ -615,5 +591,5 @@ def rank_program(g, core, T, topo):
                 else: queue[e].wait_ge(T.sem["s" + ops[w]["eng"]], count[w])
             ins = ops[i]["fn"]()
             if i in marked: ins.then_inc(T.sem["s" + e], 1)
-    for s in ("st0", "st1", "st2", "st3"): g.sync.wait_ge(T.sem[s], 16)
+    for s in range(6): g.sync.wait_ge(T.sem["st%d" % s], 16)
     g.wait_ge(T.sem.sent, nsent)

@@ -5,8 +5,8 @@ V, R, L, RO = 2048, 4096, 256, 5
 CUT = tuple((w, h, c) for w in ("wa", "wb", "wc") for h in (0, 1) for c in (0, 1))
 APART = (0,)
 SPLIT = "A"
-VG = (("wa", 1, 1, 0), ("wa", 1, 1, 1), ("wb", 1, 1, 1), ("wb", 0, 1, 1))
-ONV = ("pT", "zT0", "Bh")
+VG = (("wa", 1, 1, 0), ("wa", 1, 1, 1), ("wb", 1, 1, 1), ("wb", 0, 1, 1), ("wc", 0, 1, 1))
+ONV = ("pT1", "zT0", "Bh1")
 KW = 131072.0
 BIG = 67108864.0
 MG = 1.5 * 2.0 ** 36
@@ -16,12 +16,12 @@ SCRATCH = {name: ("sbuf", [128] + list(shape), kind) for kind, bufs in (
     (BF, {"win": [R + RO * 2 * L], "rmt": [R + 16], "SJ": [2048], "MK": [256], "ZS": [RO * 2 * L], "ones": [128], "idb": [128], "negi": [256],
           "bo": [128], "fs": [144], "ih": [128], "iq": [128], "ie": [128], "ic": [128], "ig": [128], "I17": [408], "E17": [408], "B17": [408],
           "KB": [512], "KC": [408], "FB": [144], "FX": [144], "FQ": [144], "EB": [384], "W": [160], "SD": [256], "rsm": [128], "rm": [L],
-          "dab": [L], "eq": [2 * L], "pp": [2 * L], "zT": [2 * L], "pT": [2 * L], "EC": [512], "eqd": [1024], "dxs": [64], "SH": [512],
+          "dab": [L], "dab2": [L], "eq": [2 * L], "pp": [2 * L], "zT": [2 * L], "pT": [2 * L], "EC": [512], "eqd": [1024], "dxs": [64], "SH": [512],
           "wa": [2048, 2], "wb": [2048, 2], "wc": [2048, 2], "mzA": [4096], "mpA": [4096], "mzB": [4096], "mpB": [4096], "mzC": [4096],
           "mpC": [4096], "Xb": [L], "nw": [L], "cs": [L], "qh": [L], "zt": [L]}),
     (HF, {"XB": [RO * L], "XN": [RO * L], "VV": [RO * 64], "LQ": [80], "Ah": [L], "Bh": [L], "Ch": [L], "yv": [L], "KT": [128], "KX": [96],
           "GX": [96], "vts": [512]}),
-    (F32, {"P": [V + L], "PO": [V], "thf": [16], "XO": [16], "xl": [16], "wk": [L], "rsb": [128], "rsc": [408], "pmf": [8], "jrow": [16], "dum": [16],
+    (F32, {"P": [V + L], "PO": [V + L], "thf": [16], "XO": [16], "xl": [16], "wk": [L], "rsb": [128], "rsc": [408], "pmf": [8], "jrow": [16], "dum": [16],
            "LF": [80], "Ab": [L], "bb": [L], "yx": [2 * L], "GL": [32], "BR": [16], "VR": [192], "OF": [32], "sb": [L], "sc": [816], "tb": [64],
            "cj": [8], "cf": [8]}),
     (I32, {"pari": [V], "reci": [16], "thi": [8], "pmi": [8]}),
@@ -32,11 +32,12 @@ SCRATCH.update({name: ("psum", [128, 512], F32) for name in ("k0", "k1", "m0", "
 SEMAPHORES = (["sV", "sA", "sP", "sG", "sent"] + ["ld%d" % i for i in range(8)] + ["st%d" % i for i in range(6)]
               + ["ax%d" % t for t in range(1, RO)] + ["a%s%d_%d" % (s, t, h) for s in "zt" for t in range(1, RO) for h in (0, 1)])
 
-CY, PCY, GA, SCA, CALL, WAKE = 1.0, 0.5, 1.56, 3.8, 60.0, 120.0
-SEED, STEADY, MOVES, HOT, COLD, PERIOD = 1, 20000, 40000, 60.0, 10.0, 35100.0
+CY, PCY, GA, SCA, CALL, WAKE = 0.86, 0.43, 1.56, 3.8, 60.0, 130.0
+SEED, STEADY, MOVES, HOT, COLD, PERIOD = 1, 5000, 40000, 40.0, 10.0, 30550.0
 EARLY = {"V": 3000.0, "A": 9000.0, "P": 0.0}
 PLAN = """rz1:-173 zT1:-120 Ah:-108 rm:-62 sh0:-50 rz1':-37 Au1:-19 SD:-16 yv:0 sh0':14 wa1_0b:16 Au0:46 yl:58 wa1_1:65 wa0_1b:102 K0:109 ones':128 K1:148 gyu:151 yu:163 rz0:167 Bh:175 pp0:188 wa1_1b:221 sh1:233 pp1:234 ab:246 sh1':272 wa1_0:280 ones:285 Bu0:307 wa1_1':319 zT0:339 rp0:345 wb1_1b:358 wb1_0:365 wa1_0':377 pT0:443 wb1_1:451 mzA1_1:475 rp1:487 mzA1_0:532 wb1_0b:537 rp0':538 rz0':589 mpA1_1:589 dab:623 wb1_1':641 mzB1_1:647 wa0_1:655 wb1_0':666 mzA1_1':692 mpB1_0:704 mzA1_0':717 wa0_0:741 mpA1_1':743 mzB1_0:761 mzB1_1':769 mpB1_0':794 mpB1_1:818 wa0_0b:826 mzB1_0':830 mpA1_0:875 mpB1_1':887 wb0_0b:912 mpA0_0:933 mpA1_0':945 K1':970 ab':983 mzA0_0:990 Xb1:1001 wb0_1:1020 mpA0_0':1021 nw1:1047 mzA0_0':1059 wk1:1078 GL:1097 Xb1':1106 sb1:1109 GX:1125 cs1:1137 tb1:1149 vn1:1161 Ab:1173 vr1:1173 wb0_1b:1186 vt1:1198 K1'':1204 vtb1:1222 wb0_0:1241 li1:1253 mzA0_1:1272 wa0_1':1304 gc1:1329 wb0_0':1339 mpB0_0:1341 Ch1:1353 wa0_0':1364 BR1:1379 sh1'':1404 KX1:1404 wb0_1':1416 Cu1:1434 mpA0_1:1453 kt:1465 mpB0_0':1472 KT:1490 mzA0_1':1497 wc1_0b:1508 mzB0_1:1510 df1:1523 mzB0_0:1568 mpA0_1':1587 wc1_1:1594 df1':1612 mpB0_1:1625 mzB0_1':1638 mzB0_0':1664 wc1_0:1680 eq1:1452 mpB0_1':1694 K0':1720 K1''':1732 eqd1:1734 eq1':1746 eq1'':1750 Xb0:1766 wc1_0':1778 wc1_1b:1785 nw0:1797 dx1:1804 wk0:1828 sb0:1858 Xb0':1871 tb0:1889 dxs1:1889 cs0:1902 vr0:1914 dd1:1914 vn0:1926 mzC1_1:1926 vt0:1950 K0'':1957 vtb0:1975 mzC1_0:1984 li0:2006 OF1:2041 mzC1_1':2057 gc0:2075 OU1:2087 BR0:2099 Ch0:2112 KX0:2124 sh0'':2150 kt':2162 Cu0:2180 mzC1_0':2182 KT':2187 eq0:2199 wc1_1':2208 wc0_1b:2211 mpC1_1:2225 df0:2234 mpC1_0:2282 wc0_0:2297 df0':2298 X0:2323 mpC1_1':2337 eqd0:2341 mpC1_0':2362 wc0_1:2383 K1'''':2388 eq0':2408 eq0'':2415 dx0:2418 sc1:2426 wc0_0b:2469 wc0_1':2481 tc1:2485 wc0_1'':2506 vy1:2510 vt1':2534 vtc1:2558 wc0_0':2567 mzC0_1:2567 dxs0:2577 vt1'':2592 mzC0_0:2624 dd0:2631 y01:2636 xs1:2670 xs1':2700 mzC0_1':2654 xn1:2679 mpC0_1:2681 mzC0_0':2731 mpC0_0:2738 K0''':2756 ql1:2770 sc0:2795 wc0_0'':2821 OF0:2829 tc0:2841 mpC0_1':2847 qu1:2853 vy0:2866 qh1:2878 P:2878 vt0':2890 mpC0_0':2897 P':2908 vtc0:2915 zp1:2922 OU0:2927 X0':2935 P'':2939 vt0'':2945 zt1:2953 scx0:2960 y00:2976 P''':2979 xn0:2984 zsb1:2995 tcx0:2998 P'''':3010 zsa1:3014 vr0':3028 cn:3035 ql0:3041 P''''':3041 zsa1':3045 cf:3059 xs:3059 xt:3071 cf1:3084 xs0:3040 xs0':3200 vtx0:3093 cf3:3096 P'''''':3096 xs':3108 qu0:3114 vtb0':3117 P''''''':3127 cf2:3136 vtx0':3148 qh0:3148 bb:3157 zp0:3186 P'''''''':3215 zt0:3217 y10:3190 zsa0:3255 P''''''''':3257 zsb0:3273 scol:3292 P'''''''''':3299 zsa0':3304 P''''''''''':3342"""
 PLAN = """rm:-58 Ah:-12 rz1:-8 yv:0 zT1:34 sh0:46 yl:59 SD:66 Au1:77 wa1_0:108 wa1_1b:108 sh0':110 K0:123 rz0:162 rz1':175 gyu:193 wa1_0b:193 yu:206 Bh:218 K1:226 ones:246 Au0:264 sh1:276 pp0:279 wa1_1:283 sh1':289 pp1:325 Bu0:369 wa0_0b:371 rp0:383 GL:400 ones':409 mzA1_0:413 ab:428 wa1_0':454 wb1_0:457 pT0:470 wa1_1':479 wb1_1b:502 mzA1_0':505 rp1:530 wb1_0b:543 rp0':582 mzA1_1:587 wb1_1:629 mpA1_0:645 mpA1_1:702 wa0_1:715 wb1_1':727 mzA1_1':752 zT0:759 wb1_0':778 mzB1_1:778 wa0_0:801 mpA1_0':803 mpA1_1':829 mpB1_0:835 rz0':855 wa0_1b:886 mpB1_1:892 mzB1_1':906 mpB1_0':931 mzB1_0:949 mpB1_1':961 dab:972 wb0_0b:1004 mzA0_0:1007 mzB1_0':1019 K1':1044 mpA0_0:1064 mzA0_0':1076 Xb1:1090 ab':1101 wb0_1:1109 nw1:1121 wk1:1152 sb1:1183 Xb1':1194 tb1:1213 cs1:1226 vr1:1238 vn1:1250 mpA0_1:1251 vt1:1275 vtb1:1299 wb0_1b:1308 wb0_0:1318 li1:1330 wa0_0':1381 gc1:1399 GX:1404 K1'':1407 mzA0_1:1411 Ch1:1425 K1''':1447 BR1:1451 wa0_1':1463 mpB0_1:1469 sh1'':1489 mzA0_1':1502 Cu1:1526 mpB0_1':1538 KX1:1545 wc1_0:1557 mzB0_1:1558 de1:1563 mpA0_0':1595 eq1:1615 mpA0_1':1621 wc1_1:1643 wb0_0':1647 mzB0_0:1647 mzB0_1':1672 kt:1698 mpB0_0:1704 eq1':1704 wb0_1':1718 KT:1728 mzB0_0':1743 wc1_0b:1747 mpB0_0':1773 K0':1799 df1:1812 Xb0:1833 nw0:1864 wk0:1895 Xb0':1895 wc1_0':1901 Ab:1914 eqd1:1919 wc1_1b:1945 sb0:1977 dx1:1989 cs0:1995 tb0:2008 vn0:2031 vr0:2032 mzC1_0:2045 vt0:2057 K0'':2063 vtb0:2081 dxs1:2100 mzC1_1:2102 li0:2112 eq1'':2163 dd1:2170 gc0:2181 mzC1_0':2192 BR0:2205 OF1:2210 Ch0:2218 wc1_1':2218 KX0:2230 sh0'':2256 kt':2269 mzC1_1':2275 Cu0:2287 KT':2293 mpC1_0:2305 wc0_0b:2317 df0:2324 mpC1_1:2363 wc0_0:2403 mpC1_0':2413 eqd0:2431 de0:2439 mpC1_1':2471 eq0:2489 wc0_1b:2489 K1'''':2497 wc0_0':2517 sc1:2535 dx0:2543 wc0_1:2575 tc1:2594 X0:2594 eq0'':2611 wc0_0'':2617 vy1:2618 OU1:2631 vt1':2643 eq0':2649 vtc1:2667 wc0_1':2673 mzC0_0:2673 dxs0:2686 vt1'':2698 dd0:2730 mzC0_1:2730 y01:2748 mzC0_0':2753 mpC0_0:2787 xn1:2792 mzC0_1':2843 OF0:2844 mpC0_1:2857 K0''':2869 ql1:2882 sc0:2914 mpC0_0':2934 qu1:2952 mpC0_1':2959 tc0:2964 xs1:2976 wc0_1'':2985 vy0:2988 qh1:2995 P:3001 X0':3010 vt0':3017 P':3031 zp1:3033 vtc0:3042 cn:3046 scx0:3049 zt1:3064 P'':3069 vt0'':3072 tcx0:3087 zsa1:3094 xn0:3094 P''':3099 y00:3113 OU0:3117 vr0':3130 zsb1:3132 P'''':3144 ql0:3146 cf:3151 xs:3164 cf1:3175 xt:3176 P''''':3188 vtx0:3197 cf2:3200 xs':3200 qu0:3215 vtb0':3221 P'''''':3227 xs0:3240 zsa1':3250 vtx0':3252 P''''''':3257 qh0:3259 XU:3262 y10:3285 bb:3288 zp0:3297 xs0':3300 cf3:3304 z1:3312 scol:3328 zt0:3340 P'''''''':3345 xs1':3350 xb0:3362 zsa0:3371 P''''''''':3388 zsb0:3390 xb1:3412 zsa0':3421 P'''''''''':3430 P''''''''''':3472 z0:3483"""
+PLAN = """rm:-53 Ah1:-13 rz1:-3 yv:0 SD:10 sh0:23 Ah0:38 Au1:53 yl:53 zT1:61 wa1_1b:83 wa1_0b:89 sh0':97 rz1':108 gyu:158 wa1_0:164 Au0:169 rz0:184 yu:186 Bh1:198 wa1_1:238 pp11:239 sh1:251 sh1':262 K1:273 pp10:279 ones:290 wa1_0':306 Bu0:313 wa0_1:319 rp0:332 mzA1_1:341 pT1:391 wb1_0b:394 zT0:419 rp1:432 mzA1_0:436 wb1_1:469 mzA1_1':476 wb1_1b:486 rz0':498 mzA1_0':542 wb1_0:544 mpA1_1:561 mpA1_0:611 wa0_1b:618 mpA1_1':624 rp0':646 mpB1_1:661 ab:690 wa0_0:693 mpB1_0:711 mpA1_0':712 mpB1_1':734 wa1_1':756 mzB1_0:761 wa0_0b:768 wb1_1':778 wb1_0':800 mzB1_1:811 mpB1_0':822 dab:842 mzB1_0':844 mpA0_0:861 mzB1_1':874 K1':896 ab':907 mzA0_0:911 Xb1:926 K0:940 wb0_1:943 nw1:961 mzA0_0':974 mzA0_1:978 Xb1':1018 wk1:1028 wb0_0b:1035 mzA0_1':1041 sb1:1058 wa0_1':1063 cs1:1075 tb1:1088 GL:1100 vn1:1109 vr1:1113 Ab:1121 wb0_1b:1124 vt1:1137 K1'':1143 vtb1:1162 wb0_0:1179 li1:1192 mpA0_1:1199 wb0_1':1236 gc1:1255 mpA0_0':1258 mzB0_0:1266 Ch1:1279 mpA0_1':1280 BR1:1302 wa0_0':1302 GX:1314 mpB0_0:1316 sh1'':1327 wb0_0':1338 Cu1:1366 mpB0_0':1379 mzB0_1:1383 wc1_0b:1396 mzB0_0':1401 de1:1423 mpB0_1:1433 ones':1451 mzB0_1':1467 wc1_0:1471 eq1:1483 mpB0_1':1496 KX1:1511 K0':1518 kt:1537 Xb0:1548 KT:1565 nw0:1578 wc1_1:1582 df1:1595 wk0:1608 sb0:1638 Xb0':1657 tb0:1668 K1''':1672 wc1_1b:1674 cs0:1687 wc1_0':1687 eqd1:1699 eq1':1709 vr0:1749 vn0:1749 mzC1_1:1762 vt0:1773 dx1:1779 vtb0:1798 mzC1_0:1812 cn:1823 li0:1828 dxs1:1842 cf:1853 mpC1_1:1862 dd1:1872 cf1:1878 eq1'':1892 mzC1_0':1897 cf2:1902 gc0:1912 mzC1_1':1920 OF1:1923 BR0:1936 mpC1_1':1942 Ch0:1948 OU1:1948 KX0:1961 cf3:1971 mpC1_0:1973 sh0'':1984 kt':1995 wc1_1':2001 KT':2020 Cu0:2023 mpC1_0':2036 wc0_0:2053 wc0_1b:2053 K1'''':2058 df0:2076 sc1:2128 wc0_1:2128 de0:2153 eqd0:2172 K0'':2181 wc0_0b:2203 wc0_1':2216 eq0:2222 dx0:2238 tc1:2250 vy1:2275 eq0':2282 mzC0_0:2290 wc0_0':2294 dxs0:2301 scol:2312 vt1':2316 X0:2321 dd0:2335 vtc1:2340 mzC0_1:2340 mzC0_0':2355 vt1'':2377 mpC0_0:2391 mzC0_1':2404 y01:2423 K0''':2426 wc0_0'':2438 OF0:2441 sc0:2457 ql1:2464 OU0:2486 tc0:2499 xn1:2508 P:2511 vy0:2527 P':2540 vt0':2552 qu1:2557 wc0_1'':2558 P'':2570 vtc0:2577 mpC0_0':2580 mpC0_1:2586 qh1:2594 eq0'':2602 vt0'':2608 xs1:2617 xn0:2624 P''':2636 y00:2643 zp1:2668 P'''':2673 mpC0_1':2679 xs:2690 zt1:2698 X0':2701 xt:2701 ql0:2707 P''''':2713 xs':2726 zsb1:2728 scx0:2729 zsa1:2745 P'''''':2747 tcx0:2763 qu0:2775 zsa1':2776 vr0':2788 XU:2789 qh0:2799 P''''''':2799 vtx0:2812 xs0:2823 bb:2829 z1:2839 vtb0':2840 xs0':2853 zp0:2853 vtx0':2870 P'''''''':2882 zt0:2883 y10:2900 xs1':2903 xb0:2916 zsa0:2917 P''''''''':2922 zsb0:2934 P'''''''''':2962 zsa0':2964 xb1:2966 P''''''''''':3002 z0:3027"""
 ORDER = []
 
 
@@ -54,7 +55,7 @@ def build(g, T, topo, core):
             if r in last_w: deps[last_w[r]] = deps.get(last_w[r], False) or not r.startswith("@")
         for r in rd: readers.setdefault(r, []).append(i)
         for r in wr: last_w[r] = i; readers[r] = []
-        name = (list(wr) + list(rd) + ["-"])[0]; nm = name.split("#")[0]
+        name = (list(wr) + list(rd) + ["-"])[0]; nm = "P" if name == "PO" else name.split("#")[0]
         times[nm] = times.get(nm, 0) + 1
         ops.append({"kin": (nm, times[nm], visit[0] < 0), "vis": visit[0], "eng": eng, "busy": busy, "lat": lat, "fn": fn, "deps": deps,
                     "sem": sem, "name": name, "after": list(after)})
@@ -264,8 +265,10 @@ def build(g, T, topo, core):
              ["%sT%d" % (s, h)], [bn, "@" + bn])
 
     def column(nm, genes, rd, b):
-        move(nm + "h", T[nm + "h"][:, :], Pw.indirect(genes), L, rd, [nm + "h"], GA)
-        for hh in (((1,), (0,)) if nm in SPLIT else ((0, 1),)): lists(nm, hh, b, 128 + 128 * hh[0], [nm + "h"])
+        for hh in (((1,), (0,)) if nm in SPLIT else ((0, 1),)):
+            a, n = hh[0], len(hh); names = ["%sh%d" % (nm, h) for h in hh]
+            move(names[-1], T[nm + "h"][:, 128 * a:128 * (a + n)], Pw.indirect(T.XU[:, genes + 8 * a:genes + 8 * (a + n)]), 128 * n, rd, names[::-1], GA)
+            lists(nm, hh, b, 128 + 128 * a, names)
 
     for t in range(RO):
         lastv = t == RO - 1
@@ -281,26 +284,34 @@ def build(g, T, topo, core):
         def xb(h): return T.XB[:, L * t + 128 * h:L * t + 128 * h + 128]
         ac(T.rm[:, :], T.rmt[:, :].indirect(xtu), L, ["rmt", "rmt1", "rmt2", "rmt3", "rmt4"] + XR, ["rm"], f=Act.Copy, per=GA)
         tt(T.yv[:, :], Pw.indirect(gxu), T.rm[:, :], Alu.min, L, PR + ["rm"] + XR, ["yv"], GA)
-        column("A", gxu, PR + XR, 0)
+        column("A", xo + 16, PR + XR, 0)
         mm([(T.m1[:, 0:16], T.fs[:, 15 - j:143 - j], T.yv[:, j:L:16], j == 0, j == 15, 64) for j in range(16)], ["fs", "yv"], ["yl", "@m1"])
         ts(gyu, T.m1[:, 0:16], 0.5, 16383.75, Alu.mult, Alu.add, 16, ["yl"], ["gyu" + tg, "@m1"])
         add(yu, T.m1[:, 0:16], 32768.0, 16, ["yl"], ["yu", "@m1"])
-        column("B", gyu, PR + ["gyu" + tg], 1)
-        for c in (0, 1): move("pp%d" % c, T.pp[:, c:2 * L:2], prof.indirect(yu), L, ["prof", "yu"], ["pp%d" % c], GA)
+        column("B", xo + 32, PR + ["gyu" + tg], 1)
+        for hh in (((1,), (0,)) if "p" in SPLIT else ((0, 1),)):
+            a, n = hh[0], len(hh); bn = "rp%d" % hh[0]
+            for c in (0, 1):
+                names = ["pp%d%d" % (h, c) for h in hh[::-1]]
+                move(names[0], T.pp[:, 256 * a + c:256 * (a + n):2], prof.indirect(T.YU[:, 8 * a:8 * (a + n)]), 128 * n, ["prof", "yu"], names, GA)
+            turn([(T[bn][:, 16 * c:16 * c + 16, :], hs(T.pp, 2 * a + c)) for c in range(2 * n)], ["pp%d%d" % (h, c) for h in hh for c in (0, 1)], [bn, "@" + bn])
+            move("pT%d" % hh[-1], T.pT[:, 256 * a:256 * (a + n)], T[bn][:, 0:32 * n, :], 256 * n, [bn], ["pT%d" % h for h in hh[::-1]] + ["@" + bn])
+            for h in hh[::-1]: fill("p", h)
         for h in HS:
             bn = "rz%d" % h; o = zo + 256 * h
             turn([(T[bn][:, 16 * c:16 * c + 16, :], T.win[:, o + 128 * c:o + 128 * c + 128]) for c in (0, 1)], [ZR[h], "zd#0"], [bn, "@" + bn])
             move("zT%d" % h, T.zT[:, 256 * h:256 * h + 256], T[bn][:, 0:32, :], 256, [bn], ["zT%d" % h, "@" + bn])
             fill("z", h)
-        turn([(T.rp0[:, 16 * c:16 * c + 16, :], hs(T.pp, c)) for c in range(4)], ["pp0", "pp1"], ["rp0", "@rp0"])
-        move("pT", T.pT[:, :], T.rp0[:, 0:64, :], 512, ["rp0"], ["pT0", "pT1", "@rp0"])
-        for h in HS: fill("p", h)
         mm([(T.m0[:, 0:L], T.idb[:, :], T.Ah[:, :], True, False, 256), (T.m0[:, 0:L], T.negi[:, 0:128], T.Bh[:, :], False, True, 256)],
-           ["idb", "negi0", "Ah", "Bh"], ["ab", "@m0"])
+           ["idb", "negi0", "Ah0", "Ah1", "Bh0", "Bh1"], ["ab", "@m0"])
         ac(T.dab[:, :], T.m0[:, 0:L], L, ["ab"], ["dab", "@m0"], f=Act.Abs)
         mm([(T.m0[:, L:2 * L], T.idb[:, :], T.Ah[:, :], True, False, 256), (T.m0[:, L:2 * L], T.idb[:, :], T.rm[:, :], False, False, 256),
-            (T.m0[:, L:2 * L], T.negi[:, 0:128], T.yv[:, :], False, True, 256)], ["idb", "negi0", "Ah", "rm", "yv"], ["ab", "@m0"])
-        ac(T.Ab[:, :], T.m0[:, L:2 * L], L, ["ab"], ["Ab", "@m0"], f=Act.Copy)
+            (T.m0[:, L:2 * L], T.negi[:, 0:128], T.yv[:, :], False, True, 256)], ["idb", "negi0", "Ah0", "Ah1", "rm", "yv"], ["ab", "@m0"])
+        ac(T.Ab[:, :], T.m0[:, L:2 * L], L, ["ab"], ["Ab", "@m0"], bias=2048.0 * lastv)
+        if lastv:
+            for q in range(4): ac(T.PO[:, 512 * q:512 * q + 512], T.P[:, 512 * q:512 * q + 512], 512, ["P"], ["PO%d" % q], bias=2048.0)
+            ac(T.dab2[:, :], T.rm[:, :], L, ["rm"], ["rm2"], bias=2048.0)
+        Wt, WN, W0 = (T.PO, "PO", ["PO%d" % q for q in range(4)]) if lastv else (T.P, "P", PR)
         cp(T.GL[:, :], T.XU[:, xo + 16:xo + 48], 32, XR + ["gyu" + tg], ["GL"])
         move("GX", T.GX[:, :], T.GL[:, :].indirect(T.cl[:, 0:6]), 96, ["GL", "cl0", "cl3"], ["GX"], GA)
         scol = T.thf[:, 8:9] if t == 0 else T.cf[:, 2:3]
@@ -317,7 +328,7 @@ def build(g, T, topo, core):
             mm([(K[:, 0:256], T.ones[:, :], T.SD[:, :], False, False, 256), (K[:, 0:128], hs(T.rm, h), T.iq[:, :], False, False, 128)],
                ["ones", "SD", "rm", "iq", kb], [])
             mm([(K[:, 0:128], hs(T.dab, h), T.ie[:, :], False, False, 128), (K[:, 256:384], hs(T.Bh, h), T.idb[:, :], False, True, 128)],
-               ["dab", "ie", "Bh", "idb"], ["K" + H, kb])
+               ["dab", "ie", "Bh" + H, "idb"], ["K" + H, kb])
             ac(hs(T.Xb, h), K[:, 0:128], 128, ["K" + H], ["Xb" + H, kb], bias=-BIG / 2, scale=BIG * 8192)
             tt(hs(T.nw, h), K[:, 128:256], hs(T.Xb, h), Alu.min, 128, ["K" + H, "Xb" + H], ["nw" + H, kb])
             tt(hs(T.wk, h), K[:, 256:384], hs(T.nw, h), Alu.min, 128, ["K" + H, "nw" + H], ["wk" + H, kb])
@@ -361,9 +372,9 @@ def build(g, T, topo, core):
             tt(T.OF[:, 16 * h:16 * h + 16], M[:, 64:80], T.dum[:, :], Alu.min, 16, ["dd" + H, "dum"], ["OF" + H, "@m1"])
             cp(T.OU[:, 16 * h:16 * h + 16], T.OF[:, 16 * h:16 * h + 16], 16, ["OF" + H], ["OU" + H])
         if not lastv:
-            mm([(T.m1[:, 400:408], T.ones[:, :], vv(h, 24, 32), h == 1, h == 0, 64) for h in HS], ["ones", "vn0" + tg, "vn1" + tg], ["cn", "@m1"])
-            A_(8, 1.0, lambda: act.activation(T.cj[:, :], T.m1[:, 400:408], Act.Identity, bias=127.0625, scale=-0.5, accum_out=T.cf[:, 0:1]),
-               ["cn"], ["cf", "cj", "@m1"])
+            mm([(T.k0[:, 448:456], T.ones[:, :], vv(h, 24, 32), h == 1, h == 0, 64) for h in HS], ["ones", "vn0" + tg, "vn1" + tg], ["cn", "@k0"])
+            A_(8, 1.0, lambda: act.activation(T.cj[:, :], T.k0[:, 448:456], Act.Identity, bias=127.0625, scale=-0.5, accum_out=T.cf[:, 0:1]),
+               ["cn"], ["cf", "cj", "@k0"])
             ac(T.cf[:, 1:2], T.cf[:, 0:1], 1, ["cf"], ["cf1"], bias=201326592.0)
             ac(T.cf[:, 3:4], T.cf[:, 1:2], 1, ["cf1"], ["cf2"], bias=201326592.0, scale=-1.0)
             ac(T.cf[:, 4:5], T.cf[:, 0:1], 1, ["cf", "thf"], ["cf3"], bias=T.thf[:, t + 1:t + 2])
@@ -379,7 +390,7 @@ def build(g, T, topo, core):
                ["ones", "KC", ZR[h], "B17", "yv", "bo", "ic", "ig", "vn" + H + tg, "idb", "LQ"], ["K" + H, kb])
             mm([(X[:, 272:408], T.ones[0:33, :], T.KC[0:33, 272:408], two, False, 136),
                 (X[:, 272:408], T.pp[:, 256 * h:256 * h + 256:2], T.B17[:, 272:408], False, False, 136),
-                (X[:, 288:408:17], xb(h), T.idb[:, 0:128:16], False, False, 64)], ["ones", "KC", "pp0", "B17", "idb", "xb" + H + tg], [xn_, xk])
+                (X[:, 288:408:17], xb(h), T.idb[:, 0:128:16], False, False, 64)], ["ones", "KC", "pp%d0" % h, "B17", "idb", "xb" + H + tg], [xn_, xk])
             gather("wc", T.Cu, "Cu" + H, h)
             mm([(K[:, 0:272], hs(T.eq, 2 * h), T.E17[:, 0:272], False, False, 272)], ["eq" + H, "E17", kb], [])
             mm([(X[:, 272:408], hs(T.eq, 2 * h + 1), T.E17[:, 272:408], False, False, 136)], ["eq" + H, "E17", xk], [])
@@ -407,7 +418,7 @@ def build(g, T, topo, core):
                 mm([it + (k == 0, k == len(its) - 1, 128) for k, it in enumerate(its)], ["idb", "rm", "EB", "vtb" + H if s else "vtc" + H], ["vt" + s + H, bn])
                 a, b = 128 * parts[0][0], 128 * parts[-1][0] + 128
                 ac(T.yx[:, 256 * h + a:256 * h + b], B[:, 128 + a:128 + b], b - a, ["vt" + s + H], ["y%d%s" % (w, H) for w, E in parts] + [bn], f=Act.Relu)
-            for F, o, nm, bank in ((T.FX, T.k1[:, 408 + 8 * h:416 + 8 * h], "xn", "@k1"), (T.FQ, K[:, 424:432], "ql", kb)):
+            for F, o, nm, bank in ((T.FX, T.m1[:, 416 + 8 * h:424 + 8 * h], "xn", "@m1"), (T.FQ, K[:, 424:432], "ql", kb)):
                 mm([(o, F[0:32, 15 - j:143 - j], T.vts[0:32, 256 * h + 128 + j:256 * h + 256:16], j == 0, j == 15, 64) for j in range(16)],
                    ["FX", "FQ", "vtc" + H], [nm + H, bank])
             add(T.QU[:, 8 * h:8 * h + 8], K[:, 424:432], 4096.0, 8, ["ql" + H], ["qu" + H, kb])
@@ -427,28 +438,24 @@ def build(g, T, topo, core):
                 send(T.win[:, R + 2 * L + o:R + 2 * L + o + 256], T.ZS[:, o:o + 256], "az%d_%d" % (t + 1, h), ["zsa" + H + tg, "zsb" + H + tg], "z" + H + nt)
             for m in (6, 4, 2, 0):
                 a = 128 * h + 16 * m
-                tt(Pall.indirect(T.OU[:, 16 * h + m:16 * h + m + 2]), T.Ab[:, a:a + 32], T.yx[:, 128 * h + a:128 * h + a + 32], Alu.subtract, 32,
-                   ["OU" + H, "Ab", "y0" + H], PR + ["P"], SCA)
-        xn = T.k1[:, 408:424]; so = 32 * t
+                tt(Wt[:, :].indirect(T.OU[:, 16 * h + m:16 * h + m + 2]), T.Ab[:, a:a + 32], T.yx[:, 128 * h + a:128 * h + a + 32], Alu.subtract, 32,
+                   ["OU" + H, "Ab", "y0" + H], [WN] + W0, SCA)
+        xn = T.m1[:, 416:432]; so = 32 * t
         if not lastv:
-            ts(T.XS[:, so + 16:so + 32], xn, 0.5, 1023.75, Alu.mult, Alu.add, 16, ["xn0", "xn1"], ["xs" + tg, "@k1"])
-            add(T.XS[:, so:so + 16], xn, 2049.0 + t, 16, ["xn0", "xn1"], ["xt" + tg, "@k1"])
+            ts(T.XS[:, so + 16:so + 32], xn, 0.5, 1023.75, Alu.mult, Alu.add, 16, ["xn0", "xn1"], ["xs" + tg, "@m1"])
+            add(T.XS[:, so:so + 16], xn, 2049.0 + t, 16, ["xn0", "xn1"], ["xt" + tg, "@m1"])
             send(T.XU[:, xo + 48:xo + 80], T.XS[:, so:so + 32], "ax%d" % (t + 1), ["xs" + tg, "xt" + tg], "XU" + nt)
         else:
-            ac(T.XO[:, :], xn, 16, ["xn0", "xn1"], ["XO", "@k1"], bias=2048.0)
-        tt(T.bb[:, :], Pw.indirect(gyu), T.rm[:, :], Alu.max, L, ["P", "gyu" + tg, "rm"], ["bb"], GA)
+            ac(T.XO[:, :], xn, 16, ["xn0", "xn1"], ["XO", "@m1"], bias=2048.0)
+        tt(T.bb[:, :], Wt[:, 0:V].indirect(gyu), (T.dab2 if lastv else T.rm)[:, :], Alu.max, L, [WN, "gyu" + tg, "rm", "rm2"], ["bb"], GA)
         for h, m in ((1, 4), (1, 0), (0, 4), (0, 0)):
             a = 128 * h + 16 * m; o = 128 * h + 128 + a
-            tt(Pall.indirect(T.OU[:, 16 * h + 8 + m:16 * h + 12 + m]), T.bb[:, a:a + 64], T.yx[:, o:o + 64], Alu.subtract, 64,
-               ["OU%d" % h, "bb", "y1%d" % h], ["P"], SCA)
+            tt(Wt[:, :].indirect(T.OU[:, 16 * h + 8 + m:16 * h + 12 + m]), T.bb[:, a:a + 64], T.yx[:, o:o + 64], Alu.subtract, 64,
+               ["OU%d" % h, "bb", "y1%d" % h], [WN], SCA)
     t = RO - 1
     dma("S", T.yrec[:, :], T.XO[:, :], "st4", 2000.0, ["XO"], [])
     dma("S", T.yz[:, :], T.ZS[:, 2 * L * t:2 * L * t + L], "st5", 2000.0, ["zsa0#%d" % t, "zsa1#%d" % t], [])
-    for q in range(4):
-        a, o = T.P[:, 512 * q:512 * q + 512], T.PO[:, 512 * q:512 * q + 512]
-        if q % 2: ac(o, a, 512, ["P"], ["out%d" % q], bias=2048.0)
-        else: add(o, a, 2048.0, 512, ["P"], ["out%d" % q])
-        dma("SA"[q % 2], T.ypar[:, 512 * q:512 * q + 512], o, "st%d" % q, 3000.0, ["out%d" % q], [])
+    for q in (0, 1): dma("SA"[q], T.ypar[:, 1024 * q:1024 * q + 1024], T.PO[:, 1024 * q:1024 * q + 1024], "st%d" % q, 3500.0, ["PO"], [])
     return ops, nsent[0]
 
 
@@ -591,5 +598,5 @@ def rank_program(g, core, T, topo):
                 else: queue[e].wait_ge(T.sem["s" + ops[w]["eng"]], count[w])
             ins = ops[i]["fn"]()
             if i in marked: ins.then_inc(T.sem["s" + e], 1)
-    for s in range(6): g.sync.wait_ge(T.sem["st%d" % s], 16)
+    for s in (0, 1, 4, 5): g.sync.wait_ge(T.sem["st%d" % s], 16)
     g.wait_ge(T.sem.sent, nsent)

import numpy as np
from concourse.mybir import AluOpType as Alu, ActivationFunctionType as Act

V, R, L, RO = 2048, 4096, 256, 5
CUT = tuple((w, h, c) for w in ("wa", "wb", "wc") for h in (0, 1) for c in (0, 1))
APART = (0,)
SPLIT = "A"
VG = (("wa", 1, 1, 0), ("wa", 1, 1, 1), ("wb", 1, 1, 1), ("wb", 0, 1, 1), ("wc", 0, 1, 1))
ONV = ("pT1", "zT0", "Bh1")
KW = 131072.0
BIG = 67108864.0
MG = 1.5 * 2.0 ** 36

BF, HF, F32, I32, U16 = "bfloat16", "float16", "float32", "int32", "uint16"
SCRATCH = {name: ("sbuf", [128] + list(shape), kind) for kind, bufs in (
    (BF, {"win": [R + RO * 2 * L], "rmt": [R + 16], "SJ": [2048], "MK": [256], "ZS": [RO * 2 * L], "ones": [128], "idb": [128], "negi": [256],
          "bo": [128], "fs": [144], "ih": [128], "iq": [128], "ie": [128], "ic": [128], "ig": [128], "I17": [408], "E17": [408], "B17": [408],
          "KB": [512], "KC": [408], "FB": [144], "FX": [144], "FQ": [144], "EB": [384], "W": [160], "SD": [256], "rsm": [128], "rm": [L],
          "dab": [L], "dab2": [L], "eq": [2 * L], "pp": [2 * L], "zT": [2 * L], "pT": [2 * L], "EC": [512], "eqd": [1024], "dxs": [64], "SH": [512],
          "wa": [2048, 2], "wb": [2048, 2], "wc": [2048, 2], "mzA": [4096], "mpA": [4096], "mzB": [4096], "mpB": [4096], "mzC": [4096],
          "mpC": [4096], "Xb": [L], "nw": [L], "cs": [L], "qh": [L], "zt": [L]}),
    (HF, {"XB": [RO * L], "XN": [RO * L], "VV": [RO * 64], "LQ": [80], "Ah": [L], "Bh": [L], "Ch": [L], "yv": [L], "KT": [128], "KX": [96],
          "GX": [96], "vts": [512]}),
    (F32, {"P": [V + L], "PO": [V + L], "thf": [16], "XO": [16], "xl": [16], "wk": [L], "rsb": [128], "rsc": [408], "pmf": [8], "jrow": [16], "dum": [16],
           "LF": [80], "Ab": [L], "bb": [L], "yx": [2 * L], "GL": [32], "BR": [16], "VR": [192], "OF": [32], "sb": [L], "sc": [816], "tb": [64],
           "cj": [8], "cf": [8]}),
    (I32, {"pari": [V], "reci": [16], "thi": [8], "pmi": [8]}),
    (U16, {"XU": [RO * 48], "XS": [RO * 32], "cl": [16], "ju": [16], "Au": [L], "Bu": [L], "Cu": [L], "YU": [16], "GC": [16], "QU": [16], "OU": [32]}),
) for name, shape in bufs.items()}
SCRATCH.update({name: ("psum", [128, 128, 8], BF) for name in ("rz0", "rz1", "rp0", "rp1")})
SCRATCH.update({name: ("psum", [128, 512], F32) for name in ("k0", "k1", "m0", "m1")})
SEMAPHORES = (["sV", "sA", "sP", "sG", "sent"] + ["ld%d" % i for i in range(8)] + ["st%d" % i for i in range(6)]
              + ["ax%d" % t for t in range(1, RO)] + ["a%s%d_%d" % (s, t, h) for s in "zt" for t in range(1, RO) for h in (0, 1)])

CY, PCY, GA, SCA, CALL, WAKE = 0.86, 0.43, 1.56, 3.8, 60.0, 130.0
SEED, STEADY, MOVES, HOT, COLD, PERIOD = 1, 5000, 40000, 40.0, 10.0, 30550.0
EARLY = {"V": 3000.0, "A": 9000.0, "P": 0.0}
PLAN = """rz1:-173 zT1:-120 Ah:-108 rm:-62 sh0:-50 rz1':-37 Au1:-19 SD:-16 yv:0 sh0':14 wa1_0b:16 Au0:46 yl:58 wa1_1:65 wa0_1b:102 K0:109 ones':128 K1:148 gyu:151 yu:163 rz0:167 Bh:175 pp0:188 wa1_1b:221 sh1:233 pp1:234 ab:246 sh1':272 wa1_0:280 ones:285 Bu0:307 wa1_1':319 zT0:339 rp0:345 wb1_1b:358 wb1_0:365 wa1_0':377 pT0:443 wb1_1:451 mzA1_1:475 rp1:487 mzA1_0:532 wb1_0b:537 rp0':538 rz0':589 mpA1_1:589 dab:623 wb1_1':641 mzB1_1:647 wa0_1:655 wb1_0':666 mzA1_1':692 mpB1_0:704 mzA1_0':717 wa0_0:741 mpA1_1':743 mzB1_0:761 mzB1_1':769 mpB1_0':794 mpB1_1:818 wa0_0b:826 mzB1_0':830 mpA1_0:875 mpB1_1':887 wb0_0b:912 mpA0_0:933 mpA1_0':945 K1':970 ab':983 mzA0_0:990 Xb1:1001 wb0_1:1020 mpA0_0':1021 nw1:1047 mzA0_0':1059 wk1:1078 GL:1097 Xb1':1106 sb1:1109 GX:1125 cs1:1137 tb1:1149 vn1:1161 Ab:1173 vr1:1173 wb0_1b:1186 vt1:1198 K1'':1204 vtb1:1222 wb0_0:1241 li1:1253 mzA0_1:1272 wa0_1':1304 gc1:1329 wb0_0':1339 mpB0_0:1341 Ch1:1353 wa0_0':1364 BR1:1379 sh1'':1404 KX1:1404 wb0_1':1416 Cu1:1434 mpA0_1:1453 kt:1465 mpB0_0':1472 KT:1490 mzA0_1':1497 wc1_0b:1508 mzB0_1:1510 df1:1523 mzB0_0:1568 mpA0_1':1587 wc1_1:1594 df1':1612 mpB0_1:1625 mzB0_1':1638 mzB0_0':1664 wc1_0:1680 eq1:1452 mpB0_1':1694 K0':1720 K1''':1732 eqd1:1734 eq1':1746 eq1'':1750 Xb0:1766 wc1_0':1778 wc1_1b:1785 nw0:1797 dx1:1804 wk0:1828 sb0:1858 Xb0':1871 tb0:1889 dxs1:1889 cs0:1902 vr0:1914 dd1:1914 vn0:1926 mzC1_1:1926 vt0:1950 K0'':1957 vtb0:1975 mzC1_0:1984 li0:2006 OF1:2041 mzC1_1':2057 gc0:2075 OU1:2087 BR0:2099 Ch0:2112 KX0:2124 sh0'':2150 kt':2162 Cu0:2180 mzC1_0':2182 KT':2187 eq0:2199 wc1_1':2208 wc0_1b:2211 mpC1_1:2225 df0:2234 mpC1_0:2282 wc0_0:2297 df0':2298 X0:2323 mpC1_1':2337 eqd0:2341 mpC1_0':2362 wc0_1:2383 K1'''':2388 eq0':2408 eq0'':2415 dx0:2418 sc1:2426 wc0_0b:2469 wc0_1':2481 tc1:2485 wc0_1'':2506 vy1:2510 vt1':2534 vtc1:2558 wc0_0':2567 mzC0_1:2567 dxs0:2577 vt1'':2592 mzC0_0:2624 dd0:2631 y01:2636 xs1:2670 xs1':2700 mzC0_1':2654 xn1:2679 mpC0_1:2681 mzC0_0':2731 mpC0_0:2738 K0''':2756 ql1:2770 sc0:2795 wc0_0'':2821 OF0:2829 tc0:2841 mpC0_1':2847 qu1:2853 vy0:2866 qh1:2878 P:2878 vt0':2890 mpC0_0':2897 P':2908 vtc0:2915 zp1:2922 OU0:2927 X0':2935 P'':2939 vt0'':2945 zt1:2953 scx0:2960 y00:2976 P''':2979 xn0:2984 zsb1:2995 tcx0:2998 P'''':3010 zsa1:3014 vr0':3028 cn:3035 ql0:3041 P''''':3041 zsa1':3045 cf:3059 xs:3059 xt:3071 cf1:3084 xs0:3040 xs0':3200 vtx0:3093 cf3:3096 P'''''':3096 xs':3108 qu0:3114 vtb0':3117 P''''''':3127 cf2:3136 vtx0':3148 qh0:3148 bb:3157 zp0:3186 P'''''''':3215 zt0:3217 y10:3190 zsa0:3255 P''''''''':3257 zsb0:3273 scol:3292 P'''''''''':3299 zsa0':3304 P''''''''''':3342"""
PLAN = """rm:-58 Ah:-12 rz1:-8 yv:0 zT1:34 sh0:46 yl:59 SD:66 Au1:77 wa1_0:108 wa1_1b:108 sh0':110 K0:123 rz0:162 rz1':175 gyu:193 wa1_0b:193 yu:206 Bh:218 K1:226 ones:246 Au0:264 sh1:276 pp0:279 wa1_1:283 sh1':289 pp1:325 Bu0:369 wa0_0b:371 rp0:383 GL:400 ones':409 mzA1_0:413 ab:428 wa1_0':454 wb1_0:457 pT0:470 wa1_1':479 wb1_1b:502 mzA1_0':505 rp1:530 wb1_0b:543 rp0':582 mzA1_1:587 wb1_1:629 mpA1_0:645 mpA1_1:702 wa0_1:715 wb1_1':727 mzA1_1':752 zT0:759 wb1_0':778 mzB1_1:778 wa0_0:801 mpA1_0':803 mpA1_1':829 mpB1_0:835 rz0':855 wa0_1b:886 mpB1_1:892 mzB1_1':906 mpB1_0':931 mzB1_0:949 mpB1_1':961 dab:972 wb0_0b:1004 mzA0_0:1007 mzB1_0':1019 K1':1044 mpA0_0:1064 mzA0_0':1076 Xb1:1090 ab':1101 wb0_1:1109 nw1:1121 wk1:1152 sb1:1183 Xb1':1194 tb1:1213 cs1:1226 vr1:1238 vn1:1250 mpA0_1:1251 vt1:1275 vtb1:1299 wb0_1b:1308 wb0_0:1318 li1:1330 wa0_0':1381 gc1:1399 GX:1404 K1'':1407 mzA0_1:1411 Ch1:1425 K1''':1447 BR1:1451 wa0_1':1463 mpB0_1:1469 sh1'':1489 mzA0_1':1502 Cu1:1526 mpB0_1':1538 KX1:1545 wc1_0:1557 mzB0_1:1558 de1:1563 mpA0_0':1595 eq1:1615 mpA0_1':1621 wc1_1:1643 wb0_0':1647 mzB0_0:1647 mzB0_1':1672 kt:1698 mpB0_0:1704 eq1':1704 wb0_1':1718 KT:1728 mzB0_0':1743 wc1_0b:1747 mpB0_0':1773 K0':1799 df1:1812 Xb0:1833 nw0:1864 wk0:1895 Xb0':1895 wc1_0':1901 Ab:1914 eqd1:1919 wc1_1b:1945 sb0:1977 dx1:1989 cs0:1995 tb0:2008 vn0:2031 vr0:2032 mzC1_0:2045 vt0:2057 K0'':2063 vtb0:2081 dxs1:2100 mzC1_1:2102 li0:2112 eq1'':2163 dd1:2170 gc0:2181 mzC1_0':2192 BR0:2205 OF1:2210 Ch0:2218 wc1_1':2218 KX0:2230 sh0'':2256 kt':2269 mzC1_1':2275 Cu0:2287 KT':2293 mpC1_0:2305 wc0_0b:2317 df0:2324 mpC1_1:2363 wc0_0:2403 mpC1_0':2413 eqd0:2431 de0:2439 mpC1_1':2471 eq0:2489 wc0_1b:2489 K1'''':2497 wc0_0':2517 sc1:2535 dx0:2543 wc0_1:2575 tc1:2594 X0:2594 eq0'':2611 wc0_0'':2617 vy1:2618 OU1:2631 vt1':2643 eq0':2649 vtc1:2667 wc0_1':2673 mzC0_0:2673 dxs0:2686 vt1'':2698 dd0:2730 mzC0_1:2730 y01:2748 mzC0_0':2753 mpC0_0:2787 xn1:2792 mzC0_1':2843 OF0:2844 mpC0_1:2857 K0''':2869 ql1:2882 sc0:2914 mpC0_0':2934 qu1:2952 mpC0_1':2959 tc0:2964 xs1:2976 wc0_1'':2985 vy0:2988 qh1:2995 P:3001 X0':3010 vt0':3017 P':3031 zp1:3033 vtc0:3042 cn:3046 scx0:3049 zt1:3064 P'':3069 vt0'':3072 tcx0:3087 zsa1:3094 xn0:3094 P''':3099 y00:3113 OU0:3117 vr0':3130 zsb1:3132 P'''':3144 ql0:3146 cf:3151 xs:3164 cf1:3175 xt:3176 P''''':3188 vtx0:3197 cf2:3200 xs':3200 qu0:3215 vtb0':3221 P'''''':3227 xs0:3240 zsa1':3250 vtx0':3252 P''''''':3257 qh0:3259 XU:3262 y10:3285 bb:3288 zp0:3297 xs0':3300 cf3:3304 z1:3312 scol:3328 zt0:3340 P'''''''':3345 xs1':3350 xb0:3362 zsa0:3371 P''''''''':3388 zsb0:3390 xb1:3412 zsa0':3421 P'''''''''':3430 P''''''''''':3472 z0:3483"""
PLAN = """rm:-53 Ah1:-13 rz1:-3 yv:0 SD:10 sh0:23 Ah0:38 Au1:53 yl:53 zT1:61 wa1_1b:83 wa1_0b:89 sh0':97 rz1':108 gyu:158 wa1_0:164 Au0:169 rz0:184 yu:186 Bh1:198 wa1_1:238 pp11:239 sh1:251 sh1':262 K1:273 pp10:279 ones:290 wa1_0':306 Bu0:313 wa0_1:319 rp0:332 mzA1_1:341 pT1:391 wb1_0b:394 zT0:419 rp1:432 mzA1_0:436 wb1_1:469 mzA1_1':476 wb1_1b:486 rz0':498 mzA1_0':542 wb1_0:544 mpA1_1:561 mpA1_0:611 wa0_1b:618 mpA1_1':624 rp0':646 mpB1_1:661 ab:690 wa0_0:693 mpB1_0:711 mpA1_0':712 mpB1_1':734 wa1_1':756 mzB1_0:761 wa0_0b:768 wb1_1':778 wb1_0':800 mzB1_1:811 mpB1_0':822 dab:842 mzB1_0':844 mpA0_0:861 mzB1_1':874 K1':896 ab':907 mzA0_0:911 Xb1:926 K0:940 wb0_1:943 nw1:961 mzA0_0':974 mzA0_1:978 Xb1':1018 wk1:1028 wb0_0b:1035 mzA0_1':1041 sb1:1058 wa0_1':1063 cs1:1075 tb1:1088 GL:1100 vn1:1109 vr1:1113 Ab:1121 wb0_1b:1124 vt1:1137 K1'':1143 vtb1:1162 wb0_0:1179 li1:1192 mpA0_1:1199 wb0_1':1236 gc1:1255 mpA0_0':1258 mzB0_0:1266 Ch1:1279 mpA0_1':1280 BR1:1302 wa0_0':1302 GX:1314 mpB0_0:1316 sh1'':1327 wb0_0':1338 Cu1:1366 mpB0_0':1379 mzB0_1:1383 wc1_0b:1396 mzB0_0':1401 de1:1423 mpB0_1:1433 ones':1451 mzB0_1':1467 wc1_0:1471 eq1:1483 mpB0_1':1496 KX1:1511 K0':1518 kt:1537 Xb0:1548 KT:1565 nw0:1578 wc1_1:1582 df1:1595 wk0:1608 sb0:1638 Xb0':1657 tb0:1668 K1''':1672 wc1_1b:1674 cs0:1687 wc1_0':1687 eqd1:1699 eq1':1709 vr0:1749 vn0:1749 mzC1_1:1762 vt0:1773 dx1:1779 vtb0:1798 mzC1_0:1812 cn:1823 li0:1828 dxs1:1842 cf:1853 mpC1_1:1862 dd1:1872 cf1:1878 eq1'':1892 mzC1_0':1897 cf2:1902 gc0:1912 mzC1_1':1920 OF1:1923 BR0:1936 mpC1_1':1942 Ch0:1948 OU1:1948 KX0:1961 cf3:1971 mpC1_0:1973 sh0'':1984 kt':1995 wc1_1':2001 KT':2020 Cu0:2023 mpC1_0':2036 wc0_0:2053 wc0_1b:2053 K1'''':2058 df0:2076 sc1:2128 wc0_1:2128 de0:2153 eqd0:2172 K0'':2181 wc0_0b:2203 wc0_1':2216 eq0:2222 dx0:2238 tc1:2250 vy1:2275 eq0':2282 mzC0_0:2290 wc0_0':2294 dxs0:2301 scol:2312 vt1':2316 X0:2321 dd0:2335 vtc1:2340 mzC0_1:2340 mzC0_0':2355 vt1'':2377 mpC0_0:2391 mzC0_1':2404 y01:2423 K0''':2426 wc0_0'':2438 OF0:2441 sc0:2457 ql1:2464 OU0:2486 tc0:2499 xn1:2508 P:2511 vy0:2527 P':2540 vt0':2552 qu1:2557 wc0_1'':2558 P'':2570 vtc0:2577 mpC0_0':2580 mpC0_1:2586 qh1:2594 eq0'':2602 vt0'':2608 xs1:2617 xn0:2624 P''':2636 y00:2643 zp1:2668 P'''':2673 mpC0_1':2679 xs:2690 zt1:2698 X0':2701 xt:2701 ql0:2707 P''''':2713 xs':2726 zsb1:2728 scx0:2729 zsa1:2745 P'''''':2747 tcx0:2763 qu0:2775 zsa1':2776 vr0':2788 XU:2789 qh0:2799 P''''''':2799 vtx0:2812 xs0:2823 bb:2829 z1:2839 vtb0':2840 xs0':2853 zp0:2853 vtx0':2870 P'''''''':2882 zt0:2883 y10:2900 xs1':2903 xb0:2916 zsa0:2917 P''''''''':2922 zsb0:2934 P'''''''''':2962 zsa0':2964 xb1:2966 P''''''''''':3002 z0:3027"""
ORDER = []


def build(g, T, topo, core):
    ops = []
    last_w, readers, times, visit = {}, {}, {}, [-1]
    vec, act, pe = g.vector, g.scalar, g.tensor

    def op(eng, busy, fn, rd=(), wr=(), lat=0.0, sem=None, after=()):
        i = len(ops); deps = {}
        for r in rd:
            if r in last_w: deps[last_w[r]] = deps.get(last_w[r], False) or not r.startswith("@")
        for r in wr:
            for j in readers.get(r, []): deps[j] = deps.get(j, False)
            if r in last_w: deps[last_w[r]] = deps.get(last_w[r], False) or not r.startswith("@")
        for r in rd: readers.setdefault(r, []).append(i)
        for r in wr: last_w[r] = i; readers[r] = []
        name = (list(wr) + list(rd) + ["-"])[0]; nm = "P" if name == "PO" else name.split("#")[0]
        times[nm] = times.get(nm, 0) + 1
        ops.append({"kin": (nm, times[nm], visit[0] < 0), "vis": visit[0], "eng": eng, "busy": busy, "lat": lat, "fn": fn, "deps": deps,
                    "sem": sem, "name": name, "after": list(after)})
        return i

    def vcost(n, per=1.0): return CALL + max(64.0, n * per) * CY
    def V_(n, per, fn, rd, wr): return op("V", vcost(n, per), fn, rd, wr)
    def A_(n, per, fn, rd, wr): return op("A", vcost(n, per), fn, rd, wr)
    def G_(n, fn, rd, wr): return op("G", 170.0 + 2 * n * CY, fn, rd, wr)

    def mm(items, rd, wr):
        def fn():
            for o, l, r, s, e, c in items: ins = pe.matmul(o, l, r, s, e)
            return ins
        return op("P", sum(max(64, it[5]) for it in items) * PCY, fn, rd, wr, lat=60.0)

    def turn(items, rd, wr):
        def fn():
            for o, a in items: ins = pe.transpose(o, a, T.idb[:, :])
            return ins
        return op("P", 128 * len(items) * PCY, fn, rd + ["idb"], wr, lat=60.0)

    def ts(out, in0, s1, s2, o0, o1, n, rd, wr, per=1.0):
        if s2 is None: return V_(n, per, lambda: vec.tensor_scalar(out, in0, s1, None, o0), rd, wr)
        return V_(n, per, lambda: vec.tensor_scalar(out, in0, s1, s2, o0, o1), rd, wr)
    def add(out, in0, c, n, rd, wr, per=1.0): return ts(out, in0, c, None, Alu.add, None, n, rd, wr, per)
    def tt(out, a, b, o, n, rd, wr, per=1.0): return V_(n, per, lambda: vec.tensor_tensor(out, a, b, o), rd, wr)
    def cp(out, a, n, rd, wr, per=1.0): return V_(n, per, lambda: vec.tensor_copy(out, a), rd, wr)
    def ms(out, c, n, wr): return V_(n, 0.5, lambda: vec.memset(out, c), [], wr)
    def scan(out, a, b, o0, o1, n, rd, wr, per=1.0): return V_(n, per, lambda: vec.tensor_tensor_scan(out, a, b, 0.0, o0, o1), rd, wr)
    def ac(out, a, n, rd, wr, f=Act.Identity, bias=0.0, scale=1.0, per=1.0):
        return A_(n, per, lambda: act.activation(out, a, f, bias=bias, scale=scale), rd, wr)
    def move(tag, out, a, n, rd, wr, per=1.0, fast=0.5):
        if tag in ONV or tag in VG: return cp(out, a, n, rd, wr, per if per > 1 else fast)
        return ac(out, a, n, rd, wr, f=Act.Copy, per=per)
    def fl(out, c, n, wr, p=(0, 128)): return ac(out, T.ones[p[0]:p[1], 0:n], n, ["ones"], wr, bias=float(c), scale=0.0)
    def sel(out, a, pat, cmp, fill, base, cm, n, rd, wr):
        return G_(n, lambda: g.affine_select(out, a, pat, cmp, fill, base, cm), rd, wr)
    def io(out, pat, base, cm, n, wr, flt=True):
        if flt: return G_(n, lambda: g.iota(out, pat, base, cm, allow_small_or_imprecise_dtypes=True), [], wr)
        return G_(n, lambda: g.iota(out, pat, base, cm), [], wr)
    def dma(eng, out, a, sem, lat, rd, wr):
        q = g.sync if eng == "S" else act
        return op(eng, 60.0, lambda: q.dma_start(out, a).then_inc(T.sem[sem], 16), rd, wr, lat=lat, sem=(sem, 16))
    def hs(buf, h): return buf[:, 128 * h:128 * h + 128]

    rank = T.rank_of(core)
    nxt = T.cores[(rank + 1) % len(T.cores)]
    rid, pid, _se = topo.addr(nxt)
    emask = topo.mask(core, nxt)
    neng = len(topo.engines(core, nxt))
    prv = T.cores[(rank - 1) % len(T.cores)]
    nin = len(topo.engines(prv, core))
    nsent = [0]

    def send(dst, src, sem, rd, landed):
        def fn():
            g.remote_dma(dst, src, T.sem[sem], T.sem.sent, pid, rid, emask)
        nsent[0] += neng
        s = op("G", 500.0, fn, rd, [])
        return op(None, 0.0, None, [], [landed], lat=2000.0, sem=(sem, nin), after=[s])

    dma("A", T.reci[:, :], T.rec[:, :], "ld5", 2500.0, [], ["reci"])
    for q in range(4):
        dma("S", T.pari[:, 512 * q:512 * q + 512], T.par[:, 512 * q:512 * q + 512], "ld%d" % q, 3000.0 + 800.0 * q, [], ["pari%d" % q])
    dma("S", T.win[:, 0:R], T.prof[:, :], "ld4", 8000.0, [], ["prof"])
    dma("A", T.zt[:, :], T.zf[:, :], "ld6", 3000.0, [], ["zt0", "zt1"])
    dma("A", T.thi[:, 0:RO], T.th[:, :], "ld7", 2500.0, [], ["thi"])
    ms(T.ones[:, :], 1.0, 128, ["ones"])
    io(T.pmi[:, 0:1], [[0, 1]], 0, 1, 1, ["pmi"], False)
    io(T.jrow[:, :], [[1, 16]], 0, 0, 16, ["jrow"])
    sel(T.idb[:, :], T.ones[:, :], [[-1, 128]], Alu.is_equal, 0.0, 0, 1, 128, ["ones"], ["idb"])
    sel(T.bo[:, :], T.ones[:, :], [[-16, 8], [0, 16]], Alu.is_ge, 0.0, 0, 1, 128, ["ones"], ["bo"])
    sel(T.bo[:, :], T.bo[:, :], [[16, 8], [0, 16]], Alu.is_ge, 0.0, 15, -1, 128, ["bo"], ["bo"])
    ts(T.pmi[:, 4:5], T.pmi[:, 0:1], 15, None, Alu.bitwise_and, None, 1, ["pmi"], ["pmi2"])
    cp(T.pmf[:, 0:1], T.pmi[:, 4:5], 1, ["pmi2"], ["pmf"])
    pj = T.pmf[:, 0:1]
    ts(T.rmt[:, 0:16], T.jrow[:, :], pj, 4096.0, Alu.is_equal, Alu.mult, 16, ["jrow", "pmf"], ["rmt"])
    add(T.rmt[:, 0:16], T.rmt[:, 0:16], -2048.0, 16, ["rmt"], ["rmt"])
    n = 16
    while n < 1024:
        cp(T.rmt[:, n:2 * n], T.rmt[:, 0:n], n, ["rmt"], ["rmt"], 0.5); n *= 2
    cp(T.rmt[:, 1024:2048], T.rmt[:, 0:1024], 1024, ["rmt"], ["rmt1"], 0.5)
    cp(T.rmt[:, 2048:3072], T.rmt[:, 0:1024], 1024, ["rmt"], ["rmt2"], 0.5)
    ac(T.rmt[:, 3072:R], T.rmt[:, 0:1024], 1024, ["rmt"], ["rmt3"], f=Act.Copy)
    ac(T.rmt[:, R:R + 16], T.rmt[:, 0:16], 16, ["rmt"], ["rmt4"], f=Act.Copy)
    bo8 = T.bo[:, 0:128:16]
    for q in (0, 1):
        for c in (0, 1):
            S = hs(T.SH, 2 * q + c)
            sel(S, T.ones[:, :], [[-16, 8], [0, 2], [-1, 8]], Alu.is_equal, 0.0, -8 * q, 1, 128, ["ones"], ["SH%d%d" % (q, c)])
            sel(S, S, [[0, 8], [1, 2], [0, 8]], Alu.is_equal, 0.0, -c, 0, 128, ["SH%d%d" % (q, c)], ["SH%d%d" % (q, c)])
    SH = ["SH00", "SH01", "SH10", "SH11"]
    ms(T.fs[:, :], 0.0, 144, ["fs"])
    ac(T.fs[:, 15:143:16], bo8, 8, ["bo", "fs"], ["fs"], f=Act.Copy)
    ac(T.win[:, R:R + 2 * L:2], T.zt[:, :], L, ["zt0", "zt1"], ["z0#0", "z1#0"], f=Act.Copy)
    ac(T.win[:, R + 1:R + 2 * L:2], T.zt[:, :], L, ["zt0", "zt1"], ["zd#0"], f=Act.Copy)
    for q in range(4):
        add(T.P[:, 512 * q:512 * q + 512], T.pari[:, 512 * q:512 * q + 512], -2048.0, 512, ["pari%d" % q], ["P%d" % q])
    cp(T.XU[:, 0:16], T.reci[:, :], 16, ["reci"], ["XT#0"])
    ts(T.XU[:, 16:32], T.reci[:, :], 0.5, -0.25, Alu.mult, Alu.add, 16, ["reci"], ["XU#0"])
    cp(T.thf[:, 8:8 + RO], T.thi[:, 0:RO], RO, ["thi"], ["thf0"])
    for c, s in ((0, -1.0), (128, -BIG)): ac(T.negi[:, c:c + 128], T.idb[:, :], 128, ["idb"], ["negi%d" % c], scale=s)
    WOF = {"mzA": 0, "mpA": 24, "wa": 48, "mzB": 64, "mpB": 88, "wb": 112}
    ms(T.W[:, :], 0.0, 160, ["W"])
    WS = ((0, 1, 2.0), (16, 1, KW), (32, 1, -2 * BIG), (40, 1, -KW), (48, 1, -1.0), (56, 1, BIG), (128, 2, -KW), (144, 1, -KW), (152, 1, 2 * KW))
    for o, s, c in WS: ac(T.W[:, o:o + 8 * s:s], bo8, 8, ["bo", "W"], ["W%d" % o], scale=c)
    ac(T.W[:, 64:128], T.W[:, 0:64], 64, ["W%d" % o for o, s, c in WS[:6]], ["W64"], scale=-1.0)
    WR = ["W64"] + ["W%d" % o for o, s, c in WS]
    ms(T.KB[0:64, :], 0.0, 512, ["KB"])
    io(T.KB[0:1, 256:384], [[0, 8], [-8192, 16]], 122880, 0, 128, ["KB"])
    for o, c in ((0, -512.0), (128, BIG / 2), (256, -120.0 * KW), (384, 30720.0)): fl(T.KB[32:33, o:o + 128], c, 128, ["KB"], (32, 33))
    for nm, c in (("iq", -0.25), ("ie", 2.0 ** -13), ("ic", 125.0 * KW), ("ig", 126.0 * KW), ("ih", 0.5)):
        ac(T[nm][:, :], T.idb[:, :], 128, ["idb"], [nm], scale=c)
    fl(T.rsb[:, :], 0.0, 128, ["rsb"]); fl(T.rsb[:, 0:128:16], -4 * BIG, 8, ["rsb"])
    sel(T.rsm[:, :], T.ones[:, :], [[0, 8], [1, 16]], Alu.is_gt, 0.0, 0, 0, 128, ["ones"], ["rsm"])

    def shifts(nm, rows, c, flag):
        F = T[nm]
        io(F[0:32, :], [[0, 144]], 0, 0, 144, [nm])
        ac(F[0:32, 15:143:16], rows, 8, ["idb", nm], [nm], scale=c)
        if flag: sel(F[0:32, 15:143:16], F[0:32, 15:143:16], [[-1, 8]], Alu.not_equal, 2048.0, -flag, 1, 8, [nm], [nm])
    shifts("FB", T.idb[0:32, 0:8], 0.5, 8)
    for o, w in ((0, 0), (48, 16)):
        for a, pat, base in ((0, [[w, 2], [1, 8]], 0), (16, [[w, 2], [2, 4]], 1), (24, [[0, 2], [4, 2], [1, 2]], w + 2),
                             (32, [[w, 2], [2, 4]], 0), (40, [[4, 2], [1, 2]], w), (44, [[4, 2], [-1, 2]], w + 1)):
            n = int(np.prod([p[1] for p in pat]))
            io(T.VR[:, o + a:o + a + n], pat, base, 0, n, ["VR%d" % (o + a)])
    tt(T.VR[:, 0:96], T.VR[:, 0:96], T.rmt[:, 0:96], Alu.min, 96, ["rmt"], ["VR"] + ["VR%d" % (o + a) for o in (0, 48) for a in (0, 16, 24, 32, 40, 44)])
    scan(T.VR[:, 96:192], T.rsb[:, 0:96], T.VR[:, 0:96], Alu.add, Alu.max, 96, ["VR", "rsb"], ["VS"])
    for o, a, c in ((0, 144, 0.0), (3, 144, 8.0), (6, 96, 0.0)): add(T.cl[:, o:o + 3], T.VR[:, a + 15:a + 48:16], c, 3, ["VS"], ["cl%d" % o])
    ms(T.I17[:, :], 1.0, 408, ["I17"])
    for a, b, w in ((0, 272, 34), (272, 408, 17)):
        I = T.I17[:, a:b]
        sel(I, I, [[0, 8], [-1, w]], Alu.is_ge, 0.0, 15, 0, b - a, ["I17"], ["I17"])
        sel(I, I, [[-16, 8], [-1, w]], Alu.is_equal, 0.0, 0, 1, b - a, ["I17"], ["I17"])
    mm([(T.k0[:, 0:408], T.bo[:, :], T.I17[:, :], True, True, 408)], ["bo", "I17"], ["K0", "@k0"])
    ac(T.B17[:, :], T.k0[:, 0:408], 408, ["K0"], ["B17", "@k0"], scale=-KW)
    ac(T.E17[:, :], T.I17[:, :], 408, ["I17"], ["E17"], scale=-BIG)
    ms(T.KC[0:64, :], 0.0, 408, ["KC"])
    io(T.KC[0:1, :], [[0, 24], [-8192, 17]], 122880, 0, 408, ["KC"])
    ms(T.KC[32:33, :], 120 * KW, 408, ["KC"])
    sel(T.KC[0:33, 0:272], T.KC[0:33, 0:272], [[0, 8], [-1, 34]], Alu.is_ge, -127.0 * KW, 15 + 32 * 64, -64, 272, ["KC"], ["KC"])
    fl(T.KC[0:64, 16:408:17], 0.0, 24, ["KC"], (0, 64))
    fl(T.KC[32:33, 288:408:17], -125.0 * KW, 8, ["KC"], (32, 33))
    fl(T.KC[32:33, 16:272:34], 30720.0, 8, ["KC"], (32, 33))
    io(T.LF[:, :], [[256, 10], [0, 8]], -2048, 2, 80, ["LF"])
    ac(T.LQ[:, :], T.LF[:, :], 80, ["LF"], ["LQ"], f=Act.Copy)
    add(T.xl[:, :], T.reci[:, :], -2048.0, 16, ["reci"], ["xl"])
    cp(T.ju[:, :], T.jrow[:, :], 16, ["jrow"], ["ju"])
    tt(T.XN[:, 0:L], T.xl[:, :].indirect(T.ju[:, :]), T.rmt[:, 0:L], Alu.min, L, ["xl", "ju", "rmt"], ["xv"], GA)
    mm([(T.k1[:, 0:L], T.bo[:, :], T.XN[:, 0:L], True, True, L)], ["bo", "xv"], ["K1", "@k1"])
    ac(T.XB[:, 0:L], T.k1[:, 0:L], L, ["K1"], ["xb0#0", "xb1#0", "@k1"], bias=30720.0)
    io(T.MK[:, :], [[0, 16], [1, 16]], 0, 0, 256, ["MK"])
    ts(T.MK[:, :], T.MK[:, :], pj, 131072.0, Alu.is_le, Alu.mult, 256, ["MK", "pmf"], ["MK"], 0.5)
    for j in range(16):
        sel(hs(T.SJ, j), T.ones[:, :], [[-16, 8], [0, 16]], Alu.is_equal, 0.0, -j, 1, 128, ["ones"], ["SJ%d" % j])
    ms(T.EC[:, :], -1.0, 512, ["EC"])
    sel(T.EC[:, :], T.EC[:, :], [[-32, 2], [-1, 16], [0, 16]], Alu.is_equal, 0.0, 0, 1, 512, ["EC"], ["EC"])
    ac(T.pmf[:, 2:3], pj, 1, ["pmf"], ["pmf2"], bias=float(V))
    ac(T.dum[:, :], T.jrow[:, :], 16, ["jrow", "pmf2"], ["dum"], bias=T.pmf[:, 2:3], scale=16.0)
    io(T.rsc[:, :], [[0, 408]], 0, 0, 408, ["rsc"]); fl(T.rsc[:, 0:272:34], -4 * BIG, 8, ["rsc"]); fl(T.rsc[:, 272:408:17], -4 * BIG, 8, ["rsc"])
    io(T.EB[0:32, :], [[0, 384]], -1, 0, 384, ["EB"])
    sel(T.EB[0:32, 0:128], T.EB[0:32, 0:128], [[-2, 8], [0, 16]], Alu.is_equal, 0.0, 0, 1, 128, ["EB"], ["EB"])
    sel(T.EB[0:32, 128:384], T.EB[0:32, 128:384], [[16, 2], [-1, 8], [0, 16]], Alu.is_equal, 0.0, -16, 1, 256, ["EB"], ["EB"])
    shifts("FX", T.idb[0:32, 0:16:2], 1.0, 0)
    shifts("FQ", T.idb[0:32, 1:16:2], 1.0, 24)
    add(T.thf[:, 0:RO], T.thi[:, 0:RO], 7.5, RO, ["thi"], ["thf"])

    Pw, Pall, prof = T.P[:, 0:V], T.P[:, 0:V + L], T.win[:, 0:R]
    KK, MM = [T.k0, T.k1], [T.m0, T.m1]
    HS = (1, 0)

    def gather(name, U, uname, h):
        for c in (0, 1):
            n = 2 if (name, h, c) in CUT else 1
            for u in range(n):
                a = 128 * h + 64 * c + 32 * u; o = 1024 * h + 512 * u; r = "%s%d_%d" % (name, h, c)
                move((name, h, c, u) if n > 1 else (name, h, c), T[name][:, o:o + 1024 // n, c], prof.indirect(U[:, a:a + 64 // n]), 1024 // n,
                     ["prof", uname], [r + "b"] if u else [r] + [r + "b"] * (n == 1), GA)

    def sums(name, h, outs, wmat, bank):
        for u in (0, 1):
            mm([(outs(k + 8 * u), T[name][:, 1024 * h + k:1024 * h + 1024:8, u], wmat, False, False, 64) for k in range(8)],
               ["%s%d_%d" % (name, h, u), "%s%d_%db" % (name, h, u), bank] + WR, [])

    def mins(name, mname, h, outs, wmat, bank):
        m = T[mname]; bn = "r%s%d" % (mname[1], h)
        for q in (0, 1):
            a = 2048 * h + 1024 * q; r = "%s%d_%d" % (mname, h, q)
            tt(m[:, a:a + 1024], T[name][:, 1024 * h + q:1024 * h + 1024:2, :], T[bn][:, :, :], Alu.min, 1024,
               ["%s%d_%s" % (name, h, u) for u in ("0", "0b", "1", "1b")] + [bn, "@" + bn], [r], 0.5)
            mm([(outs(2 * (e // 2) + q + 8 * (e % 2)), m[:, a + e:a + 1024:8], wmat, False, False, 64) for e in range(8)], [r, bank] + WR, [])

    def lists(nm, hh, b, o, rd, more=()):
        for i, h in enumerate(hh):
            a = o + 128 * i
            its = [(MM[b][:, a + 64 * q:a + 64 * q + 64], hs(T.SH, 2 * q + c), T[nm + "h"][:, 128 * h + c:128 * h + 128:2], 64) for q in (0, 1) for c in (0, 1)]
            its += list(more)
            mm([it[0:3] + (k == 0, k == len(its) - 1, it[3]) for k, it in enumerate(its)], SH + rd, ["sh%d" % b, "@m%d" % b])
        add(T[nm + "u"][:, 128 * hh[0]:128 * hh[-1] + 128], MM[b][:, o:o + 128 * len(hh)], 2048.0, 128 * len(hh),
            ["sh%d" % b], ["%su%d" % (nm, h) for h in hh] + ["@m%d" % b])

    def fill(s, h):
        bn = "r%s%d" % (s, h); o = 256 * h
        turn([(T[bn][:, 64 * c:64 * c + 64, k:k + 2], T[s + "T"][:, o + 128 * c:o + 128 * c + 128]) for c in (0, 1) for k in range(0, 8, 2)],
             ["%sT%d" % (s, h)], [bn, "@" + bn])

    def column(nm, genes, rd, b):
        for hh in (((1,), (0,)) if nm in SPLIT else ((0, 1),)):
            a, n = hh[0], len(hh); names = ["%sh%d" % (nm, h) for h in hh]
            move(names[-1], T[nm + "h"][:, 128 * a:128 * (a + n)], Pw.indirect(T.XU[:, genes + 8 * a:genes + 8 * (a + n)]), 128 * n, rd, names[::-1], GA)
            lists(nm, hh, b, 128 + 128 * a, names)

    for t in range(RO):
        lastv = t == RO - 1
        times.clear(); visit[0] = t
        xo = 48 * t; tg = "#%d" % t; nt = "#%d" % (t + 1)
        xtu, gxu, gyu, yu = T.XU[:, xo:xo + 16], T.XU[:, xo + 16:xo + 32], T.XU[:, xo + 32:xo + 48], T.YU[:, :]
        XR = ["XU#0", "XT#0"] if t == 0 else ["XU" + tg]
        PR = ["P%d" % q for q in range(4)] if t == 0 else ["P"]
        zo = R + 2 * L * t
        def zz(h): return T.win[:, zo + 256 * h:zo + 256 * h + 256:2]
        ZR = ["z%d%s" % (h, tg) for h in (0, 1)]
        def vv(h, a, b): return T.VV[:, 64 * t + 32 * h + a:64 * t + 32 * h + b]
        def xb(h): return T.XB[:, L * t + 128 * h:L * t + 128 * h + 128]
        ac(T.rm[:, :], T.rmt[:, :].indirect(xtu), L, ["rmt", "rmt1", "rmt2", "rmt3", "rmt4"] + XR, ["rm"], f=Act.Copy, per=GA)
        tt(T.yv[:, :], Pw.indirect(gxu), T.rm[:, :], Alu.min, L, PR + ["rm"] + XR, ["yv"], GA)
        column("A", xo + 16, PR + XR, 0)
        mm([(T.m1[:, 0:16], T.fs[:, 15 - j:143 - j], T.yv[:, j:L:16], j == 0, j == 15, 64) for j in range(16)], ["fs", "yv"], ["yl", "@m1"])
        ts(gyu, T.m1[:, 0:16], 0.5, 16383.75, Alu.mult, Alu.add, 16, ["yl"], ["gyu" + tg, "@m1"])
        add(yu, T.m1[:, 0:16], 32768.0, 16, ["yl"], ["yu", "@m1"])
        column("B", xo + 32, PR + ["gyu" + tg], 1)
        for hh in (((1,), (0,)) if "p" in SPLIT else ((0, 1),)):
            a, n = hh[0], len(hh); bn = "rp%d" % hh[0]
            for c in (0, 1):
                names = ["pp%d%d" % (h, c) for h in hh[::-1]]
                move(names[0], T.pp[:, 256 * a + c:256 * (a + n):2], prof.indirect(T.YU[:, 8 * a:8 * (a + n)]), 128 * n, ["prof", "yu"], names, GA)
            turn([(T[bn][:, 16 * c:16 * c + 16, :], hs(T.pp, 2 * a + c)) for c in range(2 * n)], ["pp%d%d" % (h, c) for h in hh for c in (0, 1)], [bn, "@" + bn])
            move("pT%d" % hh[-1], T.pT[:, 256 * a:256 * (a + n)], T[bn][:, 0:32 * n, :], 256 * n, [bn], ["pT%d" % h for h in hh[::-1]] + ["@" + bn])
            for h in hh[::-1]: fill("p", h)
        for h in HS:
            bn = "rz%d" % h; o = zo + 256 * h
            turn([(T[bn][:, 16 * c:16 * c + 16, :], T.win[:, o + 128 * c:o + 128 * c + 128]) for c in (0, 1)], [ZR[h], "zd#0"], [bn, "@" + bn])
            move("zT%d" % h, T.zT[:, 256 * h:256 * h + 256], T[bn][:, 0:32, :], 256, [bn], ["zT%d" % h, "@" + bn])
            fill("z", h)
        mm([(T.m0[:, 0:L], T.idb[:, :], T.Ah[:, :], True, False, 256), (T.m0[:, 0:L], T.negi[:, 0:128], T.Bh[:, :], False, True, 256)],
           ["idb", "negi0", "Ah0", "Ah1", "Bh0", "Bh1"], ["ab", "@m0"])
        ac(T.dab[:, :], T.m0[:, 0:L], L, ["ab"], ["dab", "@m0"], f=Act.Abs)
        mm([(T.m0[:, L:2 * L], T.idb[:, :], T.Ah[:, :], True, False, 256), (T.m0[:, L:2 * L], T.idb[:, :], T.rm[:, :], False, False, 256),
            (T.m0[:, L:2 * L], T.negi[:, 0:128], T.yv[:, :], False, True, 256)], ["idb", "negi0", "Ah0", "Ah1", "rm", "yv"], ["ab", "@m0"])
        ac(T.Ab[:, :], T.m0[:, L:2 * L], L, ["ab"], ["Ab", "@m0"], bias=2048.0 * lastv)
        if lastv:
            for q in range(4): ac(T.PO[:, 512 * q:512 * q + 512], T.P[:, 512 * q:512 * q + 512], 512, ["P"], ["PO%d" % q], bias=2048.0)
            ac(T.dab2[:, :], T.rm[:, :], L, ["rm"], ["rm2"], bias=2048.0)
        Wt, WN, W0 = (T.PO, "PO", ["PO%d" % q for q in range(4)]) if lastv else (T.P, "P", PR)
        cp(T.GL[:, :], T.XU[:, xo + 16:xo + 48], 32, XR + ["gyu" + tg], ["GL"])
        move("GX", T.GX[:, :], T.GL[:, :].indirect(T.cl[:, 0:6]), 96, ["GL", "cl0", "cl3"], ["GX"], GA)
        scol = T.thf[:, 8:9] if t == 0 else T.cf[:, 2:3]
        ac(T.SD[:, :], T.negi[:, :], 256, ["negi0", "negi128", "thf0", "scol"], ["SD"], scale=scol)
        for h in HS:
            K = KK[h]; kb = "@k%d" % h; M = MM[h]; mb = "@m%d" % h; H = str(h)
            mm([(K[:, 0:384], T.ones[0:33, :], T.KB[0:33, 0:384], True, False, 384)], ["ones", "KB"], ["K" + H, kb])
            wm = lambda nm, n: T.W[:, WOF[nm]:WOF[nm] + n]
            for nm in "AB":
                w = "w" + nm.lower()
                gather(w, T[nm + "u"], nm + "u" + H, h)
                sums(w, h, lambda k: K[:, k:256:16], wm(w, 16), kb)
                for s in "zp": mins(w, "m" + s + nm, h, lambda k: K[:, k:384:16], wm("m" + s + nm, 24), kb)
            mm([(K[:, 0:256], T.ones[:, :], T.SD[:, :], False, False, 256), (K[:, 0:128], hs(T.rm, h), T.iq[:, :], False, False, 128)],
               ["ones", "SD", "rm", "iq", kb], [])
            mm([(K[:, 0:128], hs(T.dab, h), T.ie[:, :], False, False, 128), (K[:, 256:384], hs(T.Bh, h), T.idb[:, :], False, True, 128)],
               ["dab", "ie", "Bh" + H, "idb"], ["K" + H, kb])
            ac(hs(T.Xb, h), K[:, 0:128], 128, ["K" + H], ["Xb" + H, kb], bias=-BIG / 2, scale=BIG * 8192)
            tt(hs(T.nw, h), K[:, 128:256], hs(T.Xb, h), Alu.min, 128, ["K" + H, "Xb" + H], ["nw" + H, kb])
            tt(hs(T.wk, h), K[:, 256:384], hs(T.nw, h), Alu.min, 128, ["K" + H, "nw" + H], ["wk" + H, kb])
            ac(hs(T.Xb, h), hs(T.nw, h), 128, ["nw" + H], ["Xb" + H], f=Act.Sign)
            scan(hs(T.sb, h), T.rsb[:, :], hs(T.wk, h), Alu.add, Alu.max, 128, ["rsb", "wk" + H], ["sb" + H])
            scan(hs(T.cs, h), T.rsm[:, :], hs(T.Xb, h), Alu.mult, Alu.add, 128, ["rsm", "Xb" + H], ["cs" + H], 0.5)
            top = T.sb[:, 128 * h + 15:128 * h + 128:16]; tb = T.tb[:, 32 * h:32 * h + 8]
            ts(tb, top, MG, MG, Alu.add, Alu.subtract, 8, ["sb" + H], ["tb" + H])
            tt(vv(h, 16, 24), top, tb, Alu.subtract, 8, ["sb" + H, "tb" + H], ["vr" + H + tg])
            ac(vv(h, 24, 32), T.cs[:, 128 * h + 15:128 * h + 128:16], 8, ["cs" + H], ["vn" + H + tg], f=Act.Sign, bias=-11.0, scale=-1.0)
            mm([(M[0:16, 0:128], vv(h, 16, 32), T.idb[:, :], True, True, 128)], ["vr" + H + tg, "vn" + H + tg, "idb"], ["vt" + H, mb])
            move("vtb", T.vts[0:16, 256 * h:256 * h + 128], M[0:16, 0:128], 128, ["vt" + H], ["vtb" + H, mb], fast=1.0)
            mm([(M[:, 384:392], T.FB[0:16, 15 - j:143 - j], T.vts[0:16, 256 * h + j:256 * h + 128:16], j == 0, j == 15, 64) for j in range(16)],
               ["FB", "vtb" + H], ["li" + H, mb])
            gcu = T.GC[:, 8 * h:8 * h + 8]
            ts(gcu, M[:, 384:392], 3071.75, 2047.25, Alu.add, Alu.min, 8, ["li" + H], ["gc" + H, mb])
            ac(T.BR[:, 8 * h:8 * h + 8], M[:, 384:392], 8, ["li" + H], ["BR" + H, mb], bias=4096.0, scale=8.0)
            move("Ch%d" % h, hs(T.Ch, h), Pw.indirect(gcu), 128, PR + ["gc" + H], ["Ch" + H], GA)
            lists("C", (h,), h, 128, ["Ch" + H])
            mm([(M[:, 256:384], T.bo[:, :], hs(T.yv, h), True, False, 128), (M[:, 256:384], T.ones[0:33, :], T.KB[0:33, 384:512], False, False, 128),
                (M[:, 384:512], T.idb[:, :], xb(h), False, False, 128), (M[:, 256:384], T.negi[:, 0:128], hs(T.Ch, h), False, False, 128),
                (M[:, 384:512], T.negi[:, 0:128], hs(T.Ch, h), False, True, 128)],
               ["Ch" + H, "negi0", "bo", "yv", "ones", "KB", "idb", "xb" + H + tg], ["de" + H, mb])
            ts(T.eq[:, 256 * h:256 * h + 256], M[:, 256:512], 0.0, None, Alu.is_equal, None, 256, ["de" + H], ["eq" + H, mb])
        for h in HS:
            H = str(h); M = T.m1; eq = 512 * h
            kx = lambda a, b: T.KX[:, 48 * h + a:48 * h + b]
            dx = lambda a, b, c=1: T.dxs[:, 32 * h + a:32 * h + b:c]
            tt(kx(0, 48), T.BR[:, 8 * h:8 * h + 8].indirect(T.cl[:, 6:9]), T.GX[:, 48 * h:48 * h + 48], Alu.max, 48, ["BR" + H, "GX", "cl6"], ["KX" + H], GA)
            mm([(M[0:48, 0:128], kx(0, 48), T.idb[:, :], True, True, 128)], ["KX" + H, "idb"], ["kt", "@m1"])
            move("KT", T.KT[0:48, :], M[0:48, 0:128], 128, ["kt"], ["KT", "@m1"], fast=1.0)
            mm([(M[:, 0:512], T.KT[0:48, :], T.EC[0:48, :], True, False, 512), (M[:, 0:256], T.idb[:, :], T.MK[:, :], False, False, 256)]
               + [(M[:, j:512:16], hs(T.SJ, j), kx(0, 32), False, j == 15, 64) for j in range(16)],
               ["SJ%d" % j for j in range(16)] + ["KX" + H, "idb", "MK", "KT", "EC"], ["df" + H, "@m1"])
            ts(T.eqd[:, eq:eq + 512], M[:, 0:512], 0.0, None, Alu.is_equal, None, 512, ["df" + H], ["eqd" + H, "@m1"])
            mm([(M[:, 0:32], T.fs[:, 15 - j:143 - j], T.eqd[:, eq + j:eq + 512:16], j == 0, j == 15, 64) for j in range(16)], ["fs", "eqd" + H], ["dx" + H, "@m1"])
            ac(dx(0, 32), M[:, 0:32], 32, ["dx" + H], ["dxs" + H, "@m1"], scale=4096.0)
            its = [(M[:, 64:80], kx(0, 16)), (M[:, 64:80], dx(0, 16)), (M[:, 65:80:2], dx(16, 24))]
            its += [(M[:, 74 + s:80:4], dx(a + s, a + 4, 2)) for a in (24, 28) for s in (0, 1)]
            mm([(o, T.idb[:, :], r, i == 0, i == len(its) - 1, 64) for i, (o, r) in enumerate(its)], ["idb", "KX" + H, "dxs" + H], ["dd" + H, "@m1"])
            tt(T.OF[:, 16 * h:16 * h + 16], M[:, 64:80], T.dum[:, :], Alu.min, 16, ["dd" + H, "dum"], ["OF" + H, "@m1"])
            cp(T.OU[:, 16 * h:16 * h + 16], T.OF[:, 16 * h:16 * h + 16], 16, ["OF" + H], ["OU" + H])
        if not lastv:
            mm([(T.k0[:, 448:456], T.ones[:, :], vv(h, 24, 32), h == 1, h == 0, 64) for h in HS], ["ones", "vn0" + tg, "vn1" + tg], ["cn", "@k0"])
            A_(8, 1.0, lambda: act.activation(T.cj[:, :], T.k0[:, 448:456], Act.Identity, bias=127.0625, scale=-0.5, accum_out=T.cf[:, 0:1]),
               ["cn"], ["cf", "cj", "@k0"])
            ac(T.cf[:, 1:2], T.cf[:, 0:1], 1, ["cf"], ["cf1"], bias=201326592.0)
            ac(T.cf[:, 3:4], T.cf[:, 1:2], 1, ["cf1"], ["cf2"], bias=201326592.0, scale=-1.0)
            ac(T.cf[:, 4:5], T.cf[:, 0:1], 1, ["cf", "thf"], ["cf3"], bias=T.thf[:, t + 1:t + 2])
            ac(T.cf[:, 2:3], T.cf[:, 3:4], 1, ["cf2", "cf3"], ["scol"], bias=T.cf[:, 4:5])
        for h in HS:
            K = KK[h]; kb = "@k%d" % h; H = str(h)
            two = h in APART
            X, xk, xn_ = (MM[h], "@m" + H, "X" + H) if two else (K, kb, "K" + H)
            mm([(K[:, 0:272], T.ones[0:33, :], T.KC[0:33, 0:272], True, False, 272),
                (K[:, 0:272], zz(h), T.B17[:, 0:272], False, False, 272), (K[:, 16:272:34], hs(T.yv, h), bo8, False, False, 64),
                (K[:, 16:272:34], T.ic[:, :], vv(h, 24, 32), False, False, 64), (K[:, 33:272:34], T.ig[:, :], vv(h, 24, 32), False, False, 64),
                (K[:, 33:272:34], T.idb[:, :], T.LQ[:, 16 * t + 8 * h:16 * t + 8 * h + 8], False, False, 64)],
               ["ones", "KC", ZR[h], "B17", "yv", "bo", "ic", "ig", "vn" + H + tg, "idb", "LQ"], ["K" + H, kb])
            mm([(X[:, 272:408], T.ones[0:33, :], T.KC[0:33, 272:408], two, False, 136),
                (X[:, 272:408], T.pp[:, 256 * h:256 * h + 256:2], T.B17[:, 272:408], False, False, 136),
                (X[:, 288:408:17], xb(h), T.idb[:, 0:128:16], False, False, 64)], ["ones", "KC", "pp%d0" % h, "B17", "idb", "xb" + H + tg], [xn_, xk])
            gather("wc", T.Cu, "Cu" + H, h)
            mm([(K[:, 0:272], hs(T.eq, 2 * h), T.E17[:, 0:272], False, False, 272)], ["eq" + H, "E17", kb], [])
            mm([(X[:, 272:408], hs(T.eq, 2 * h + 1), T.E17[:, 272:408], False, False, 136)], ["eq" + H, "E17", xk], [])
            if two:
                sums("wc", h, lambda k: K[:, k:272:34], T.W[:, 144:152], kb)
                sums("wc", h, lambda k: X[:, 272 + k:408:17], T.W[:, 144:152], xk)
            else: sums("wc", h, lambda k: K[:, k:408:17], T.W[:, 128:152], kb)
            mins("wc", "mzC", h, lambda k: K[:, k:272:34], T.W[:, 152:160], kb)
            mins("wc", "mpC", h, lambda k: X[:, 272 + k:408:17], T.W[:, 152:160], xk)
            so = 408 * h; vt = T.vts[0:32, 256 * h + 128:256 * h + 256]
            for B, bn, nm, a, b, s in ((K, kb, "K" + H, 0, 272, ""), (X, xk, xn_, 272, 408, "x")) if two else ((K, kb, "K" + H, 0, 408, ""),):
                mm([(B[:, a:b], hs(T.Ch, h), T.I17[:, a:b], False, True, b - a)], ["Ch" + H, "I17"], [nm, bn])
                scan(T.sc[:, so + a:so + b], T.rsc[:, a:b], B[:, a:b], Alu.add, Alu.max, b - a, ["rsc", nm], ["sc" + s + H, bn])
                top = T.sc[:, so + a + 16:so + b:17]; tb = T.tb[:, 32 * h + 8 + a // 17:32 * h + 8 + b // 17]
                ts(tb, top, MG, MG, Alu.add, Alu.subtract, 24, ["sc" + s + H], ["tc" + s + H])
                tt(vv(h, a // 17, b // 17), top, tb, Alu.subtract, 24, ["sc" + s + H, "tc" + s + H],
                   ["vy" + H + tg] * (not s) + ["vr" + H + tg] * (s == "x" or not two))
                rows, src, dst = (8, vv(h, 16, 24), T.vts[0:8, 256 * h:256 * h + 128]) if s else (32, vv(h, 0, 32), vt)
                mm([(B[0:rows, 0:128], src, T.idb[:, :], True, True, 128)], ["vy" + H + tg, "vr" + H + tg, "vn" + H + tg, "idb"], ["vt" + s + H, bn])
                move("vtc", dst, B[0:rows, 0:128], 128, ["vt" + s + H], ["vtb" + H if s else "vtc" + H, bn], fast=1.0)
                parts = [(1, T.EB[0:8, 256:384])] if s else [(0, T.EB[0:32, 0:128])] + ([] if two else [(1, T.EB[0:32, 128:256])])
                its = []
                for w, E in parts: its += [(B[:, 128 + 128 * w:256 + 128 * w], T.idb[:, :], hs(T.rm, h)), (B[:, 128 + 128 * w:256 + 128 * w], E, dst)]
                if not (s or lastv): its += [(B[:, 0:128], T.EB[0:32, 0:128], dst)]
                mm([it + (k == 0, k == len(its) - 1, 128) for k, it in enumerate(its)], ["idb", "rm", "EB", "vtb" + H if s else "vtc" + H], ["vt" + s + H, bn])
                a, b = 128 * parts[0][0], 128 * parts[-1][0] + 128
                ac(T.yx[:, 256 * h + a:256 * h + b], B[:, 128 + a:128 + b], b - a, ["vt" + s + H], ["y%d%s" % (w, H) for w, E in parts] + [bn], f=Act.Relu)
            for F, o, nm, bank in ((T.FX, T.m1[:, 416 + 8 * h:424 + 8 * h], "xn", "@m1"), (T.FQ, K[:, 424:432], "ql", kb)):
                mm([(o, F[0:32, 15 - j:143 - j], T.vts[0:32, 256 * h + 128 + j:256 * h + 256:16], j == 0, j == 15, 64) for j in range(16)],
                   ["FX", "FQ", "vtc" + H], [nm + H, bank])
            add(T.QU[:, 8 * h:8 * h + 8], K[:, 424:432], 4096.0, 8, ["ql" + H], ["qu" + H, kb])
            if not lastv:
                o = L * (t + 1) + 128 * h
                ac(T.XN[:, o:o + 128], K[:, 0:128], 128, ["vt" + H], ["xs" + H + tg, kb], scale=-1.0)
                send(T.XB[:, o:o + 128], T.XN[:, o:o + 128], "at%d_%d" % (t + 1, h), ["xs" + H + tg], "xb" + H + nt)
            ac(hs(T.qh, h), T.win[:, 0:zo + 2 * L].indirect(T.QU[:, 8 * h:8 * h + 8]), 128,
               ["prof", "qu" + H, "zd#0"] + ["z%d#%d" % (v, u) for u in range(t + 1) for v in (0, 1)], ["qh" + H], bias=-0.25, scale=0.5, per=GA)
            mm([(K[:, 0:128], T.idb[:, :], hs(T.qh, h), True, False, 128), (K[:, 0:128], T.ih[:, :], zz(h), False, True, 128)],
               ["idb", "ih", "qh" + H, ZR[h]], ["zp" + H, kb])
            o = 2 * L * t + 256 * h
            zs = [T.ZS[:, o - 128 * h:o - 128 * h + 128]] if lastv else [T.ZS[:, o + c:o + 256:2] for c in (0, 1)]
            ac(hs(T.zt, h), K[:, 0:128], 128, ["zp" + H], ["zt" + H, kb], bias=128.0)
            for c, out in enumerate(zs): ac(out, hs(T.zt, h), 128, ["zt" + H], ["zs" + "ab"[c] + H + tg], bias=-128.0)
            if not lastv:
                send(T.win[:, R + 2 * L + o:R + 2 * L + o + 256], T.ZS[:, o:o + 256], "az%d_%d" % (t + 1, h), ["zsa" + H + tg, "zsb" + H + tg], "z" + H + nt)
            for m in (6, 4, 2, 0):
                a = 128 * h + 16 * m
                tt(Wt[:, :].indirect(T.OU[:, 16 * h + m:16 * h + m + 2]), T.Ab[:, a:a + 32], T.yx[:, 128 * h + a:128 * h + a + 32], Alu.subtract, 32,
                   ["OU" + H, "Ab", "y0" + H], [WN] + W0, SCA)
        xn = T.m1[:, 416:432]; so = 32 * t
        if not lastv:
            ts(T.XS[:, so + 16:so + 32], xn, 0.5, 1023.75, Alu.mult, Alu.add, 16, ["xn0", "xn1"], ["xs" + tg, "@m1"])
            add(T.XS[:, so:so + 16], xn, 2049.0 + t, 16, ["xn0", "xn1"], ["xt" + tg, "@m1"])
            send(T.XU[:, xo + 48:xo + 80], T.XS[:, so:so + 32], "ax%d" % (t + 1), ["xs" + tg, "xt" + tg], "XU" + nt)
        else:
            ac(T.XO[:, :], xn, 16, ["xn0", "xn1"], ["XO", "@m1"], bias=2048.0)
        tt(T.bb[:, :], Wt[:, 0:V].indirect(gyu), (T.dab2 if lastv else T.rm)[:, :], Alu.max, L, [WN, "gyu" + tg, "rm", "rm2"], ["bb"], GA)
        for h, m in ((1, 4), (1, 0), (0, 4), (0, 0)):
            a = 128 * h + 16 * m; o = 128 * h + 128 + a
            tt(Wt[:, :].indirect(T.OU[:, 16 * h + 8 + m:16 * h + 12 + m]), T.bb[:, a:a + 64], T.yx[:, o:o + 64], Alu.subtract, 64,
               ["OU%d" % h, "bb", "y1%d" % h], [WN], SCA)
    t = RO - 1
    dma("S", T.yrec[:, :], T.XO[:, :], "st4", 2000.0, ["XO"], [])
    dma("S", T.yz[:, :], T.ZS[:, 2 * L * t:2 * L * t + L], "st5", 2000.0, ["zsa0#%d" % t, "zsa1#%d" % t], [])
    for q in (0, 1): dma("SA"[q], T.ypar[:, 1024 * q:1024 * q + 1024], T.PO[:, 1024 * q:1024 * q + 1024], "st%d" % q, 3500.0, ["PO"], [])
    return ops, nsent[0]


def schedule(ops):
    rng = np.random.default_rng(SEED)
    num = {"V": 0, "A": 1, "P": 2, "G": 3, "S": 4, None: -1}

    def improve(idx, kin, base, off, rounds, hot, mark, free):
        n = len(idx); at = {x: i for i, x in enumerate(idx)}; every = range(n)
        busy = [ops[x]["busy"] for x in idx]; eng = [num[ops[x]["eng"]] for x in idx]; vis = [ops[x]["vis"] for x in idx]
        lat = [ops[x]["lat"] if ops[x]["sem"] else 0.0 for x in idx]; pre = []; anc = []
        for x in idx:
            o = ops[x]; l = []; a = 0
            for j in list(o["deps"]) + o["after"]:
                if j in at:
                    d = ops[j]
                    same = d["eng"] == o["eng"] and (not o["deps"].get(j, False) or d["eng"] == "P") and d["sem"] is None
                    l.append((at[j], 0.0 if same else d["lat"] + WAKE)); a |= anc[at[j]] | (1 << at[j])
            anc.append(a)
            pre.append([(j, gp) for j, gp in l if not any(k != j and anc[k] >> j & 1 and busy[k] + g2 >= gp for k, g2 in l)])

        def decode(o):
            key = [0.0] * n; end = [0.0] * n; why = [-1] * n; last = [-1] * 5; idle = [0.0] * 5
            for i in every:
                k = o[kin[i]] + base[i]
                for j, gp in pre[i]:
                    if k <= key[j]: k = key[j] + 1e-3
                key[i] = k
            seq = sorted(every, key=lambda i: key[i]); span = 0.0
            for i in seq:
                e = eng[i]
                if e >= 0: t = idle[e]; w = -2 - last[e]
                else: t = 0.0; w = -1
                for j, gp in pre[i]:
                    if end[j] + gp >= t: t = end[j] + gp; w = j
                t += busy[i]; end[i] = t; why[i] = w
                if e >= 0: idle[e] = t; last[e] = i
                if t + lat[i] > span: span = t + lat[i]; z = i
            return span, end, key, why, z, seq

        def arcs(now):
            i = now[4]; why = now[3]; out = []
            while why[i] != -1:
                if why[i] <= -2:
                    if free[i] or free[-2 - why[i]]: out.append((-2 - why[i], i))
                    i = -2 - why[i]
                else: i = why[i]
            return out

        now = decode(off); top = (now, off); ar = arcs(now); loose = [i for i in every if free[i]]
        for it in range(1, rounds + 1):
            o = off[:]; end, key = now[1], now[2]; r = rng.random(6)
            if it % 64 == 0:
                zero = min(end[i] - busy[i] - key[i] for i in mark)
                for i in mark: o[kin[i]] = end[i] - busy[i] - base[i] - zero
            elif r[0] < 0.8 and ar:
                a = int(r[1] * len(ar)); u, v = ar[a]
                if r[2] < 0.5:
                    while a + 1 < len(ar) and ar[a + 1][1] == ar[a][0] and rng.random() < 0.6: a += 1
                    u = ar[a][0]
                if free[v] and (r[3] < 0.5 or not free[u]):
                    todo = [(v, key[u] - 1e-2)]
                    while todo:
                        x, k = todo.pop(); o[kin[x]] = min(o[kin[x]], k - base[x])
                        todo += [(j, k - 1e-2) for j, gp in pre[x] if key[j] >= k and vis[j] == vis[x]]
                else: o[kin[u]] = key[v] + 1e-2 - base[u] + (r[4] * 1500.0 if r[5] < 0.3 else 0.0)
            else: o[kin[loose[int(r[1] * len(loose))]]] += float(rng.normal()) * (2000.0 if r[2] < 0.3 else 500.0)
            new = decode(o)
            if new[0] <= now[0] or rng.random() < np.exp((now[0] - new[0]) / (hot * (COLD / hot) ** (it / rounds))):
                now, off = new, o; ar = arcs(now)
                if new[0] < top[0][0]: top = (new, o)
        now = top[0]
        return now[0], {x: now[1][i] - busy[i] for i, x in enumerate(idx)}, [idx[i] for i in now[5]]

    def calls(idx, key, rounds, hot, free):
        n = len(idx)
        return improve(idx, list(range(n)), [0.0] * n, [key[x] for x in idx], rounds, hot, list(range(n)), [free(ops[x]["vis"]) for x in idx])

    n = len(ops); vis = [o["vis"] for o in ops]; kin = [o["kin"] for o in ops]
    plan = {k: 10.0 * int(v) for k, v in (e.split(":") for e in PLAN.split())}
    sub = [i for i in range(n) if vis[i] in (1, 2)]; names = sorted(set(kin[i] for i in sub))
    span, start, seq = improve(sub, [names.index(kin[i]) for i in sub], [PERIOD * vis[i] for i in sub],
                               [plan.get(k[0] + "'" * (k[1] - 1), -2000.0) for k in names], STEADY, HOT,
                               [i for i, x in enumerate(sub) if vis[x] == 2], [True] * len(sub))
    first = {v: min(start[i] for i in sub if vis[i] == v and kin[i][0] == "yv") for v in (1, 2)}
    per = first[2] - first[1]; off = {kin[i]: start[i] - first[2] for i in sub if vis[i] == 2}; key = [0.0] * n
    for i in range(n - 1, -1, -1):
        if kin[i] in off: key[i] = off[kin[i]] + per * vis[i]
        else: key[i] = min([key[s] - ops[i]["busy"] - WAKE for s in range(i + 1, n) if i in ops[s]["deps"]] + [per * RO])
    for i in range(n):
        if vis[i] < 0 and ops[i]["eng"] in "GS": key[i] = i - 2 * per
        elif vis[i] < 0 and key[i] < EARLY[ops[i]["eng"]]: key[i] -= per
    span, start, seq = calls([i for i in range(n) if vis[i] <= 1], key, MOVES, HOT, lambda v: v < 1)
    at = {kin[i]: start[i] for i in start if vis[i] == 1}
    for i in range(n): key[i] = start[i] if vis[i] <= 1 else at.get(kin[i], max(at.values())) + per * (vis[i] - 1)
    rear = [i for i in range(n) if vis[i] >= RO - 2]
    span, start, seq = calls(rear, key, MOVES // 2, HOT / 2, lambda v: v == RO - 1)
    i = min(rear, key=lambda i: key[i]); zero = key[i] - start[i]
    for i in rear: key[i] = start[i] + zero
    span, start, seq = calls(list(range(n)), key, MOVES // 8, HOT / 4, lambda v: True)
    order = {}
    for i in seq:
        if ops[i]["eng"] is not None: order.setdefault(ops[i]["eng"], []).append(i)
    return order, [start[i] + ops[i]["busy"] + ops[i]["lat"] for i in range(n)]


def rank_program(g, core, T, topo):
    if T.rank_of(core) is None:
        return
    ops, nsent = build(g, T, topo, core)
    if not ORDER: ORDER.append(schedule(ops)[0])
    order = ORDER[0]
    queue = {"V": g.vector, "A": g.scalar, "P": g.tensor, "G": g, "S": g.sync}
    pos = {}
    for e in order:
        for k, i in enumerate(order[e]): pos[i] = k
    waits = {}; marked = set()
    for e in order:
        seen = {}
        for i in order[e]:
            need = {}; ws = []
            for j, raw in ops[i]["deps"].items():
                d = ops[j]
                if d["sem"] is not None:
                    if d["sem"] not in seen: seen[d["sem"]] = 1; ws.append(d["sem"])
                elif d["eng"] != e or (raw and e != "P"):
                    if pos[j] > seen.get(d["eng"], -1) and pos[j] > need.get(d["eng"], (-1, 0))[0]: need[d["eng"]] = (pos[j], j)
            for q in need:
                seen[q] = need[q][0]; marked.add(need[q][1]); ws.append(need[q][1])
            waits[i] = ws
    count = {}
    for e in order:
        c = 0
        for i in order[e]:
            if i in marked: c += 1; count[i] = c
    for e in order:
        for i in order[e]:
            for w in waits[i]:
                if isinstance(w, tuple): queue[e].wait_ge(T.sem[w[0]], w[1])
                else: queue[e].wait_ge(T.sem["s" + ops[w]["eng"]], count[w])
            ins = ops[i]["fn"]()
            if i in marked: ins.then_inc(T.sem["s" + e], 1)
    for s in (0, 1, 4, 5): g.sync.wait_ge(T.sem["st%d" % s], 16)
    g.wait_ge(T.sem.sent, nsent)
